import numpy as np
import ml_dtypes


def mxq(x, axis, fmt="e4m3"):
    dtype, down = {"e4m3": (ml_dtypes.float8_e4m3fn, 7), "e5m2": (ml_dtypes.float8_e5m2, 14)}[fmt]
    v = np.moveaxis(np.asarray(x, np.float32).astype(ml_dtypes.bfloat16).astype(np.float64), axis, -1)
    blocks = v.reshape(v.shape[:-1] + (-1, 32))
    amax = np.abs(blocks).max(-1, keepdims=True)
    byte = np.maximum(np.where(amax > 0, np.frexp(amax)[1] - 1 + 127, 0) - down, 1)
    scale = np.exp2(byte - 127.0)
    codes = (blocks / scale).astype(np.float32).astype(dtype).astype(np.float64)
    return np.moveaxis((codes * scale).reshape(v.shape), -1, axis)


WIDE = False


def mx_kscale(k):
    if not WIDE:
        return np.ones(k)
    levels = np.array([10, -10, 5, -5, 0])
    if k % 512:
        return np.exp2(np.random.permutation(np.resize(levels, k // 32))).repeat(32)
    a = np.empty((k // 512, 16))
    for p in range(k // 512):
        a[p, :8] = np.random.permutation(np.resize(levels, 8))
        for g in range(8):
            far = levels[np.abs(levels - a[p, g]) >= 10]
            a[p, g + 8] = far[np.random.randint(len(far))]
    return np.exp2(a.ravel()).repeat(32)


def f64(x):
    return np.asarray(x).astype(np.float64)


def striped(idx):
    return np.tile(idx.reshape(-1, 16).T, (8, 1)).astype(np.uint16)


def unstriped(offs):
    return offs[:16].T.reshape(-1).astype(np.int64)


E2M1 = np.array([0.0, 0.5, 1.0, 1.5, 2.0, 3.0, 4.0, 6.0, -0.0, -0.5, -1.0, -1.5, -2.0, -3.0, -4.0, -6.0])


def pack_weight(w, fmt):
    k, n = w.shape
    w = f64(np.asarray(w, np.float32).astype(ml_dtypes.bfloat16)).reshape(k // 32, 32, n)
    amax = np.abs(w).max(1)
    if fmt == "e4m3":
        byte = np.frexp(amax)[1] - 1 + 127 - 7
    else:
        mant, ex = np.frexp(amax / 6.0)
        byte = np.where(mant > 0.5, ex, ex - 1) + 127
    byte = np.clip(np.where(amax > 0, byte, 1), 1, 254)
    scaled = (w * np.exp2(127.0 - byte)[:, None, :]).reshape(k, n).astype(np.float32)
    by_word = np.ascontiguousarray(scaled.reshape(k // 512, 128, 4, n).transpose(0, 1, 3, 2))
    if fmt == "e4m3":
        words = by_word.astype(ml_dtypes.float8_e4m3fn).view(np.uint8)
    else:
        c = by_word.astype(ml_dtypes.float4_e2m1fn).view(np.uint8) & 0xF
        words = (c[..., 0::2] | (c[..., 1::2] << 4)).reshape(k // 512, 128, 2 * n)
    return np.ascontiguousarray(words), np.ascontiguousarray(byte.astype(np.uint8).reshape(k // 512, 16, n))


def unpack_weight(words, scales, fmt):
    g, _, n = scales.shape
    words = np.ascontiguousarray(words).reshape(g, 128, n, -1)
    if fmt == "e4m3":
        vals = words.view(ml_dtypes.float8_e4m3fn).astype(np.float64)
    else:
        nib = np.empty((g, 128, n, 4), np.uint8)
        nib[..., 0::2] = words & 0xF
        nib[..., 1::2] = words >> 4
        vals = E2M1[nib]
    vals = vals * np.repeat(np.exp2(scales.astype(np.float64) - 127.0), 8, axis=1)[..., None]
    return vals.transpose(0, 1, 3, 2).reshape(g * 512, n)


def gelu(v):
    return 0.5 * v * (1.0 + np.tanh(np.sqrt(2.0 / np.pi) * (v + 0.044715 * v**3)))


K, T, S, H, T2, P, N = 512, 4096, 1024, 1024, 2048, 1024, 384

def setup_inputs():
    n = np.random.standard_normal
    s = mx_kscale(K)[:, None]
    u = mx_kscale(H)[:, None]
    d = {}
    d["tab_words"], d["tab_scales"] = pack_weight(n((K, T)) * s, "e4m3")
    d["offs"] = striped(np.random.permutation(T)[:S])
    d["w4_words"], d["w4_scales"] = pack_weight(n((K, H)) / np.sqrt(K) / s * u.T, "e2m1")
    d["wgs"] = np.exp(0.3 * n((128, S))).astype(np.float32)
    d["offs2"] = striped(np.random.permutation(T2)[:S])
    d["load"] = (n((H, T2)) * u).astype(np.float32)
    d["wa"] = (n((H, N)) / np.sqrt(H) / u).astype(np.float32)
    d["w8_words"], d["w8_scales"] = pack_weight(n((H, N)) / np.sqrt(H) / u, "e4m3")
    d["offs3"] = striped(np.random.permutation(T2)[:P])
    d["offs4"] = striped(np.random.permutation(T2)[:P])
    d["wgo"] = np.exp(0.3 * n((128, P))).astype(np.float32)
    return d

def reference(tab_words, tab_scales, offs, w4_words, w4_scales, wgs, offs2, load,
              wa, w8_words, w8_scales, offs3, offs4, wgo):
    v = unpack_weight(tab_words, tab_scales, "e4m3")[:, unstriped(offs)]
    w4 = unpack_weight(w4_words, w4_scales, "e2m1")
    h = w4.T @ v
    page = np.zeros((H, T2))
    page[:, unstriped(offs2)] = np.tile(f64(wgs), (H // 128, 1)) * h
    z = np.maximum(page, f64(load))
    zq = mxq(z, 0, "e4m3")
    ya = mxq(f64(wa), 0, "e4m3").T @ zq
    w8 = unpack_weight(w8_words, w8_scales, "e4m3")
    yb = w8.T @ zq
    xa = ya[:, unstriped(offs3)]
    xb = yb[:, unstriped(offs3)]
    x = xa / (1.0 + np.abs(xb))
    out = np.zeros((N, T2))
    out[:, unstriped(offs4)] = np.tile(f64(wgo), (N // 128, 1)) * x
    return out

@@ -1,0 +1,270 @@
+from contextlib import ExitStack
+
+import concourse.mybir as mybir
+
+K, T, S, H, T2, M, N = 512, 4096, 1024, 1024, 2048, 1024, 384
+FLOPS = 2 * K * H * S + 2 * 2 * H * N * T2
+
+F32 = mybir.dt.float32
+BF16 = mybir.dt.bfloat16
+I32 = mybir.dt.int32
+U32 = mybir.dt.uint32
+U16 = mybir.dt.uint16
+U8 = mybir.dt.uint8
+FP8X4 = mybir.dt.float8_e4m3fn_x4
+FP4X4 = mybir.dt.float4_e2m1fn_x4
+ACT = mybir.ActivationFunctionType
+MULT = mybir.AluOpType.mult
+MAX = mybir.AluOpType.max
+
+P = 128
+PACK = 4
+QUADS = 4
+QUAD = 32
+BANK = 512
+PASSES = H // (P * PACK)
+CHUNKS = T2 // BANK
+TILES = PASSES * PACK
+OUT_TILES = N // P
+HALVES = 2
+HALF = S // HALVES
+HALF_COLS = HALF // 16
+
+
+def tile_list_print_run_forecast_kernel(
+    tc, tab_words, tab_scales, offs, w4_words, w4_scales, wgs, offs2, load,
+    wa, w8_words, w8_scales, offs3, offs4, wgo, out,
+):
+    nc = tc.nc
+    with ExitStack() as ctx:
+        lists = ctx.enter_context(tc.tile_pool(name="lists", bufs=1))
+        keep = ctx.enter_context(tc.tile_pool(name="keep", bufs=1))
+        ring = ctx.enter_context(tc.tile_pool(name="ring", bufs=1))
+        psum = ctx.enter_context(tc.psum_pool(name="psum", bufs=8))
+
+        def load_list(name, src):
+            tile = lists.tile([P, S // 16], U16, name=name)
+            nc.sync.dma_start(tile[:], src)
+            return tile
+
+        def load_scale_rows(queue, tile, src):
+            nc.vector.memset(tile[:].bitcast(I32), 0)
+            rows = src.rearrange("a (q r) c -> r q a c", r=4)
+            for r in range(4):
+                queue.dma_start(tile[r:P:QUAD, :, :].bitcast(I32), rows[r].bitcast(I32))
+
+        def wide(name):
+            return ring.tile([P, T2], F32, name=name, tag="wide", bufs=5)
+
+        def row(name):
+            return ring.tile([P, S], F32, name=name, tag="row", bufs=6)
+
+        idx1 = load_list("idx1", offs)
+        tab_s = keep.tile([P, 1, T], U8, align_bytes=64)
+        load_scale_rows(nc.scalar, tab_s, tab_scales)
+        w4_raw = keep.tile([P, 2 * H], U8, align_bytes=64)
+        nc.sync.dma_start(w4_raw[:].bitcast(I32), w4_words[0].bitcast(I32))
+        tab_w = keep.tile([P, T], U32, align_bytes=64)
+        nc.sync.dma_start(tab_w[:].bitcast(I32), tab_words[0].rearrange("p t i -> p (t i)").bitcast(I32))
+        w4_s_raw = keep.tile([P, 1, H], U8, align_bytes=64)
+        load_scale_rows(nc.gpsimd, w4_s_raw, w4_scales)
+        idx2 = load_list("idx2", offs2)
+
+        wgs_rows = wgs.rearrange("(q t) j -> q t j", t=PACK)
+        wgs_of_slot = []
+        for first, count in ((0, 1), (1, 1), (2, 2)):
+            part = keep.tile([P, count, S], F32, name="wgs%d" % first)
+            for q in range(QUADS):
+                nc.sync.dma_start(part[QUAD * q : QUAD * (q + 1)], wgs_rows[:, first : first + count, :])
+            wgs_of_slot.extend(part[:, i, :] for i in range(count))
+
+        pages = [keep.tile([P, T2], F32, name="page%d" % i) for i in range(2)]
+        outs = [keep.tile([P, T2], F32, name="placed%d" % i) for i in range(2)]
+        for tile in pages + outs:
+            nc.vector.memset(tile[:], 0.0)
+
+        v_s = keep.tile([P, S], U8, align_bytes=64)
+        nc.vector.tensor_copy(v_s[:], tab_s[:, 0, :].indirect(idx1[:]))
+
+        w4_w = keep.tile([P, 2 * H], U8, align_bytes=64)
+        w4_s = keep.tile([P, H], U8, align_bytes=64)
+        nc.vector.tensor_copy(
+            w4_w[:].bitcast(U16).rearrange("p (b t m) -> p b t m", b=PASSES, t=PACK),
+            w4_raw[:].bitcast(U16).rearrange("p (b m t) -> p b t m", b=PASSES, t=PACK),
+        )
+        nc.vector.tensor_copy(
+            w4_s[:].rearrange("p (b t m) -> p b t m", b=PASSES, t=PACK),
+            w4_s_raw[:, 0, :].rearrange("p (b m t) -> p b t m", b=PASSES, t=PACK),
+        )
+
+        v_w = []
+        for i in range(HALVES):
+            half = keep.tile([P, HALF], U32, name="v_w%d" % i, align_bytes=64)
+            nc.vector.tensor_copy(half[:], tab_w[:].indirect(idx1[:, HALF_COLS * i : HALF_COLS * (i + 1)]))
+            v_w.append(half)
+
+        h_tiles = {}
+
+        def first_product(k):
+            h = row("h")
+            for i in range(HALVES):
+                bank = psum.tile([P, BANK], F32, name="bank")
+                nc.tensor.matmul_mx(
+                    out=bank[:],
+                    lhsT=w4_w[:, 2 * P * k : 2 * P * (k + 1)].bitcast(FP4X4),
+                    lhsT_scale=w4_s[:, P * k : P * (k + 1)],
+                    rhs=v_w[i][:].bitcast(FP8X4),
+                    rhs_scale=v_s[:, HALF * i : HALF * (i + 1)],
+                    start=True,
+                    stop=True,
+                )
+                nc.scalar.copy(h[:, HALF * i : HALF * (i + 1)], bank[:])
+            h_tiles[k] = h
+
+        load_bf = {}
+
+        def round_load(b, c):
+            raw = wide("load_raw")
+            raw3 = raw[:].rearrange("p (t c) -> p t c", t=PACK)
+            nc.sync.dma_start(
+                raw3,
+                load[P * PACK * b : P * PACK * (b + 1), BANK * c : BANK * (c + 1)].rearrange("(p t) c -> p t c", t=PACK),
+            )
+            rounded = ring.tile([P, BANK * PACK], BF16, name="load_bf", bufs=6)
+            nc.scalar.copy(
+                rounded[:].rearrange("p (c i t) -> p c t i", i=4, t=PACK),
+                raw[:].rearrange("p (t c i) -> p c t i", t=PACK, i=4),
+            )
+            load_bf[b, c] = rounded
+
+        def place_h(k):
+            page, h, w = pages[k % 2], h_tiles[k], wgs_of_slot[k % PACK]
+            if k == 0:
+                for i in range(HALVES):
+                    cols = slice(HALF * i, HALF * (i + 1))
+                    nc.vector.tensor_tensor(
+                        page[:].indirect(idx2[:, HALF_COLS * i : HALF_COLS * (i + 1)]), h[:, cols], w[:, cols], MULT
+                    )
+            else:
+                nc.vector.tensor_tensor(page[:].indirect(idx2[:]), h[:], w, MULT)
+
+        page_bf = [keep.tile([P, 2, BANK, 2], BF16, name="page_bf%d" % c) for c in range(CHUNKS)]
+
+        def round_page(k):
+            t = k % PACK
+            for c in range(CHUNKS):
+                nc.scalar.copy(page_bf[c][:, t // 2, :, t % 2], pages[k % 2][:, BANK * c : BANK * (c + 1)])
+
+        z_w, z_s = {}, {}
+
+        def make_z(b, c):
+            z = ring.tile([P, BANK * PACK], BF16, name="z", bufs=3, align_bytes=64)
+            nc.vector.tensor_tensor(
+                z[:].rearrange("p (c u e) -> p c u e", u=2, e=2),
+                page_bf[c][:].rearrange("p u c e -> p c u e"),
+                load_bf[b, c][:].rearrange("p (c u e) -> p c u e", u=2, e=2),
+                MAX,
+            )
+            z_w[b, c] = keep.tile([P, BANK], U32, name="z_w%d%d" % (b, c), align_bytes=64)
+            z_s[b, c] = keep.tile([P, BANK], U8, name="z_s%d%d" % (b, c), align_bytes=64)
+            nc.vector.quantize_mx(out=z_w[b, c][:].bitcast(FP8X4), scales=z_s[b, c][:], in_=z[:])
+
+        wa_w = keep.tile([P, PASSES * N], U32, align_bytes=64)
+        wa_s = keep.tile([P, PASSES * N], U8, align_bytes=64)
+        w8_w = keep.tile([P, PASSES * N], U32, align_bytes=64)
+        w8_s = keep.tile([P, PASSES, N], U8, align_bytes=64)
+
+        def prepare_second_weights():
+            wa_bf = keep.tile([P, PASSES * N * PACK], BF16, align_bytes=64)
+            for b in range(PASSES):
+                raw = wide("wa_raw")
+                nc.sync.dma_start(
+                    raw[:, : PACK * N], wa[P * PACK * b : P * PACK * (b + 1), :].rearrange("(p t) n -> p (t n)", t=PACK)
+                )
+                nc.scalar.copy(
+                    wa_bf[:, N * PACK * b : N * PACK * (b + 1)].rearrange("p (c i t) -> p c t i", i=4, t=PACK),
+                    raw[:, : PACK * N].rearrange("p (t c i) -> p c t i", t=PACK, i=4),
+                )
+            for lo, hi in ((0, 512), (512, PASSES * N)):
+                nc.vector.quantize_mx(
+                    out=wa_w[:, lo:hi].bitcast(FP8X4), scales=wa_s[:, lo:hi], in_=wa_bf[:, PACK * lo : PACK * hi]
+                )
+            nc.sync.dma_start(
+                w8_w[:].bitcast(I32).rearrange("p (a c) -> p a c", a=PASSES),
+                w8_words.rearrange("a p c i -> p a (c i)").bitcast(I32),
+            )
+            load_scale_rows(nc.sync, w8_s, w8_scales)
+
+        weights = {"a": (wa_w, wa_s[:]), "b": (w8_w, w8_s[:].rearrange("p a c -> p (a c)"))}
+        banks = {}
+
+        def second_pass(which, n, c, b):
+            if b == 0:
+                banks[which, n, c] = psum.tile([P, BANK], F32, name="bank")
+            words, scales = weights[which]
+            cols = slice(N * b + P * n, N * b + P * (n + 1))
+            nc.tensor.matmul_mx(
+                out=banks[which, n, c][:],
+                lhsT=words[:, cols].bitcast(FP8X4),
+                lhsT_scale=scales[:, cols],
+                rhs=z_w[b, c][:].bitcast(FP8X4),
+                rhs_scale=z_s[b, c][:],
+                start=(b == 0),
+                stop=(b == PASSES - 1),
+            )
+
+        y = {}
+
+        def empty_bank(which, n, c):
+            if c == 0:
+                y[which, n] = wide("y")
+            nc.scalar.copy(y[which, n][:, BANK * c : BANK * (c + 1)], banks[which, n, c][:])
+
+        first_product(0)
+        first_product(1)
+        for k in range(TILES):
+            if k + 2 < TILES:
+                first_product(k + 2)
+            round_load(k // PACK, k % PACK)
+            place_h(k)
+            if k == PACK:
+                for c in range(CHUNKS):
+                    make_z(0, c)
+            round_page(k)
+            if k == PACK - 1:
+                prepare_second_weights()
+        idx3 = load_list("idx3", offs3)
+        idx4 = load_list("idx4", offs4)
+        wgo_sb = keep.tile([P, M], F32)
+        nc.sync.dma_start(wgo_sb[:], wgo)
+
+        for which in "ba":
+            for c in range(CHUNKS):
+                second_pass(which, 0, c, 0)
+        y["b", 0] = wide("y")
+        y["a", 0] = wide("y")
+        for c in range(CHUNKS):
+            make_z(1, c)
+            for which in "ba":
+                second_pass(which, 0, c, 1)
+                nc.scalar.copy(y[which, 0][:, BANK * c : BANK * (c + 1)], banks[which, 0, c][:])
+
+        for n in range(OUT_TILES):
+            damp = row("damp")
+            for i in range(HALVES):
+                cols = slice(HALF * i, HALF * (i + 1))
+                nc.vector.tensor_copy(damp[:, cols], y["b", n][:].indirect(idx3[:, HALF_COLS * i : HALF_COLS * (i + 1)]))
+                nc.scalar.activation(damp[:, cols], damp[:, cols], ACT.Abs)
+                nc.scalar.activation(damp[:, cols], damp[:, cols], ACT.Abs_reciprocal_sqrt, bias=1.0)
+                nc.scalar.activation(damp[:, cols], damp[:, cols], ACT.Square)
+            score = row("score")
+            nc.vector.tensor_tensor(score[:], y["a", n][:].indirect(idx3[:]), wgo_sb[:], MULT)
+            placed = outs[n % 2]
+            nc.vector.tensor_tensor(placed[:].indirect(idx4[:]), score[:], damp[:], MULT)
+            nc.sync.dma_start(out[P * n : P * (n + 1), :], placed[:])
+            if n + 1 < OUT_TILES:
+                for which in "ba":
+                    for c in range(CHUNKS):
+                        for b in range(PASSES):
+                            second_pass(which, n + 1, c, b)
+                        empty_bank(which, n + 1, c)

@@ -47,8 +47,8 @@ def tile_list_print_run_forecast_kernel(
             nc.sync.dma_start(tile[:], src)
             return tile
 
-        def load_scale_rows(queue, tile, src):
-            nc.vector.memset(tile[:].bitcast(I32), 0)
+        def load_scale_rows(queue, tile, src, clear):
+            clear.memset(tile[:].bitcast(I32), 0)
             rows = src.rearrange("a (q r) c -> r q a c", r=4)
             for r in range(4):
                 queue.dma_start(tile[r:P:QUAD, :, :].bitcast(I32), rows[r].bitcast(I32))
@@ -60,27 +60,29 @@ def tile_list_print_run_forecast_kernel(
             return ring.tile([P, S], F32, name=name, tag="row", bufs=6)
 
         idx1 = load_list("idx1", offs)
-        tab_s = keep.tile([P, 1, T], U8, align_bytes=64)
-        load_scale_rows(nc.scalar, tab_s, tab_scales)
         w4_raw = keep.tile([P, 2 * H], U8, align_bytes=64)
         nc.sync.dma_start(w4_raw[:].bitcast(I32), w4_words[0].bitcast(I32))
-        tab_w = keep.tile([P, T], U32, align_bytes=64)
-        nc.sync.dma_start(tab_w[:].bitcast(I32), tab_words[0].rearrange("p t i -> p (t i)").bitcast(I32))
         w4_s_raw = keep.tile([P, 1, H], U8, align_bytes=64)
-        load_scale_rows(nc.gpsimd, w4_s_raw, w4_scales)
+        load_scale_rows(nc.sync, w4_s_raw, w4_scales, nc.gpsimd)
+        tab_s = keep.tile([P, 1, T], U8, tag="bytes_words_out", align_bytes=64)
+        load_scale_rows(nc.sync, tab_s, tab_scales, nc.vector)
+        tab_w = keep.tile([P, T], U32, tag="table_out", align_bytes=64)
+        nc.sync.dma_start(tab_w[:].bitcast(I32), tab_words[0].rearrange("p t i -> p (t i)").bitcast(I32))
         idx2 = load_list("idx2", offs2)
+        warm = keep.tile([P, 1], F32)
+        nc.vector.memset(warm[:], 1.0)
+        nc.scalar.activation(warm[:], warm[:], ACT.Abs_reciprocal_sqrt)
 
         wgs_rows = wgs.rearrange("(q t) j -> q t j", t=PACK)
         wgs_of_slot = []
         for first, count in ((0, 1), (1, 1), (2, 2)):
-            part = keep.tile([P, count, S], F32, name="wgs%d" % first)
+            part = keep.tile([P, count, S], F32, name="wgs", tag="wgs%d" % first, align_bytes=64)
             for q in range(QUADS):
                 nc.sync.dma_start(part[QUAD * q : QUAD * (q + 1)], wgs_rows[:, first : first + count, :])
             wgs_of_slot.extend(part[:, i, :] for i in range(count))
 
         pages = [keep.tile([P, T2], F32, name="page%d" % i) for i in range(2)]
-        outs = [keep.tile([P, T2], F32, name="placed%d" % i) for i in range(2)]
-        for tile in pages + outs:
+        for tile in pages:
             nc.vector.memset(tile[:], 0.0)
 
         v_s = keep.tile([P, S], U8, align_bytes=64)
@@ -97,11 +99,11 @@ def tile_list_print_run_forecast_kernel(
             w4_s_raw[:, 0, :].rearrange("p (b m t) -> p b t m", b=PASSES, t=PACK),
         )
 
-        v_w = []
+        v_w = keep.tile([P, S], U32, tag="bytes_words_out", align_bytes=64)
         for i in range(HALVES):
-            half = keep.tile([P, HALF], U32, name="v_w%d" % i, align_bytes=64)
-            nc.vector.tensor_copy(half[:], tab_w[:].indirect(idx1[:, HALF_COLS * i : HALF_COLS * (i + 1)]))
-            v_w.append(half)
+            nc.vector.tensor_copy(
+                v_w[:, HALF * i : HALF * (i + 1)], tab_w[:].indirect(idx1[:, HALF_COLS * i : HALF_COLS * (i + 1)])
+            )
 
         h_tiles = {}
 
@@ -113,7 +115,7 @@ def tile_list_print_run_forecast_kernel(
                     out=bank[:],
                     lhsT=w4_w[:, 2 * P * k : 2 * P * (k + 1)].bitcast(FP4X4),
                     lhsT_scale=w4_s[:, P * k : P * (k + 1)],
-                    rhs=v_w[i][:].bitcast(FP8X4),
+                    rhs=v_w[:, HALF * i : HALF * (i + 1)].bitcast(FP8X4),
                     rhs_scale=v_s[:, HALF * i : HALF * (i + 1)],
                     start=True,
                     stop=True,
@@ -169,13 +171,12 @@ def tile_list_print_run_forecast_kernel(
             z_s[b, c] = keep.tile([P, BANK], U8, name="z_s%d%d" % (b, c), align_bytes=64)
             nc.vector.quantize_mx(out=z_w[b, c][:].bitcast(FP8X4), scales=z_s[b, c][:], in_=z[:])
 
-        wa_w = keep.tile([P, PASSES * N], U32, align_bytes=64)
+        wa_bf = keep.tile([P, PASSES * N * PACK], BF16, align_bytes=64)
         wa_s = keep.tile([P, PASSES * N], U8, align_bytes=64)
         w8_w = keep.tile([P, PASSES * N], U32, align_bytes=64)
         w8_s = keep.tile([P, PASSES, N], U8, align_bytes=64)
 
         def prepare_second_weights():
-            wa_bf = keep.tile([P, PASSES * N * PACK], BF16, align_bytes=64)
             for b in range(PASSES):
                 raw = wide("wa_raw")
                 nc.sync.dma_start(
@@ -185,17 +186,13 @@ def tile_list_print_run_forecast_kernel(
                     wa_bf[:, N * PACK * b : N * PACK * (b + 1)].rearrange("p (c i t) -> p c t i", i=4, t=PACK),
                     raw[:, : PACK * N].rearrange("p (t c i) -> p c t i", t=PACK, i=4),
                 )
-            for lo, hi in ((0, 512), (512, PASSES * N)):
-                nc.vector.quantize_mx(
-                    out=wa_w[:, lo:hi].bitcast(FP8X4), scales=wa_s[:, lo:hi], in_=wa_bf[:, PACK * lo : PACK * hi]
-                )
             nc.sync.dma_start(
                 w8_w[:].bitcast(I32).rearrange("p (a c) -> p a c", a=PASSES),
                 w8_words.rearrange("a p c i -> p a (c i)").bitcast(I32),
             )
-            load_scale_rows(nc.sync, w8_s, w8_scales)
+            load_scale_rows(nc.sync, w8_s, w8_scales, nc.vector)
 
-        weights = {"a": (wa_w, wa_s[:]), "b": (w8_w, w8_s[:].rearrange("p a c -> p (a c)"))}
+        weights = {"b": (w8_w, w8_s[:].rearrange("p a c -> p (a c)"))}
         banks = {}
 
         def second_pass(which, n, c, b):
@@ -237,6 +234,19 @@ def tile_list_print_run_forecast_kernel(
         idx4 = load_list("idx4", offs4)
         wgo_sb = keep.tile([P, M], F32)
         nc.sync.dma_start(wgo_sb[:], wgo)
+
+        wa_w = keep.tile([P, PASSES * N], U32, tag="wgs2", align_bytes=64)
+        for lo, hi in ((0, 512), (512, PASSES * N)):
+            nc.vector.quantize_mx(
+                out=wa_w[:, lo:hi].bitcast(FP8X4), scales=wa_s[:, lo:hi], in_=wa_bf[:, PACK * lo : PACK * hi]
+            )
+        weights = {"a": (wa_w, wa_s[:]), "b": weights["b"]}
+
+        outs = []
+        for tag in ("table_out", "bytes_words_out"):
+            placed = keep.tile([P, T2], F32, name="placed", tag=tag, align_bytes=64)
+            nc.gpsimd.memset(placed[:], 0.0)
+            outs.append(placed)
 
         for which in "ba":
             for c in range(CHUNKS):

@@ -26,6 +26,7 @@ PASSES = H // (P * PACK)
 CHUNKS = T2 // BANK
 TILES = PASSES * PACK
 OUT_TILES = N // P
+PAGES = 2
 HALVES = 2
 HALF = S // HALVES
 HALF_COLS = HALF // 16
@@ -81,7 +82,7 @@ def tile_list_print_run_forecast_kernel(
                 nc.sync.dma_start(part[QUAD * q : QUAD * (q + 1)], wgs_rows[:, first : first + count, :])
             wgs_of_slot.extend(part[:, i, :] for i in range(count))
 
-        pages = [keep.tile([P, T2], F32, name="page%d" % i) for i in range(2)]
+        pages = [keep.tile([P, T2], F32, name="page%d" % i) for i in range(PAGES)]
         for tile in pages:
             nc.vector.memset(tile[:], 0.0)
 
@@ -132,7 +133,7 @@ def tile_list_print_run_forecast_kernel(
                 raw3,
                 load[P * PACK * b : P * PACK * (b + 1), BANK * c : BANK * (c + 1)].rearrange("(p t) c -> p t c", t=PACK),
             )
-            rounded = ring.tile([P, BANK * PACK], BF16, name="load_bf", bufs=6)
+            rounded = ring.tile([P, BANK * PACK], BF16, name="load_bf", bufs=8)
             nc.scalar.copy(
                 rounded[:].rearrange("p (c i t) -> p c t i", i=4, t=PACK),
                 raw[:].rearrange("p (t c i) -> p c t i", t=PACK, i=4),
@@ -140,7 +141,7 @@ def tile_list_print_run_forecast_kernel(
             load_bf[b, c] = rounded
 
         def place_h(k):
-            page, h, w = pages[k % 2], h_tiles[k], wgs_of_slot[k % PACK]
+            page, h, w = pages[k % PAGES], h_tiles[k], wgs_of_slot[k % PACK]
             if k == 0:
                 for i in range(HALVES):
                     cols = slice(HALF * i, HALF * (i + 1))
@@ -150,26 +151,36 @@ def tile_list_print_run_forecast_kernel(
             else:
                 nc.vector.tensor_tensor(page[:].indirect(idx2[:]), h[:], w, MULT)
 
-        page_bf = [keep.tile([P, 2, BANK, 2], BF16, name="page_bf%d" % c) for c in range(CHUNKS)]
+        page_bf = [keep.tile([P, 2, BANK, 2], BF16, name="page_bf", tag="page_bf%d" % c, align_bytes=64) for c in range(CHUNKS)]
 
         def round_page(k):
             t = k % PACK
             for c in range(CHUNKS):
-                nc.scalar.copy(page_bf[c][:, t // 2, :, t % 2], pages[k % 2][:, BANK * c : BANK * (c + 1)])
+                nc.scalar.copy(page_bf[c][:, t // 2, :, t % 2], pages[k % PAGES][:, BANK * c : BANK * (c + 1)])
 
-        z_w, z_s = {}, {}
+        z_bf, z_w, z_s = {}, {}, {}
 
-        def make_z(b, c):
-            z = ring.tile([P, BANK * PACK], BF16, name="z", bufs=3, align_bytes=64)
+        def make_z(b, c, held=False):
+            if held:
+                z = keep.tile([P, BANK * PACK], BF16, name="z_held", tag="wgs0", align_bytes=64)
+            else:
+                z = ring.tile([P, BANK * PACK], BF16, name="z", bufs=3, align_bytes=64)
             nc.vector.tensor_tensor(
                 z[:].rearrange("p (c u e) -> p c u e", u=2, e=2),
                 page_bf[c][:].rearrange("p u c e -> p c u e"),
                 load_bf[b, c][:].rearrange("p (c u e) -> p c u e", u=2, e=2),
                 MAX,
             )
-            z_w[b, c] = keep.tile([P, BANK], U32, name="z_w%d%d" % (b, c), align_bytes=64)
+            z_bf[b, c] = z
+
+        def quantise_z(b, c, words):
+            z_w[b, c] = words
             z_s[b, c] = keep.tile([P, BANK], U8, name="z_s%d%d" % (b, c), align_bytes=64)
-            nc.vector.quantize_mx(out=z_w[b, c][:].bitcast(FP8X4), scales=z_s[b, c][:], in_=z[:])
+            nc.vector.quantize_mx(out=words.bitcast(FP8X4), scales=z_s[b, c][:], in_=z_bf[b, c][:])
+
+        def new_z_words(b, c):
+            words = keep.tile([P, BANK], U32, name="z_w%d%d" % (b, c), align_bytes=64)
+            return words[:]
 
         wa_bf = keep.tile([P, PASSES * N * PACK], BF16, align_bytes=64)
         wa_s = keep.tile([P, PASSES * N], U8, align_bytes=64)
@@ -183,8 +194,8 @@ def tile_list_print_run_forecast_kernel(
                     raw[:, : PACK * N], wa[P * PACK * b : P * PACK * (b + 1), :].rearrange("(p t) n -> p (t n)", t=PACK)
                 )
                 nc.scalar.copy(
-                    wa_bf[:, N * PACK * b : N * PACK * (b + 1)].rearrange("p (c i t) -> p c t i", i=4, t=PACK),
-                    raw[:, : PACK * N].rearrange("p (t c i) -> p c t i", t=PACK, i=4),
+                    wa_bf[:].rearrange("p (n b c i t) -> p b n c t i", n=OUT_TILES, b=PASSES, i=4, t=PACK)[:, b],
+                    raw[:, : PACK * N].rearrange("p (t n c i) -> p n c t i", t=PACK, n=OUT_TILES, i=4),
                 )
             nc.sync.dma_start(
                 w8_w[:].bitcast(I32).rearrange("p (a c) -> p a c", a=PASSES),
@@ -192,19 +203,30 @@ def tile_list_print_run_forecast_kernel(
             )
             load_scale_rows(nc.sync, w8_s, w8_scales, nc.vector)
 
-        weights = {"b": (w8_w, w8_s[:].rearrange("p a c -> p (a c)"))}
+        weights = {}
+        for n in range(OUT_TILES):
+            for b in range(PASSES):
+                cols = slice(P * n, P * (n + 1))
+                weights["b", n, b] = (w8_w[:, N * b + P * n : N * b + P * (n + 1)], w8_s[:, b, cols])
         banks = {}
+
+        def quantise_wa(first, count, words):
+            lo, hi = PASSES * P * first, PASSES * P * (first + count)
+            nc.vector.quantize_mx(out=words.bitcast(FP8X4), scales=wa_s[:, lo:hi], in_=wa_bf[:, PACK * lo : PACK * hi])
+            for n in range(first, first + count):
+                for b in range(PASSES):
+                    at = P * (PASSES * n + b)
+                    weights["a", n, b] = (words[:, at - lo : at - lo + P], wa_s[:, at : at + P])
 
         def second_pass(which, n, c, b):
             if b == 0:
                 banks[which, n, c] = psum.tile([P, BANK], F32, name="bank")
-            words, scales = weights[which]
-            cols = slice(N * b + P * n, N * b + P * (n + 1))
+            words, scales = weights[which, n, b]
             nc.tensor.matmul_mx(
                 out=banks[which, n, c][:],
-                lhsT=words[:, cols].bitcast(FP8X4),
-                lhsT_scale=scales[:, cols],
-                rhs=z_w[b, c][:].bitcast(FP8X4),
+                lhsT=words.bitcast(FP8X4),
+                lhsT_scale=scales,
+                rhs=z_w[b, c].bitcast(FP8X4),
                 rhs_scale=z_s[b, c][:],
                 start=(b == 0),
                 stop=(b == PASSES - 1),
@@ -226,7 +248,9 @@ def tile_list_print_run_forecast_kernel(
             place_h(k)
             if k == PACK:
                 for c in range(CHUNKS):
-                    make_z(0, c)
+                    make_z(0, c, held=(c == CHUNKS - 1))
+                    if c < CHUNKS - 1:
+                        quantise_z(0, c, new_z_words(0, c))
             round_page(k)
             if k == PACK - 1:
                 prepare_second_weights()
@@ -235,12 +259,9 @@ def tile_list_print_run_forecast_kernel(
         wgo_sb = keep.tile([P, M], F32)
         nc.sync.dma_start(wgo_sb[:], wgo)
 
-        wa_w = keep.tile([P, PASSES * N], U32, tag="wgs2", align_bytes=64)
-        for lo, hi in ((0, 512), (512, PASSES * N)):
-            nc.vector.quantize_mx(
-                out=wa_w[:, lo:hi].bitcast(FP8X4), scales=wa_s[:, lo:hi], in_=wa_bf[:, PACK * lo : PACK * hi]
-            )
-        weights = {"a": (wa_w, wa_s[:]), "b": weights["b"]}
+        late = keep.tile([P, PASSES * P + BANK], U32, tag="wgs2", align_bytes=64)
+        quantise_wa(0, 1, late[:, : PASSES * P])
+        quantise_z(0, CHUNKS - 1, late[:, PASSES * P :])
 
         outs = []
         for tag in ("table_out", "bytes_words_out"):
@@ -251,30 +272,58 @@ def tile_list_print_run_forecast_kernel(
         for which in "ba":
             for c in range(CHUNKS):
                 second_pass(which, 0, c, 0)
-        y["b", 0] = wide("y")
-        y["a", 0] = wide("y")
+        two = keep.tile([P, 2 * BANK], U32, tag="wgs1", align_bytes=64)
         for c in range(CHUNKS):
             make_z(1, c)
+            quantise_z(1, c, two[:, BANK * c : BANK * (c + 1)] if c < 2 else new_z_words(1, c))
             for which in "ba":
                 second_pass(which, 0, c, 1)
-                nc.scalar.copy(y[which, 0][:, BANK * c : BANK * (c + 1)], banks[which, 0, c][:])
+                empty_bank(which, 0, c)
+        wa_rest = keep.tile([P, PASSES * P * (OUT_TILES - 1)], U32, tag="page_bf%d" % (CHUNKS - 1), align_bytes=64)
+        quantise_wa(1, OUT_TILES - 1, wa_rest[:])
 
-        for n in range(OUT_TILES):
-            damp = row("damp")
-            for i in range(HALVES):
-                cols = slice(HALF * i, HALF * (i + 1))
-                nc.vector.tensor_copy(damp[:, cols], y["b", n][:].indirect(idx3[:, HALF_COLS * i : HALF_COLS * (i + 1)]))
-                nc.scalar.activation(damp[:, cols], damp[:, cols], ACT.Abs)
-                nc.scalar.activation(damp[:, cols], damp[:, cols], ACT.Abs_reciprocal_sqrt, bias=1.0)
-                nc.scalar.activation(damp[:, cols], damp[:, cols], ACT.Square)
-            score = row("score")
-            nc.vector.tensor_tensor(score[:], y["a", n][:].indirect(idx3[:]), wgo_sb[:], MULT)
+        def second_product(which, n):
+            for c in range(CHUNKS):
+                for b in range(PASSES):
+                    second_pass(which, n, c, b)
+                empty_bank(which, n, c)
+
+        damp, score = {}, {}
+
+        def pick_damping(n, gathers, pieces):
+            damp[n] = row("damp")
+            width = M // gathers
+            for i in range(gathers):
+                nc.vector.tensor_copy(
+                    damp[n][:, width * i : width * (i + 1)],
+                    y["b", n][:].indirect(idx3[:, width // 16 * i : width // 16 * (i + 1)]),
+                )
+            width = M // pieces
+            for i in range(pieces):
+                part = damp[n][:, width * i : width * (i + 1)]
+                nc.scalar.activation(part, part, ACT.Abs)
+                nc.scalar.activation(part, part, ACT.Abs_reciprocal_sqrt, bias=1.0)
+                nc.scalar.activation(part, part, ACT.Square)
+
+        def pick_score(n):
+            score[n] = row("score")
+            nc.vector.tensor_tensor(score[n][:], y["a", n][:].indirect(idx3[:]), wgo_sb[:], MULT)
+
+        def place_out(n):
             placed = outs[n % 2]
-            nc.vector.tensor_tensor(placed[:].indirect(idx4[:]), score[:], damp[:], MULT)
+            nc.vector.tensor_tensor(placed[:].indirect(idx4[:]), score[n][:], damp[n][:], MULT)
             nc.sync.dma_start(out[P * n : P * (n + 1), :], placed[:])
-            if n + 1 < OUT_TILES:
-                for which in "ba":
-                    for c in range(CHUNKS):
-                        for b in range(PASSES):
-                            second_pass(which, n + 1, c, b)
-                        empty_bank(which, n + 1, c)
+
+        pick_damping(0, 4, 4)
+        pick_score(0)
+        place_out(0)
+        second_product("b", 1)
+        second_product("a", 1)
+        second_product("b", 2)
+        pick_damping(1, 1, 2)
+        pick_score(1)
+        pick_damping(2, 1, 2)
+        place_out(1)
+        second_product("a", 2)
+        pick_score(2)
+        place_out(2)

@@ -27,6 +27,7 @@ CHUNKS = T2 // BANK
 TILES = PASSES * PACK
 OUT_TILES = N // P
 PAGES = 2
+ROWS = 6
 HALVES = 2
 HALF = S // HALVES
 HALF_COLS = HALF // 16
@@ -58,7 +59,7 @@ def tile_list_print_run_forecast_kernel(
             return ring.tile([P, T2], F32, name=name, tag="wide", bufs=5)
 
         def row(name):
-            return ring.tile([P, S], F32, name=name, tag="row", bufs=6)
+            return ring.tile([P, S], F32, name=name, tag="row", bufs=ROWS)
 
         idx1 = load_list("idx1", offs)
         w4_raw = keep.tile([P, 2 * H], U8, align_bytes=64)
@@ -75,12 +76,16 @@ def tile_list_print_run_forecast_kernel(
         nc.scalar.activation(warm[:], warm[:], ACT.Abs_reciprocal_sqrt)
 
         wgs_rows = wgs.rearrange("(q t) j -> q t j", t=PACK)
-        wgs_of_slot = []
-        for first, count in ((0, 1), (1, 1), (2, 2)):
+        wgs_of_slot = {}
+
+        def load_wgs(first, count):
             part = keep.tile([P, count, S], F32, name="wgs", tag="wgs%d" % first, align_bytes=64)
-            for q in range(QUADS):
+            for q in (0, 2, 1, 3):
                 nc.sync.dma_start(part[QUAD * q : QUAD * (q + 1)], wgs_rows[:, first : first + count, :])
-            wgs_of_slot.extend(part[:, i, :] for i in range(count))
+            for i in range(count):
+                wgs_of_slot[first + i] = part[:, i, :]
+
+        load_wgs(0, 1)
 
         pages = [keep.tile([P, T2], F32, name="page%d" % i) for i in range(PAGES)]
         for tile in pages:
@@ -239,12 +244,17 @@ def tile_list_print_run_forecast_kernel(
                 y[which, n] = wide("y")
             nc.scalar.copy(y[which, n][:, BANK * c : BANK * (c + 1)], banks[which, n, c][:])
 
-        first_product(0)
-        first_product(1)
+        for k in range(ROWS):
+            first_product(k)
         for k in range(TILES):
-            if k + 2 < TILES:
-                first_product(k + 2)
-            round_load(k // PACK, k % PACK)
+            if k in (1, 2):
+                load_wgs(k, k)
+            if k <= PACK:
+                round_load(k // PACK, k % PACK)
+            if PACK <= k < TILES - 1:
+                round_load(1, k + 1 - PACK)
+            if k == PACK:
+                prepare_second_weights()
             place_h(k)
             if k == PACK:
                 for c in range(CHUNKS):
@@ -252,8 +262,8 @@ def tile_list_print_run_forecast_kernel(
                     if c < CHUNKS - 1:
                         quantise_z(0, c, new_z_words(0, c))
             round_page(k)
-            if k == PACK - 1:
-                prepare_second_weights()
+            if k + ROWS < TILES:
+                first_product(k + ROWS)
         idx3 = load_list("idx3", offs3)
         idx4 = load_list("idx4", offs4)
         wgo_sb = keep.tile([P, M], F32)

@@ -140,8 +140,8 @@ def tile_list_print_run_forecast_kernel(
             )
             rounded = ring.tile([P, BANK * PACK], BF16, name="load_bf", bufs=8)
             nc.scalar.copy(
-                rounded[:].rearrange("p (c i t) -> p c t i", i=4, t=PACK),
-                raw[:].rearrange("p (t c i) -> p c t i", t=PACK, i=4),
+                rounded[:].rearrange("p (u c e) -> p u c e", u=2, e=2),
+                raw[:].rearrange("p (u e c) -> p u c e", u=2, e=2),
             )
             load_bf[b, c] = rounded
 
@@ -173,7 +173,7 @@ def tile_list_print_run_forecast_kernel(
             nc.vector.tensor_tensor(
                 z[:].rearrange("p (c u e) -> p c u e", u=2, e=2),
                 page_bf[c][:].rearrange("p u c e -> p c u e"),
-                load_bf[b, c][:].rearrange("p (c u e) -> p c u e", u=2, e=2),
+                load_bf[b, c][:].rearrange("p (u c e) -> p c u e", u=2, e=2),
                 MAX,
             )
             z_bf[b, c] = z
@@ -241,7 +241,10 @@ def tile_list_print_run_forecast_kernel(
 
         def empty_bank(which, n, c):
             if c == 0:
-                y[which, n] = wide("y")
+                if which == "b" and n < 2:
+                    y[which, n] = keep.tile([P, T2], F32, name="y_b", tag="y_b")
+                else:
+                    y[which, n] = wide("y")
             nc.scalar.copy(y[which, n][:, BANK * c : BANK * (c + 1)], banks[which, n, c][:])
 
         for k in range(ROWS):
@@ -259,8 +262,8 @@ def tile_list_print_run_forecast_kernel(
             if k == PACK:
                 for c in range(CHUNKS):
                     make_z(0, c, held=(c == CHUNKS - 1))
-                    if c < CHUNKS - 1:
-                        quantise_z(0, c, new_z_words(0, c))
+                    if c > 0:
+                        quantise_z(0, c - 1, new_z_words(0, c - 1))
             round_page(k)
             if k + ROWS < TILES:
                 first_product(k + ROWS)
@@ -283,14 +286,27 @@ def tile_list_print_run_forecast_kernel(
             for c in range(CHUNKS):
                 second_pass(which, 0, c, 0)
         two = keep.tile([P, 2 * BANK], U32, tag="wgs1", align_bytes=64)
-        for c in range(CHUNKS):
-            make_z(1, c)
+
+        def finish_chunk(c):
             quantise_z(1, c, two[:, BANK * c : BANK * (c + 1)] if c < 2 else new_z_words(1, c))
             for which in "ba":
                 second_pass(which, 0, c, 1)
                 empty_bank(which, 0, c)
-        wa_rest = keep.tile([P, PASSES * P * (OUT_TILES - 1)], U32, tag="page_bf%d" % (CHUNKS - 1), align_bytes=64)
-        quantise_wa(1, OUT_TILES - 1, wa_rest[:])
+
+        def quantise_wa_after_chunk(n, c):
+            words = keep.tile([P, PASSES * P], U32, name="wa_w", tag="page_bf%d" % c, align_bytes=64)
+            quantise_wa(n, 1, words[:])
+
+        make_z(1, 0)
+        make_z(1, 1)
+        finish_chunk(0)
+        make_z(1, 2)
+        finish_chunk(1)
+        finish_chunk(2)
+        make_z(1, 3)
+        quantise_wa_after_chunk(1, 2)
+        finish_chunk(3)
+        quantise_wa_after_chunk(2, 3)
 
         def second_product(which, n):
             for c in range(CHUNKS):
@@ -327,13 +343,11 @@ def tile_list_print_run_forecast_kernel(
         pick_damping(0, 4, 4)
         pick_score(0)
         place_out(0)
-        second_product("b", 1)
-        second_product("a", 1)
-        second_product("b", 2)
-        pick_damping(1, 1, 2)
-        pick_score(1)
-        pick_damping(2, 1, 2)
-        place_out(1)
-        second_product("a", 2)
-        pick_score(2)
-        place_out(2)
+        for n in range(1, OUT_TILES):
+            second_product("b", n)
+            second_product("a", n)
+        for n in range(1, OUT_TILES):
+            pick_damping(n, 1, 2)
+            pick_score(n)
+        for n in range(1, OUT_TILES):
+            place_out(n)

@@ -140,8 +140,8 @@ def tile_list_print_run_forecast_kernel(
             )
             rounded = ring.tile([P, BANK * PACK], BF16, name="load_bf", bufs=8)
             nc.scalar.copy(
-                rounded[:].rearrange("p (u c e) -> p u c e", u=2, e=2),
-                raw[:].rearrange("p (u e c) -> p u c e", u=2, e=2),
+                rounded[:].rearrange("p (c i t) -> p c t i", i=4, t=PACK),
+                raw[:].rearrange("p (t c i) -> p c t i", t=PACK, i=4),
             )
             load_bf[b, c] = rounded
 
@@ -173,15 +173,20 @@ def tile_list_print_run_forecast_kernel(
             nc.vector.tensor_tensor(
                 z[:].rearrange("p (c u e) -> p c u e", u=2, e=2),
                 page_bf[c][:].rearrange("p u c e -> p c u e"),
-                load_bf[b, c][:].rearrange("p (u c e) -> p c u e", u=2, e=2),
+                load_bf[b, c][:].rearrange("p (c u e) -> p c u e", u=2, e=2),
                 MAX,
             )
             z_bf[b, c] = z
 
-        def quantise_z(b, c, words):
-            z_w[b, c] = words
-            z_s[b, c] = keep.tile([P, BANK], U8, name="z_s%d%d" % (b, c), align_bytes=64)
-            nc.vector.quantize_mx(out=words.bitcast(FP8X4), scales=z_s[b, c][:], in_=z_bf[b, c][:])
+        def quantise_z(b, c, words, cols=slice(0, BANK)):
+            if cols.start == 0:
+                z_w[b, c] = words
+                z_s[b, c] = keep.tile([P, BANK], U8, name="z_s%d%d" % (b, c), align_bytes=64)
+            nc.vector.quantize_mx(
+                out=z_w[b, c][:, cols].bitcast(FP8X4),
+                scales=z_s[b, c][:, cols],
+                in_=z_bf[b, c][:, PACK * cols.start : PACK * cols.stop],
+            )
 
         def new_z_words(b, c):
             words = keep.tile([P, BANK], U32, name="z_w%d%d" % (b, c), align_bytes=64)
@@ -223,29 +228,33 @@ def tile_list_print_run_forecast_kernel(
                     at = P * (PASSES * n + b)
                     weights["a", n, b] = (words[:, at - lo : at - lo + P], wa_s[:, at : at + P])
 
-        def second_pass(which, n, c, b):
+        def second_pass(which, n, c, b, cols=slice(0, BANK)):
+            key = which, n, c, cols.start
             if b == 0:
-                banks[which, n, c] = psum.tile([P, BANK], F32, name="bank")
+                banks[key] = psum.tile([P, BANK], F32, name="bank")
             words, scales = weights[which, n, b]
             nc.tensor.matmul_mx(
-                out=banks[which, n, c][:],
+                out=banks[key][:, : cols.stop - cols.start],
                 lhsT=words.bitcast(FP8X4),
                 lhsT_scale=scales,
-                rhs=z_w[b, c].bitcast(FP8X4),
-                rhs_scale=z_s[b, c][:],
+                rhs=z_w[b, c][:, cols].bitcast(FP8X4),
+                rhs_scale=z_s[b, c][:, cols],
                 start=(b == 0),
                 stop=(b == PASSES - 1),
             )
 
         y = {}
 
-        def empty_bank(which, n, c):
+        def empty_bank(which, n, c, cols=slice(0, BANK)):
             if c == 0:
                 if which == "b" and n < 2:
                     y[which, n] = keep.tile([P, T2], F32, name="y_b", tag="y_b")
                 else:
                     y[which, n] = wide("y")
-            nc.scalar.copy(y[which, n][:, BANK * c : BANK * (c + 1)], banks[which, n, c][:])
+            nc.scalar.copy(
+                y[which, n][:, BANK * c + cols.start : BANK * c + cols.stop],
+                banks[which, n, c, cols.start][:, : cols.stop - cols.start],
+            )
 
         for k in range(ROWS):
             first_product(k)
@@ -282,9 +291,13 @@ def tile_list_print_run_forecast_kernel(
             nc.gpsimd.memset(placed[:], 0.0)
             outs.append(placed)
 
+        last = CHUNKS - 1
+        last_parts = [slice(0, BANK // 2), slice(BANK // 2, BANK)]
         for which in "ba":
-            for c in range(CHUNKS):
+            for c in range(last):
                 second_pass(which, 0, c, 0)
+        for cols in last_parts:
+            second_pass("b", 0, last, 0, cols)
         two = keep.tile([P, 2 * BANK], U32, tag="wgs1", align_bytes=64)
 
         def finish_chunk(c):
@@ -305,7 +318,14 @@ def tile_list_print_run_forecast_kernel(
         finish_chunk(2)
         make_z(1, 3)
         quantise_wa_after_chunk(1, 2)
-        finish_chunk(3)
+        last_words = new_z_words(1, last)
+        for cols in last_parts:
+            quantise_z(1, last, last_words, cols)
+            second_pass("b", 0, last, 1, cols)
+            empty_bank("b", 0, last, cols)
+        for b in range(PASSES):
+            second_pass("a", 0, last, b)
+        empty_bank("a", 0, last)
         quantise_wa_after_chunk(2, 3)
 
         def second_product(which, n):

@@ -91,6 +91,9 @@ def tile_list_print_run_forecast_kernel(
         for tile in pages:
             nc.vector.memset(tile[:], 0.0)
 
+        out_odd = keep.tile([P, T2], F32)
+        nc.vector.memset(out_odd[:], 0.0)
+
         v_s = keep.tile([P, S], U8, align_bytes=64)
         nc.vector.tensor_copy(v_s[:], tab_s[:, 0, :].indirect(idx1[:]))
 
@@ -285,12 +288,6 @@ def tile_list_print_run_forecast_kernel(
         quantise_wa(0, 1, late[:, : PASSES * P])
         quantise_z(0, CHUNKS - 1, late[:, PASSES * P :])
 
-        outs = []
-        for tag in ("table_out", "bytes_words_out"):
-            placed = keep.tile([P, T2], F32, name="placed", tag=tag, align_bytes=64)
-            nc.gpsimd.memset(placed[:], 0.0)
-            outs.append(placed)
-
         last = CHUNKS - 1
         last_parts = [slice(0, BANK // 2), slice(BANK // 2, BANK)]
         for which in "ba":
@@ -316,7 +313,7 @@ def tile_list_print_run_forecast_kernel(
         make_z(1, 2)
         finish_chunk(1)
         finish_chunk(2)
-        make_z(1, 3)
+        make_z(1, 3, held=True)
         quantise_wa_after_chunk(1, 2)
         last_words = new_z_words(1, last)
         for cols in last_parts:
@@ -326,7 +323,9 @@ def tile_list_print_run_forecast_kernel(
         for b in range(PASSES):
             second_pass("a", 0, last, b)
         empty_bank("a", 0, last)
-        quantise_wa_after_chunk(2, 3)
+        out_even = keep.tile([P, T2], F32, tag="page_bf3", align_bytes=64)
+        nc.vector.memset(out_even[:], 0.0)
+        outs = [out_even, out_odd]
 
         def second_product(which, n):
             for c in range(CHUNKS):
@@ -362,6 +361,8 @@ def tile_list_print_run_forecast_kernel(
 
         pick_damping(0, 4, 4)
         pick_score(0)
+        wa_last = keep.tile([P, PASSES * P], U32, tag="wgs0", align_bytes=64)
+        quantise_wa(2, 1, wa_last[:])
         place_out(0)
         for n in range(1, OUT_TILES):
             second_product("b", n)

@@ -78,14 +78,15 @@ def tile_list_print_run_forecast_kernel(
         wgs_rows = wgs.rearrange("(q t) j -> q t j", t=PACK)
         wgs_of_slot = {}
 
-        def load_wgs(first, count):
+        def load_wgs(first, count, parts=(slice(0, S),)):
             part = keep.tile([P, count, S], F32, name="wgs", tag="wgs%d" % first, align_bytes=64)
-            for q in (0, 2, 1, 3):
-                nc.sync.dma_start(part[QUAD * q : QUAD * (q + 1)], wgs_rows[:, first : first + count, :])
+            for cols in parts:
+                for q in (0, 2, 1, 3):
+                    nc.sync.dma_start(part[QUAD * q : QUAD * (q + 1), :, cols], wgs_rows[:, first : first + count, cols])
             for i in range(count):
                 wgs_of_slot[first + i] = part[:, i, :]
 
-        load_wgs(0, 1)
+        load_wgs(0, 1, (slice(0, HALF // 2), slice(HALF // 2, S)))
 
         pages = [keep.tile([P, T2], F32, name="page%d" % i) for i in range(PAGES)]
         for tile in pages:
@@ -115,21 +116,24 @@ def tile_list_print_run_forecast_kernel(
             )
 
         h_tiles = {}
+        halves = [slice(0, HALF), slice(HALF, S)]
+        first_parts = [slice(0, HALF // 2), slice(HALF // 2, HALF), slice(HALF, S)]
 
         def first_product(k):
             h = row("h")
-            for i in range(HALVES):
+            for cols in first_parts if k == 0 else halves:
                 bank = psum.tile([P, BANK], F32, name="bank")
+                width = cols.stop - cols.start
                 nc.tensor.matmul_mx(
-                    out=bank[:],
+                    out=bank[:, :width],
                     lhsT=w4_w[:, 2 * P * k : 2 * P * (k + 1)].bitcast(FP4X4),
                     lhsT_scale=w4_s[:, P * k : P * (k + 1)],
-                    rhs=v_w[:, HALF * i : HALF * (i + 1)].bitcast(FP8X4),
-                    rhs_scale=v_s[:, HALF * i : HALF * (i + 1)],
+                    rhs=v_w[:, cols].bitcast(FP8X4),
+                    rhs_scale=v_s[:, cols],
                     start=True,
                     stop=True,
                 )
-                nc.scalar.copy(h[:, HALF * i : HALF * (i + 1)], bank[:])
+                nc.scalar.copy(h[:, cols], bank[:, :width])
             h_tiles[k] = h
 
         load_bf = {}
@@ -151,10 +155,9 @@ def tile_list_print_run_forecast_kernel(
         def place_h(k):
             page, h, w = pages[k % PAGES], h_tiles[k], wgs_of_slot[k % PACK]
             if k == 0:
-                for i in range(HALVES):
-                    cols = slice(HALF * i, HALF * (i + 1))
+                for cols in (slice(0, HALF // 2), slice(HALF // 2, S)):
                     nc.vector.tensor_tensor(
-                        page[:].indirect(idx2[:, HALF_COLS * i : HALF_COLS * (i + 1)]), h[:, cols], w[:, cols], MULT
+                        page[:].indirect(idx2[:, cols.start // 16 : cols.stop // 16]), h[:, cols], w[:, cols], MULT
                     )
             else:
                 nc.vector.tensor_tensor(page[:].indirect(idx2[:]), h[:], w, MULT)
@@ -357,7 +360,11 @@ def tile_list_print_run_forecast_kernel(
         def place_out(n):
             placed = outs[n % 2]
             nc.vector.tensor_tensor(placed[:].indirect(idx4[:]), score[n][:], damp[n][:], MULT)
-            nc.sync.dma_start(out[P * n : P * (n + 1), :], placed[:])
+            if n < OUT_TILES - 1:
+                nc.sync.dma_start(out[P * n : P * (n + 1), :], placed[:])
+            else:
+                for queue, cols in ((nc.sync, slice(0, T2 // 2)), (nc.scalar, slice(T2 // 2, T2))):
+                    queue.dma_start(out[P * n : P * (n + 1), cols], placed[:, cols])
 
         pick_damping(0, 4, 4)
         pick_score(0)

@@ -62,12 +62,22 @@ def tile_list_print_run_forecast_kernel(
             return ring.tile([P, S], F32, name=name, tag="row", bufs=ROWS)
 
         idx1 = load_list("idx1", offs)
-        w4_raw = keep.tile([P, 2 * H], U8, align_bytes=64)
-        nc.sync.dma_start(w4_raw[:].bitcast(I32), w4_words[0].bitcast(I32))
         w4_s_raw = keep.tile([P, 1, H], U8, align_bytes=64)
-        load_scale_rows(nc.sync, w4_s_raw, w4_scales, nc.gpsimd)
+
+        def load_w4_scales(q):
+            nc.sync.dma_start(
+                w4_s_raw[QUAD * q : QUAD * (q + 1), 0, :].bitcast(I32),
+                w4_scales[0, 4 * q : 4 * q + 4, :].bitcast(I32).unsqueeze(0).to_broadcast([QUAD // 4, 4, H // 4]),
+            )
+
+        for q in (0, 2):
+            load_w4_scales(q)
         tab_s = keep.tile([P, 1, T], U8, tag="bytes_words_out", align_bytes=64)
         load_scale_rows(nc.sync, tab_s, tab_scales, nc.vector)
+        for q in (1, 3):
+            load_w4_scales(q)
+        w4_raw = keep.tile([P, 2 * H], U8, align_bytes=64)
+        nc.sync.dma_start(w4_raw[:].bitcast(I32), w4_words[0].bitcast(I32))
         tab_w = keep.tile([P, T], U32, tag="table_out", align_bytes=64)
         nc.sync.dma_start(tab_w[:].bitcast(I32), tab_words[0].rearrange("p t i -> p (t i)").bitcast(I32))
         idx2 = load_list("idx2", offs2)
@@ -95,9 +105,6 @@ def tile_list_print_run_forecast_kernel(
         out_odd = keep.tile([P, T2], F32)
         nc.vector.memset(out_odd[:], 0.0)
 
-        v_s = keep.tile([P, S], U8, align_bytes=64)
-        nc.vector.tensor_copy(v_s[:], tab_s[:, 0, :].indirect(idx1[:]))
-
         w4_w = keep.tile([P, 2 * H], U8, align_bytes=64)
         w4_s = keep.tile([P, H], U8, align_bytes=64)
         nc.vector.tensor_copy(
@@ -108,6 +115,9 @@ def tile_list_print_run_forecast_kernel(
             w4_s[:].rearrange("p (b t m) -> p b t m", b=PASSES, t=PACK),
             w4_s_raw[:, 0, :].rearrange("p (b m t) -> p b t m", b=PASSES, t=PACK),
         )
+
+        v_s = keep.tile([P, S], U8, align_bytes=64)
+        nc.vector.tensor_copy(v_s[:], tab_s[:, 0, :].indirect(idx1[:]))
 
         v_w = keep.tile([P, S], U32, tag="bytes_words_out", align_bytes=64)
         for i in range(HALVES):

@@ -31,6 +31,27 @@ ROWS = 6
 HALVES = 2
 HALF = S // HALVES
 HALF_COLS = HALF // 16
+KIB = 1024
+SCALE_ROWS = 16
+LANDING = P - 2 * SCALE_ROWS
+
+AT_TABLE = 0
+AT_PAGE_ODD = 73 * KIB
+AT_WINDOW = 79 * KIB
+AT_WGS0 = 81 * KIB
+AT_PICKED = 20 * KIB
+AT_W4_RAW = 24 * KIB
+AT_W4_S_RAW = 32 * KIB
+AT_RAW = (AT_W4_RAW, AT_W4_S_RAW, AT_TABLE + 8 * KIB)
+AT_WGS = {0: AT_WGS0, 1: AT_PICKED, 2: AT_TABLE}
+AT_Y_B = 40 * KIB
+AT_V_W = 46 * KIB
+AT_W8_W = 48 * KIB
+AT_OUT_ODD = 52 * KIB
+AT_W4_W = 59 * KIB
+AT_WGO = 60 * KIB
+AT_V_S = 64 * KIB
+AT_Y_LAST = 65 * KIB
 
 
 def tile_list_print_run_forecast_kernel(
@@ -42,7 +63,11 @@ def tile_list_print_run_forecast_kernel(
         lists = ctx.enter_context(tc.tile_pool(name="lists", bufs=1))
         keep = ctx.enter_context(tc.tile_pool(name="keep", bufs=1))
         ring = ctx.enter_context(tc.tile_pool(name="ring", bufs=1))
+        placed = ctx.enter_context(tc.tile_pool(name="placed", bufs=1))
         psum = ctx.enter_context(tc.psum_pool(name="psum", bufs=8))
+
+        def place(name, offset, shape, dtype):
+            return placed.tile(shape, dtype, name=name, tag=name, offset=offset, align_bytes=64)
 
         def load_list(name, src):
             tile = lists.tile([P, S // 16], U16, name=name)
@@ -55,32 +80,42 @@ def tile_list_print_run_forecast_kernel(
             for r in range(4):
                 queue.dma_start(tile[r:P:QUAD, :, :].bitcast(I32), rows[r].bitcast(I32))
 
-        def wide(name):
-            return ring.tile([P, T2], F32, name=name, tag="wide", bufs=5)
+        raw_uses = []
+
+        def raw_rows():
+            raw_uses.append(len(raw_uses))
+            return place("raw%d" % raw_uses[-1], AT_RAW[raw_uses[-1] % len(AT_RAW)], [P, T2], F32)
 
         def row(name):
             return ring.tile([P, S], F32, name=name, tag="row", bufs=ROWS)
 
         idx1 = load_list("idx1", offs)
-        w4_s_raw = keep.tile([P, 1, H], U8, align_bytes=64)
-
-        def load_w4_scales(q):
+        tab_s = place("tab_s", AT_WINDOW, [P, T], U8)
+        nc.sync.dma_start(
+            tab_s[LANDING:, :].bitcast(I32),
+            tab_scales[0].bitcast(I32).unsqueeze(1).to_broadcast([SCALE_ROWS, 2, T // 4]),
+        )
+        nc.vector.memset(tab_s[:LANDING, :].bitcast(I32), 0)
+        w4_s_raw = place("w4_s_raw", AT_W4_S_RAW, [P, H], U8)
+        for q in (0, 2, 1, 3):
             nc.sync.dma_start(
-                w4_s_raw[QUAD * q : QUAD * (q + 1), 0, :].bitcast(I32),
+                w4_s_raw[QUAD * q : QUAD * (q + 1), :].bitcast(I32),
                 w4_scales[0, 4 * q : 4 * q + 4, :].bitcast(I32).unsqueeze(0).to_broadcast([QUAD // 4, 4, H // 4]),
             )
-
-        for q in (0, 2):
-            load_w4_scales(q)
-        tab_s = keep.tile([P, 1, T], U8, tag="bytes_words_out", align_bytes=64)
-        load_scale_rows(nc.sync, tab_s, tab_scales, nc.vector)
-        for q in (1, 3):
-            load_w4_scales(q)
-        w4_raw = keep.tile([P, 2 * H], U8, align_bytes=64)
+        w4_raw = place("w4_raw", AT_W4_RAW, [P, 2 * H], U8)
         nc.sync.dma_start(w4_raw[:].bitcast(I32), w4_words[0].bitcast(I32))
-        tab_w = keep.tile([P, T], U32, tag="table_out", align_bytes=64)
+        tab_w = place("tab_w", AT_TABLE, [P, T], U32)
         nc.sync.dma_start(tab_w[:].bitcast(I32), tab_words[0].rearrange("p t i -> p (t i)").bitcast(I32))
         idx2 = load_list("idx2", offs2)
+        idx3 = load_list("idx3", offs3)
+        idx4 = load_list("idx4", offs4)
+
+        v_s = place("v_s", AT_V_S, [P, S], U8)
+        nc.vector.memset(v_s[:].bitcast(I32), 0)
+        picked = place("picked", AT_PICKED, [P, S], U8)
+        nc.vector.tensor_copy(picked[:], tab_s[:].indirect(idx1[:]))
+        for r in range(4):
+            nc.sync.dma_start(v_s[r:P:QUAD, :].bitcast(I32), picked[LANDING + 2 * r : P : 8, :].bitcast(I32))
         warm = keep.tile([P, 1], F32)
         nc.vector.memset(warm[:], 1.0)
         nc.scalar.activation(warm[:], warm[:], ACT.Abs_reciprocal_sqrt)
@@ -89,7 +124,7 @@ def tile_list_print_run_forecast_kernel(
         wgs_of_slot = {}
 
         def load_wgs(first, count, parts=(slice(0, S),)):
-            part = keep.tile([P, count, S], F32, name="wgs", tag="wgs%d" % first, align_bytes=64)
+            part = place("wgs%d" % first, AT_WGS[first], [P, count, S], F32)
             for cols in parts:
                 for q in (0, 2, 1, 3):
                     nc.sync.dma_start(part[QUAD * q : QUAD * (q + 1), :, cols], wgs_rows[:, first : first + count, cols])
@@ -98,14 +133,10 @@ def tile_list_print_run_forecast_kernel(
 
         load_wgs(0, 1, (slice(0, HALF // 2), slice(HALF // 2, S)))
 
-        pages = [keep.tile([P, T2], F32, name="page%d" % i) for i in range(PAGES)]
-        for tile in pages:
-            nc.vector.memset(tile[:], 0.0)
+        page_even = keep.tile([P, T2], F32)
+        nc.vector.memset(page_even[:], 0.0)
 
-        out_odd = keep.tile([P, T2], F32)
-        nc.vector.memset(out_odd[:], 0.0)
-
-        w4_w = keep.tile([P, 2 * H], U8, align_bytes=64)
+        w4_w = place("w4_w", AT_W4_W, [P, 2 * H], U8)
         w4_s = keep.tile([P, H], U8, align_bytes=64)
         nc.vector.tensor_copy(
             w4_w[:].bitcast(U16).rearrange("p (b t m) -> p b t m", b=PASSES, t=PACK),
@@ -113,13 +144,14 @@ def tile_list_print_run_forecast_kernel(
         )
         nc.vector.tensor_copy(
             w4_s[:].rearrange("p (b t m) -> p b t m", b=PASSES, t=PACK),
-            w4_s_raw[:, 0, :].rearrange("p (b m t) -> p b t m", b=PASSES, t=PACK),
+            w4_s_raw[:].rearrange("p (b m t) -> p b t m", b=PASSES, t=PACK),
         )
 
-        v_s = keep.tile([P, S], U8, align_bytes=64)
-        nc.vector.tensor_copy(v_s[:], tab_s[:, 0, :].indirect(idx1[:]))
+        page_odd = place("page_odd", AT_PAGE_ODD, [P, T2], F32)
+        nc.vector.memset(page_odd[:], 0.0)
+        pages = [page_even, page_odd]
 
-        v_w = keep.tile([P, S], U32, tag="bytes_words_out", align_bytes=64)
+        v_w = place("v_w", AT_V_W, [P, S], U32)
         for i in range(HALVES):
             nc.vector.tensor_copy(
                 v_w[:, HALF * i : HALF * (i + 1)], tab_w[:].indirect(idx1[:, HALF_COLS * i : HALF_COLS * (i + 1)])
@@ -149,7 +181,7 @@ def tile_list_print_run_forecast_kernel(
         load_bf = {}
 
         def round_load(b, c):
-            raw = wide("load_raw")
+            raw = raw_rows()
             raw3 = raw[:].rearrange("p (t c) -> p t c", t=PACK)
             nc.sync.dma_start(
                 raw3,
@@ -183,7 +215,7 @@ def tile_list_print_run_forecast_kernel(
 
         def make_z(b, c, held=False):
             if held:
-                z = keep.tile([P, BANK * PACK], BF16, name="z_held", tag="wgs0", align_bytes=64)
+                z = place("z_held%d" % b, AT_WGS[0], [P, BANK * PACK], BF16)
             else:
                 z = ring.tile([P, BANK * PACK], BF16, name="z", bufs=3, align_bytes=64)
             nc.vector.tensor_tensor(
@@ -210,12 +242,12 @@ def tile_list_print_run_forecast_kernel(
 
         wa_bf = keep.tile([P, PASSES * N * PACK], BF16, align_bytes=64)
         wa_s = keep.tile([P, PASSES * N], U8, align_bytes=64)
-        w8_w = keep.tile([P, PASSES * N], U32, align_bytes=64)
-        w8_s = keep.tile([P, PASSES, N], U8, align_bytes=64)
+        w8_w = place("w8_w", AT_W8_W, [P, PASSES * N], U32)
+        w8_s = place("w8_s", AT_V_S, [P, PASSES, N], U8)
 
         def prepare_second_weights():
             for b in range(PASSES):
-                raw = wide("wa_raw")
+                raw = raw_rows()
                 nc.sync.dma_start(
                     raw[:, : PACK * N], wa[P * PACK * b : P * PACK * (b + 1), :].rearrange("(p t) n -> p (t n)", t=PACK)
                 )
@@ -227,7 +259,7 @@ def tile_list_print_run_forecast_kernel(
                 w8_w[:].bitcast(I32).rearrange("p (a c) -> p a c", a=PASSES),
                 w8_words.rearrange("a p c i -> p a (c i)").bitcast(I32),
             )
-            load_scale_rows(nc.sync, w8_s, w8_scales, nc.vector)
+            load_scale_rows(nc.sync, w8_s, w8_scales, nc.gpsimd)
 
         weights = {}
         for n in range(OUT_TILES):
@@ -264,9 +296,11 @@ def tile_list_print_run_forecast_kernel(
         def empty_bank(which, n, c, cols=slice(0, BANK)):
             if c == 0:
                 if which == "b" and n < 2:
-                    y[which, n] = keep.tile([P, T2], F32, name="y_b", tag="y_b")
+                    y[which, n] = place("y_b%d" % n, AT_Y_B, [P, T2], F32)
+                elif which == "a" and n == OUT_TILES - 1:
+                    y[which, n] = place("y_last", AT_Y_LAST, [P, T2], F32)
                 else:
-                    y[which, n] = wide("y")
+                    y[which, n] = raw_rows()
             nc.scalar.copy(
                 y[which, n][:, BANK * c + cols.start : BANK * c + cols.stop],
                 banks[which, n, c, cols.start][:, : cols.stop - cols.start],
@@ -292,12 +326,12 @@ def tile_list_print_run_forecast_kernel(
             round_page(k)
             if k + ROWS < TILES:
                 first_product(k + ROWS)
-        idx3 = load_list("idx3", offs3)
-        idx4 = load_list("idx4", offs4)
-        wgo_sb = keep.tile([P, M], F32)
+        out_odd = place("out_odd", AT_OUT_ODD, [P, T2], F32)
+        nc.gpsimd.memset(out_odd[:], 0.0)
+        wgo_sb = place("wgo_sb", AT_WGO, [P, M], F32)
         nc.sync.dma_start(wgo_sb[:], wgo)
 
-        late = keep.tile([P, PASSES * P + BANK], U32, tag="wgs2", align_bytes=64)
+        late = place("late", AT_WGS[2], [P, PASSES * P + BANK], U32)
         quantise_wa(0, 1, late[:, : PASSES * P])
         quantise_z(0, CHUNKS - 1, late[:, PASSES * P :])
 
@@ -308,7 +342,7 @@ def tile_list_print_run_forecast_kernel(
                 second_pass(which, 0, c, 0)
         for cols in last_parts:
             second_pass("b", 0, last, 0, cols)
-        two = keep.tile([P, 2 * BANK], U32, tag="wgs1", align_bytes=64)
+        two = place("two", AT_WGS[1], [P, 2 * BANK], U32)
 
         def finish_chunk(c):
             quantise_z(1, c, two[:, BANK * c : BANK * (c + 1)] if c < 2 else new_z_words(1, c))
@@ -378,7 +412,7 @@ def tile_list_print_run_forecast_kernel(
 
         pick_damping(0, 4, 4)
         pick_score(0)
-        wa_last = keep.tile([P, PASSES * P], U32, tag="wgs0", align_bytes=64)
+        wa_last = place("wa_last", AT_WGS[0], [P, PASSES * P], U32)
         quantise_wa(2, 1, wa_last[:])
         place_out(0)
         for n in range(1, OUT_TILES):

@@ -36,22 +36,26 @@ SCALE_ROWS = 16
 LANDING = P - 2 * SCALE_ROWS
 
 AT_TABLE = 0
-AT_PAGE_ODD = 73 * KIB
-AT_WINDOW = 79 * KIB
-AT_WGS0 = 81 * KIB
-AT_PICKED = 20 * KIB
-AT_W4_RAW = 24 * KIB
-AT_W4_S_RAW = 32 * KIB
+AT_PICKED = 16 * KIB
+AT_W4_RAW = 20 * KIB
+AT_W4_S_RAW = 28 * KIB
 AT_RAW = (AT_W4_RAW, AT_W4_S_RAW, AT_TABLE + 8 * KIB)
+AT_Y_B = 36 * KIB
+AT_V_W = 43 * KIB
+AT_W8_LAST = 44 * KIB
+AT_W8_FIRST = 45 * KIB
+AT_OUT_ODD = 49 * KIB
+AT_W4_W = 56 * KIB
+AT_WGO = 57 * KIB
+AT_V_S = 61 * KIB
+AT_Y_LAST = 62 * KIB
+AT_PAGE_ODD = 70 * KIB
+AT_WINDOW = 76 * KIB
+AT_WGS0 = 78 * KIB
+AT_OUT_EVEN = 82 * KIB
+AT_W4_S = 89 * KIB
+AT_WA_BF = 90 * KIB
 AT_WGS = {0: AT_WGS0, 1: AT_PICKED, 2: AT_TABLE}
-AT_Y_B = 40 * KIB
-AT_V_W = 46 * KIB
-AT_W8_W = 48 * KIB
-AT_OUT_ODD = 52 * KIB
-AT_W4_W = 59 * KIB
-AT_WGO = 60 * KIB
-AT_V_S = 64 * KIB
-AT_Y_LAST = 65 * KIB
 
 
 def tile_list_print_run_forecast_kernel(
@@ -137,7 +141,7 @@ def tile_list_print_run_forecast_kernel(
         nc.vector.memset(page_even[:], 0.0)
 
         w4_w = place("w4_w", AT_W4_W, [P, 2 * H], U8)
-        w4_s = keep.tile([P, H], U8, align_bytes=64)
+        w4_s = place("w4_s", AT_W4_S, [P, H], U8)
         nc.vector.tensor_copy(
             w4_w[:].bitcast(U16).rearrange("p (b t m) -> p b t m", b=PASSES, t=PACK),
             w4_raw[:].bitcast(U16).rearrange("p (b m t) -> p b t m", b=PASSES, t=PACK),
@@ -240,9 +244,10 @@ def tile_list_print_run_forecast_kernel(
             words = keep.tile([P, BANK], U32, name="z_w%d%d" % (b, c), align_bytes=64)
             return words[:]
 
-        wa_bf = keep.tile([P, PASSES * N * PACK], BF16, align_bytes=64)
+        wa_bf = place("wa_bf", AT_WA_BF, [P, PASSES * N * PACK], BF16)
         wa_s = keep.tile([P, PASSES * N], U8, align_bytes=64)
-        w8_w = place("w8_w", AT_W8_W, [P, PASSES * N], U32)
+        w8_first = place("w8_first", AT_W8_FIRST, [P, PASSES, 2 * P], U32)
+        w8_last = place("w8_last", AT_W8_LAST, [P, PASSES, P], U32)
         w8_s = place("w8_s", AT_V_S, [P, PASSES, N], U8)
 
         def prepare_second_weights():
@@ -255,17 +260,16 @@ def tile_list_print_run_forecast_kernel(
                     wa_bf[:].rearrange("p (n b c i t) -> p b n c t i", n=OUT_TILES, b=PASSES, i=4, t=PACK)[:, b],
                     raw[:, : PACK * N].rearrange("p (t n c i) -> p n c t i", t=PACK, n=OUT_TILES, i=4),
                 )
-            nc.sync.dma_start(
-                w8_w[:].bitcast(I32).rearrange("p (a c) -> p a c", a=PASSES),
-                w8_words.rearrange("a p c i -> p a (c i)").bitcast(I32),
-            )
+            words = w8_words.rearrange("a p c i -> p a (c i)").bitcast(I32)
+            nc.sync.dma_start(w8_first[:].bitcast(I32), words[:, :, : 2 * P])
+            nc.sync.dma_start(w8_last[:].bitcast(I32), words[:, :, 2 * P :])
             load_scale_rows(nc.sync, w8_s, w8_scales, nc.gpsimd)
 
         weights = {}
         for n in range(OUT_TILES):
             for b in range(PASSES):
                 cols = slice(P * n, P * (n + 1))
-                weights["b", n, b] = (w8_w[:, N * b + P * n : N * b + P * (n + 1)], w8_s[:, b, cols])
+                weights["b", n, b] = (w8_first[:, b, cols] if n < 2 else w8_last[:, b, :], w8_s[:, b, cols])
         banks = {}
 
         def quantise_wa(first, count, words):
@@ -293,15 +297,17 @@ def tile_list_print_run_forecast_kernel(
 
         y = {}
 
-        def empty_bank(which, n, c, cols=slice(0, BANK)):
+        def empty_bank(which, n, c, cols=slice(0, BANK), copy=nc.scalar.copy):
             if c == 0:
-                if which == "b" and n < 2:
+                if which == "b" and n != 1:
                     y[which, n] = place("y_b%d" % n, AT_Y_B, [P, T2], F32)
-                elif which == "a" and n == OUT_TILES - 1:
+                elif which == "b":
+                    y[which, n] = place("y_b1", AT_WA_BF, [P, T2], F32)
+                elif n == OUT_TILES - 1:
                     y[which, n] = place("y_last", AT_Y_LAST, [P, T2], F32)
                 else:
                     y[which, n] = raw_rows()
-            nc.scalar.copy(
+            copy(
                 y[which, n][:, BANK * c + cols.start : BANK * c + cols.stop],
                 banks[which, n, c, cols.start][:, : cols.stop - cols.start],
             )
@@ -321,19 +327,23 @@ def tile_list_print_run_forecast_kernel(
             if k == PACK:
                 for c in range(CHUNKS):
                     make_z(0, c, held=(c == CHUNKS - 1))
-                    if c > 0:
+                    if c in (1, 2):
                         quantise_z(0, c - 1, new_z_words(0, c - 1))
             round_page(k)
             if k + ROWS < TILES:
                 first_product(k + ROWS)
         out_odd = place("out_odd", AT_OUT_ODD, [P, T2], F32)
-        nc.gpsimd.memset(out_odd[:], 0.0)
+        out_even = place("out_even", AT_OUT_EVEN, [P, T2], F32)
+        outs = [out_even, out_odd]
+        for tile in outs:
+            nc.gpsimd.memset(tile[:], 0.0)
         wgo_sb = place("wgo_sb", AT_WGO, [P, M], F32)
         nc.sync.dma_start(wgo_sb[:], wgo)
 
-        late = place("late", AT_WGS[2], [P, PASSES * P + BANK], U32)
+        late = place("late", AT_WGS[2], [P, PASSES * P + 2 * BANK], U32)
         quantise_wa(0, 1, late[:, : PASSES * P])
-        quantise_z(0, CHUNKS - 1, late[:, PASSES * P :])
+        for c in (2, 3):
+            quantise_z(0, c, late[:, PASSES * P + BANK * (c - 2) : PASSES * P + BANK * (c - 1)])
 
         last = CHUNKS - 1
         last_parts = [slice(0, BANK // 2), slice(BANK // 2, BANK)]
@@ -348,31 +358,27 @@ def tile_list_print_run_forecast_kernel(
             quantise_z(1, c, two[:, BANK * c : BANK * (c + 1)] if c < 2 else new_z_words(1, c))
             for which in "ba":
                 second_pass(which, 0, c, 1)
-                empty_bank(which, 0, c)
-
-        def quantise_wa_after_chunk(n, c):
-            words = keep.tile([P, PASSES * P], U32, name="wa_w", tag="page_bf%d" % c, align_bytes=64)
-            quantise_wa(n, 1, words[:])
+                if (which, c) != ("a", last - 1):
+                    empty_bank(which, 0, c)
 
         make_z(1, 0)
         make_z(1, 1)
         finish_chunk(0)
         make_z(1, 2)
         finish_chunk(1)
-        finish_chunk(2)
         make_z(1, 3, held=True)
-        quantise_wa_after_chunk(1, 2)
+        finish_chunk(2)
         last_words = new_z_words(1, last)
         for cols in last_parts:
             quantise_z(1, last, last_words, cols)
             second_pass("b", 0, last, 1, cols)
             empty_bank("b", 0, last, cols)
+        wa_rest = place("wa_rest", AT_WGS[0], [P, 2 * PASSES * P], U32)
+        quantise_wa(1, 2, wa_rest[:])
+        empty_bank("a", 0, last - 1, copy=nc.vector.tensor_copy)
         for b in range(PASSES):
             second_pass("a", 0, last, b)
         empty_bank("a", 0, last)
-        out_even = keep.tile([P, T2], F32, tag="page_bf3", align_bytes=64)
-        nc.vector.memset(out_even[:], 0.0)
-        outs = [out_even, out_odd]
 
         def second_product(which, n):
             for c in range(CHUNKS):
@@ -382,20 +388,20 @@ def tile_list_print_run_forecast_kernel(
 
         damp, score = {}, {}
 
-        def pick_damping(n, gathers, pieces):
-            damp[n] = row("damp")
-            width = M // gathers
-            for i in range(gathers):
-                nc.vector.tensor_copy(
-                    damp[n][:, width * i : width * (i + 1)],
-                    y["b", n][:].indirect(idx3[:, width // 16 * i : width // 16 * (i + 1)]),
-                )
-            width = M // pieces
-            for i in range(pieces):
-                part = damp[n][:, width * i : width * (i + 1)]
-                nc.scalar.activation(part, part, ACT.Abs)
-                nc.scalar.activation(part, part, ACT.Abs_reciprocal_sqrt, bias=1.0)
-                nc.scalar.activation(part, part, ACT.Square)
+        picked_b = {}
+
+        def pick_damping(n):
+            picked_b[n] = row("picked_b")
+            nc.vector.tensor_copy(picked_b[n][:], y["b", n][:].indirect(idx3[:]))
+
+        def make_damping(n):
+            damp[n] = place("damp0", AT_W8_FIRST, [P, M], F32) if n == 0 else picked_b[n]
+            for cols in halves:
+                nc.scalar.activation(damp[n][:, cols], picked_b[n][:, cols], ACT.Abs)
+            for cols in halves:
+                nc.scalar.activation(damp[n][:, cols], damp[n][:, cols], ACT.Abs_reciprocal_sqrt, bias=1.0)
+            for cols in halves:
+                nc.scalar.activation(damp[n][:, cols], damp[n][:, cols], ACT.Square)
 
         def pick_score(n):
             score[n] = row("score")
@@ -410,16 +416,19 @@ def tile_list_print_run_forecast_kernel(
                 for queue, cols in ((nc.sync, slice(0, T2 // 2)), (nc.scalar, slice(T2 // 2, T2))):
                     queue.dma_start(out[P * n : P * (n + 1), cols], placed[:, cols])
 
-        pick_damping(0, 4, 4)
+        pick_damping(0)
         pick_score(0)
-        wa_last = place("wa_last", AT_WGS[0], [P, PASSES * P], U32)
-        quantise_wa(2, 1, wa_last[:])
+        second_product("b", 1)
+        pick_damping(1)
+        make_damping(0)
         place_out(0)
-        for n in range(1, OUT_TILES):
-            second_product("b", n)
-            second_product("a", n)
-        for n in range(1, OUT_TILES):
-            pick_damping(n, 1, 2)
-            pick_score(n)
-        for n in range(1, OUT_TILES):
-            place_out(n)
+        second_product("a", 1)
+        second_product("b", 2)
+        make_damping(1)
+        second_product("a", 2)
+        pick_score(1)
+        pick_damping(2)
+        make_damping(2)
+        pick_score(2)
+        place_out(1)
+        place_out(2)

@@ -34,28 +34,28 @@ HALF_COLS = HALF // 16
 KIB = 1024
 SCALE_ROWS = 16
 LANDING = P - 2 * SCALE_ROWS
+LEAD = HALF // 2
 
-AT_TABLE = 0
-AT_PICKED = 16 * KIB
-AT_W4_RAW = 20 * KIB
-AT_W4_S_RAW = 28 * KIB
-AT_RAW = (AT_W4_RAW, AT_W4_S_RAW, AT_TABLE + 8 * KIB)
-AT_Y_B = 36 * KIB
-AT_V_W = 43 * KIB
-AT_W8_LAST = 44 * KIB
-AT_W8_FIRST = 45 * KIB
-AT_OUT_ODD = 49 * KIB
-AT_W4_W = 56 * KIB
-AT_WGO = 57 * KIB
-AT_V_S = 61 * KIB
-AT_Y_LAST = 62 * KIB
-AT_PAGE_ODD = 70 * KIB
-AT_WINDOW = 76 * KIB
-AT_WGS0 = 78 * KIB
-AT_OUT_EVEN = 82 * KIB
-AT_W4_S = 89 * KIB
-AT_WA_BF = 90 * KIB
-AT_WGS = {0: AT_WGS0, 1: AT_PICKED, 2: AT_TABLE}
+AT_TABLE = 8 * KIB - 64
+AT_WGS = {0: 31 * KIB, 1: 16 * KIB, 2: 8 * KIB}
+AT_W4_RAW = 34 * KIB
+AT_RAW = (35 * KIB, 0, 23 * KIB)
+AT_Y_B = 43 * KIB
+AT_V_W = 50 * KIB
+AT_W8_LAST = 51 * KIB
+AT_W8_FIRST = 52 * KIB
+AT_OUT_ODD = 56 * KIB
+AT_W4_W = 63 * KIB
+AT_WGO = 64 * KIB
+AT_Y_LAST = 68 * KIB
+AT_WINDOW = 68 * KIB
+AT_W4_S_RAW = 72 * KIB
+AT_STAGED = 73 * KIB
+AT_PAGE_ODD = 76 * KIB
+AT_OUT_EVEN = 84 * KIB
+AT_PLANES = 91 * KIB
+AT_W8_S = 92 * KIB
+AT_WA_BF = 93 * KIB
 
 
 def tile_list_print_run_forecast_kernel(
@@ -93,67 +93,66 @@ def tile_list_print_run_forecast_kernel(
         def row(name):
             return ring.tile([P, S], F32, name=name, tag="row", bufs=ROWS)
 
-        idx1 = load_list("idx1", offs)
-        tab_s = place("tab_s", AT_WINDOW, [P, T], U8)
-        nc.sync.dma_start(
-            tab_s[LANDING:, :].bitcast(I32),
-            tab_scales[0].bitcast(I32).unsqueeze(1).to_broadcast([SCALE_ROWS, 2, T // 4]),
-        )
-        nc.vector.memset(tab_s[:LANDING, :].bitcast(I32), 0)
-        w4_s_raw = place("w4_s_raw", AT_W4_S_RAW, [P, H], U8)
-        for q in (0, 2, 1, 3):
+        def land_scale_rows(name, offset, src, width):
+            tile = place(name, offset, [P, width], U8)
             nc.sync.dma_start(
-                w4_s_raw[QUAD * q : QUAD * (q + 1), :].bitcast(I32),
-                w4_scales[0, 4 * q : 4 * q + 4, :].bitcast(I32).unsqueeze(0).to_broadcast([QUAD // 4, 4, H // 4]),
+                tile[LANDING:, :].bitcast(I32),
+                src.bitcast(I32).unsqueeze(1).to_broadcast([SCALE_ROWS, 2, width // 4]),
             )
+            nc.gpsimd.memset(tile[:LANDING, :].bitcast(I32), 0)
+            return tile
+
+        idx1 = load_list("idx1", offs)
+        tab_s = land_scale_rows("tab_s", AT_WINDOW, tab_scales[0], T)
+        w4_s_raw = land_scale_rows("w4_s_raw", AT_W4_S_RAW, w4_scales[0], H)
         w4_raw = place("w4_raw", AT_W4_RAW, [P, 2 * H], U8)
         nc.sync.dma_start(w4_raw[:].bitcast(I32), w4_words[0].bitcast(I32))
+        idx2 = load_list("idx2", offs2)
         tab_w = place("tab_w", AT_TABLE, [P, T], U32)
         nc.sync.dma_start(tab_w[:].bitcast(I32), tab_words[0].rearrange("p t i -> p (t i)").bitcast(I32))
-        idx2 = load_list("idx2", offs2)
+        wgs_rows = wgs.rearrange("(q t) j -> q t j", t=PACK)
+        wgs_lead = place("wgs_lead", AT_PAGE_ODD, [P, LEAD], F32)
+        nc.sync.dma_start(wgs_lead[:], wgs_rows[:, 0, :LEAD].unsqueeze(0).to_broadcast([QUADS, QUAD, LEAD]))
         idx3 = load_list("idx3", offs3)
         idx4 = load_list("idx4", offs4)
 
-        v_s = place("v_s", AT_V_S, [P, S], U8)
-        nc.vector.memset(v_s[:].bitcast(I32), 0)
-        picked = place("picked", AT_PICKED, [P, S], U8)
+        planes = place("planes", AT_PLANES, [P, H + S], U8)
+        nc.vector.memset(planes[:].bitcast(I32), 0)
+        w4_s, v_s = planes[:, :H], planes[:, H:]
+        picked = place("picked", AT_W4_W, [P, S], U8)
         nc.vector.tensor_copy(picked[:], tab_s[:].indirect(idx1[:]))
-        for r in range(4):
-            nc.sync.dma_start(v_s[r:P:QUAD, :].bitcast(I32), picked[LANDING + 2 * r : P : 8, :].bitcast(I32))
+        staged = place("staged", AT_STAGED, [P, H + S], U8)
+        nc.vector.tensor_copy(
+            staged[:, :H].rearrange("p (b t m) -> p b t m", b=PASSES, t=PACK),
+            w4_s_raw[:].rearrange("p (b m t) -> p b t m", b=PASSES, t=PACK),
+        )
+        nc.vector.tensor_copy(staged[:, H:].bitcast(I32), picked[:].bitcast(I32))
         warm = keep.tile([P, 1], F32)
         nc.vector.memset(warm[:], 1.0)
         nc.scalar.activation(warm[:], warm[:], ACT.Abs_reciprocal_sqrt)
-
-        wgs_rows = wgs.rearrange("(q t) j -> q t j", t=PACK)
-        wgs_of_slot = {}
-
-        def load_wgs(first, count, parts=(slice(0, S),)):
-            part = place("wgs%d" % first, AT_WGS[first], [P, count, S], F32)
-            for cols in parts:
-                for q in (0, 2, 1, 3):
-                    nc.sync.dma_start(part[QUAD * q : QUAD * (q + 1), :, cols], wgs_rows[:, first : first + count, cols])
-            for i in range(count):
-                wgs_of_slot[first + i] = part[:, i, :]
-
-        load_wgs(0, 1, (slice(0, HALF // 2), slice(HALF // 2, S)))
-
-        page_even = keep.tile([P, T2], F32)
-        nc.vector.memset(page_even[:], 0.0)
+        for r in range(4):
+            nc.scalar.dma_start(planes[r:P:QUAD, :].bitcast(I32), staged[LANDING + 2 * r : P : 8, :].bitcast(I32))
 
         w4_w = place("w4_w", AT_W4_W, [P, 2 * H], U8)
-        w4_s = place("w4_s", AT_W4_S, [P, H], U8)
         nc.vector.tensor_copy(
             w4_w[:].bitcast(U16).rearrange("p (b t m) -> p b t m", b=PASSES, t=PACK),
             w4_raw[:].bitcast(U16).rearrange("p (b m t) -> p b t m", b=PASSES, t=PACK),
         )
-        nc.vector.tensor_copy(
-            w4_s[:].rearrange("p (b t m) -> p b t m", b=PASSES, t=PACK),
-            w4_s_raw[:].rearrange("p (b m t) -> p b t m", b=PASSES, t=PACK),
-        )
 
-        page_odd = place("page_odd", AT_PAGE_ODD, [P, T2], F32)
-        nc.vector.memset(page_odd[:], 0.0)
-        pages = [page_even, page_odd]
+        wgs_of_slot = {}
+
+        def load_wgs(first, count):
+            part = place("wgs%d" % first, AT_WGS[first], [P, count, S], F32)
+            for q in (0, 2, 1, 3):
+                nc.sync.dma_start(part[QUAD * q : QUAD * (q + 1), :, :], wgs_rows[:, first : first + count, :])
+            for i in range(count):
+                wgs_of_slot[first + i] = part[:, i, :]
+
+        load_wgs(0, 1)
+
+        page_even = keep.tile([P, T2], F32)
+        nc.vector.memset(page_even[:], 0.0)
+        pages = [page_even]
 
         v_w = place("v_w", AT_V_W, [P, S], U32)
         for i in range(HALVES):
@@ -201,10 +200,11 @@ def tile_list_print_run_forecast_kernel(
         def place_h(k):
             page, h, w = pages[k % PAGES], h_tiles[k], wgs_of_slot[k % PACK]
             if k == 0:
-                for cols in (slice(0, HALF // 2), slice(HALF // 2, S)):
-                    nc.vector.tensor_tensor(
-                        page[:].indirect(idx2[:, cols.start // 16 : cols.stop // 16]), h[:, cols], w[:, cols], MULT
-                    )
+                nc.vector.tensor_tensor(page[:].indirect(idx2[:, : LEAD // 16]), h[:, :LEAD], wgs_lead[:], MULT)
+                page_odd = place("page_odd", AT_PAGE_ODD, [P, T2], F32)
+                nc.gpsimd.memset(page_odd[:], 0.0)
+                pages.append(page_odd)
+                nc.vector.tensor_tensor(page[:].indirect(idx2[:, LEAD // 16 :]), h[:, LEAD:], w[:, LEAD:], MULT)
             else:
                 nc.vector.tensor_tensor(page[:].indirect(idx2[:]), h[:], w, MULT)
 
@@ -248,7 +248,7 @@ def tile_list_print_run_forecast_kernel(
         wa_s = keep.tile([P, PASSES * N], U8, align_bytes=64)
         w8_first = place("w8_first", AT_W8_FIRST, [P, PASSES, 2 * P], U32)
         w8_last = place("w8_last", AT_W8_LAST, [P, PASSES, P], U32)
-        w8_s = place("w8_s", AT_V_S, [P, PASSES, N], U8)
+        w8_s = place("w8_s", AT_W8_S, [P, PASSES, N], U8)
 
         def prepare_second_weights():
             for b in range(PASSES):

@@ -1,6 +1,7 @@
 from contextlib import ExitStack
 
 import concourse.mybir as mybir
+from concourse.masks import make_identity
 
 K, T, S, H, T2, M, N = 512, 4096, 1024, 1024, 2048, 1024, 384
 FLOPS = 2 * K * H * S + 2 * 2 * H * N * T2
@@ -108,11 +109,11 @@ def tile_list_print_run_forecast_kernel(
         w4_raw = place("w4_raw", AT_W4_RAW, [P, 2 * H], U8)
         nc.sync.dma_start(w4_raw[:].bitcast(I32), w4_words[0].bitcast(I32))
         idx2 = load_list("idx2", offs2)
+        lead_rows = keep.tile([P, LEAD], F32)
+        nc.sync.dma_start(lead_rows[:], wgs[:, :LEAD])
         tab_w = place("tab_w", AT_TABLE, [P, T], U32)
         nc.sync.dma_start(tab_w[:].bitcast(I32), tab_words[0].rearrange("p t i -> p (t i)").bitcast(I32))
         wgs_rows = wgs.rearrange("(q t) j -> q t j", t=PACK)
-        wgs_lead = place("wgs_lead", AT_PAGE_ODD, [P, LEAD], F32)
-        nc.sync.dma_start(wgs_lead[:], wgs_rows[:, 0, :LEAD].unsqueeze(0).to_broadcast([QUADS, QUAD, LEAD]))
         idx3 = load_list("idx3", offs3)
         idx4 = load_list("idx4", offs4)
 
@@ -130,6 +131,23 @@ def tile_list_print_run_forecast_kernel(
         warm = keep.tile([P, 1], F32)
         nc.vector.memset(warm[:], 1.0)
         nc.scalar.activation(warm[:], warm[:], ACT.Abs_reciprocal_sqrt)
+
+        identity = keep.tile([P, P], F32)
+        make_identity(nc, identity[:])
+        blocks = LEAD // P
+        turned = psum.tile([P, BANK], F32, name="bank")
+        for i in range(blocks):
+            nc.tensor.transpose(turned[:, P * i : P * (i + 1)], lead_rows[:, P * i : P * (i + 1)], identity[:])
+        dealt = keep.tile([P, blocks, QUADS, QUAD], F32)
+        nc.scalar.copy(
+            dealt[:],
+            turned[:, :LEAD].rearrange("p (b q t) -> p b t q", b=blocks, t=PACK)[:, :, 0:1, :].to_broadcast([P, blocks, QUADS, QUAD]),
+        )
+        back = psum.tile([P, BANK], F32, name="bank")
+        for i in range(blocks):
+            nc.tensor.transpose(back[:, P * i : P * (i + 1)], dealt[:, i].rearrange("p a q -> p (a q)"), identity[:])
+        wgs_lead = place("wgs_lead", AT_PAGE_ODD, [P, LEAD], F32)
+        nc.scalar.copy(wgs_lead[:], back[:, :LEAD])
         for r in range(4):
             nc.scalar.dma_start(planes[r:P:QUAD, :].bitcast(I32), staged[LANDING + 2 * r : P : 8, :].bitcast(I32))
 

@@ -38,25 +38,30 @@ LANDING = P - 2 * SCALE_ROWS
 LEAD = HALF // 2
 
 AT_TABLE = 8 * KIB - 64
-AT_WGS = {0: 31 * KIB, 1: 16 * KIB, 2: 8 * KIB}
+AT_WGS = {0: 31 * KIB, 1: 35 * KIB, 2: 8 * KIB}
 AT_W4_RAW = 34 * KIB
-AT_RAW = (35 * KIB, 0, 23 * KIB)
+AT_RAW = (129 * KIB, 0, 23 * KIB)
 AT_Y_B = 43 * KIB
 AT_V_W = 50 * KIB
 AT_W8_LAST = 51 * KIB
 AT_W8_FIRST = 52 * KIB
 AT_OUT_ODD = 56 * KIB
 AT_W4_W = 63 * KIB
-AT_WGO = 64 * KIB
-AT_Y_LAST = 68 * KIB
+AT_Y_LAST = 64 * KIB
 AT_WINDOW = 68 * KIB
 AT_W4_S_RAW = 72 * KIB
-AT_STAGED = 73 * KIB
+AT_STAGED = 129 * KIB
 AT_PAGE_ODD = 76 * KIB
 AT_OUT_EVEN = 84 * KIB
 AT_PLANES = 91 * KIB
 AT_W8_S = 92 * KIB
 AT_WA_BF = 93 * KIB
+AT_SLOTS = [(101 + 4 * i) * KIB for i in range(7)]
+AT_H = AT_SLOTS[:3] + [AT_WA_BF] + AT_SLOTS[3:6] + AT_SLOTS[:1]
+AT_LOAD_BF = AT_H[:3] + AT_SLOTS[6:] + [AT_H[4], AT_H[1], AT_H[5], AT_H[6]]
+AT_WGO = AT_SLOTS[6]
+AT_RAW_SPARE = {(0, CHUNKS - 1): AT_Y_B, (1, 0): AT_Y_LAST}
+AHEAD = TILES - 1
 
 
 def tile_list_print_run_forecast_kernel(
@@ -183,7 +188,7 @@ def tile_list_print_run_forecast_kernel(
         first_parts = [slice(0, HALF // 2), slice(HALF // 2, HALF), slice(HALF, S)]
 
         def first_product(k):
-            h = row("h")
+            h = place("h%d" % k, AT_H[k], [P, S], F32)
             for cols in first_parts if k == 0 else halves:
                 bank = psum.tile([P, BANK], F32, name="bank")
                 width = cols.stop - cols.start
@@ -202,13 +207,13 @@ def tile_list_print_run_forecast_kernel(
         load_bf = {}
 
         def round_load(b, c):
-            raw = raw_rows()
+            raw = place("spare%d" % b, AT_RAW_SPARE[b, c], [P, T2], F32) if (b, c) in AT_RAW_SPARE else raw_rows()
             raw3 = raw[:].rearrange("p (t c) -> p t c", t=PACK)
             nc.sync.dma_start(
                 raw3,
                 load[P * PACK * b : P * PACK * (b + 1), BANK * c : BANK * (c + 1)].rearrange("(p t) c -> p t c", t=PACK),
             )
-            rounded = ring.tile([P, BANK * PACK], BF16, name="load_bf", bufs=8)
+            rounded = place("load_bf%d%d" % (b, c), AT_LOAD_BF[CHUNKS * b + c], [P, BANK * PACK], BF16)
             nc.scalar.copy(
                 rounded[:].rearrange("p (c i t) -> p c t i", i=4, t=PACK),
                 raw[:].rearrange("p (t c i) -> p c t i", t=PACK, i=4),
@@ -330,26 +335,29 @@ def tile_list_print_run_forecast_kernel(
                 banks[which, n, c, cols.start][:, : cols.stop - cols.start],
             )
 
-        for k in range(ROWS):
+        for k in range(AHEAD):
             first_product(k)
         for k in range(TILES):
             if k in (1, 2):
                 load_wgs(k, k)
-            if k <= PACK:
-                round_load(k // PACK, k % PACK)
-            if PACK <= k < TILES - 1:
-                round_load(1, k + 1 - PACK)
-            if k == PACK:
-                prepare_second_weights()
             place_h(k)
             if k == PACK:
+                round_load(1, 0)
                 for c in range(CHUNKS):
                     make_z(0, c, held=(c == CHUNKS - 1))
                     if c in (1, 2):
                         quantise_z(0, c - 1, new_z_words(0, c - 1))
             round_page(k)
-            if k + ROWS < TILES:
-                first_product(k + ROWS)
+            if k < PACK - 1:
+                round_load(0, k)
+            if k == PACK - 2:
+                round_load(0, k + 1)
+            if k == PACK - 1:
+                prepare_second_weights()
+            if k == PACK:
+                first_product(AHEAD)
+            if PACK <= k < TILES - 1:
+                round_load(1, k + 1 - PACK)
         out_odd = place("out_odd", AT_OUT_ODD, [P, T2], F32)
         out_even = place("out_even", AT_OUT_EVEN, [P, T2], F32)
         outs = [out_even, out_odd]

@@ -1,7 +1,6 @@
 from contextlib import ExitStack
 
 import concourse.mybir as mybir
-from concourse.masks import make_identity
 
 K, T, S, H, T2, M, N = 512, 4096, 1024, 1024, 2048, 1024, 384
 FLOPS = 2 * K * H * S + 2 * 2 * H * N * T2
@@ -39,8 +38,7 @@ LEAD = HALF // 2
 
 AT_TABLE = 8 * KIB - 64
 AT_WGS = {0: 31 * KIB, 1: 35 * KIB, 2: 8 * KIB}
-AT_W4_RAW = 34 * KIB
-AT_RAW = (129 * KIB, 0, 23 * KIB)
+AT_RAW = (138 * KIB, 0, 23 * KIB)
 AT_Y_B = 43 * KIB
 AT_V_W = 50 * KIB
 AT_W8_LAST = 51 * KIB
@@ -50,8 +48,12 @@ AT_W4_W = 63 * KIB
 AT_Y_LAST = 64 * KIB
 AT_WINDOW = 68 * KIB
 AT_W4_S_RAW = 72 * KIB
-AT_STAGED = 129 * KIB
+AT_PAGE_EVEN = 129 * KIB
 AT_PAGE_ODD = 76 * KIB
+AT_STAGED = 137 * KIB
+AT_W4_SECOND = 137 * KIB
+AT_PICKED = 35 * KIB - 512
+AT_LEAD = AT_PAGE_ODD
 AT_OUT_EVEN = 84 * KIB
 AT_PLANES = 91 * KIB
 AT_W8_S = 92 * KIB
@@ -108,24 +110,45 @@ def tile_list_print_run_forecast_kernel(
             nc.gpsimd.memset(tile[:LANDING, :].bitcast(I32), 0)
             return tile
 
+        warm = keep.tile([P, 1], F32)
+        nc.gpsimd.memset(warm[:], 1.0)
+        nc.scalar.activation(warm[:], warm[:], ACT.Abs_reciprocal_sqrt)
+
         idx1 = load_list("idx1", offs)
         tab_s = land_scale_rows("tab_s", AT_WINDOW, tab_scales[0], T)
         w4_s_raw = land_scale_rows("w4_s_raw", AT_W4_S_RAW, w4_scales[0], H)
-        w4_raw = place("w4_raw", AT_W4_RAW, [P, 2 * H], U8)
-        nc.sync.dma_start(w4_raw[:].bitcast(I32), w4_words[0].bitcast(I32))
+        wgs_rows = wgs.rearrange("(q t) j -> q t j", t=PACK)
+        wgs_lead = place("wgs_lead", AT_LEAD, [P, LEAD], F32)
+        for q in range(QUADS // 2):
+            nc.sync.dma_start(wgs_lead[QUAD * q : QUAD * (q + 1), :], wgs_rows[:, 0, :LEAD])
+        nc.scalar.copy(wgs_lead[P // 2 :, :], wgs_lead[: P // 2, :])
         idx2 = load_list("idx2", offs2)
-        lead_rows = keep.tile([P, LEAD], F32)
-        nc.sync.dma_start(lead_rows[:], wgs[:, :LEAD])
+        idx3 = load_list("idx3", offs3)
         tab_w = place("tab_w", AT_TABLE, [P, T], U32)
         nc.sync.dma_start(tab_w[:].bitcast(I32), tab_words[0].rearrange("p t i -> p (t i)").bitcast(I32))
-        wgs_rows = wgs.rearrange("(q t) j -> q t j", t=PACK)
-        idx3 = load_list("idx3", offs3)
+        w4_w = place("w4_w", AT_W4_W, [P, 2 * H], U8)
+
+        def load_w4(b, raw):
+            nc.sync.dma_start(raw[:].bitcast(I32), w4_words[0].bitcast(I32)[:, 2 * P * b : 2 * P * (b + 1)])
+
+        def deal_w4(b, raw):
+            nc.scalar.copy(
+                w4_w[:, H * b : H * (b + 1)].bitcast(U16).rearrange("p (t m) -> p t m", t=PACK),
+                raw[:].bitcast(U16).rearrange("p (m t) -> p t m", t=PACK),
+            )
+
+        w4_first = keep.tile([P, H], U8)
+        load_w4(0, w4_first)
         idx4 = load_list("idx4", offs4)
+        wgs_of_slot = {}
 
         planes = place("planes", AT_PLANES, [P, H + S], U8)
-        nc.vector.memset(planes[:].bitcast(I32), 0)
+        nc.gpsimd.memset(planes[:].bitcast(I32), 0)
         w4_s, v_s = planes[:, :H], planes[:, H:]
-        picked = place("picked", AT_W4_W, [P, S], U8)
+        page_even = place("page_even", AT_PAGE_EVEN, [P, T2], F32)
+        nc.gpsimd.memset(page_even[:], 0.0)
+
+        picked = place("picked", AT_PICKED, [P, S], U8)
         nc.vector.tensor_copy(picked[:], tab_s[:].indirect(idx1[:]))
         staged = place("staged", AT_STAGED, [P, H + S], U8)
         nc.vector.tensor_copy(
@@ -133,36 +156,11 @@ def tile_list_print_run_forecast_kernel(
             w4_s_raw[:].rearrange("p (b m t) -> p b t m", b=PASSES, t=PACK),
         )
         nc.vector.tensor_copy(staged[:, H:].bitcast(I32), picked[:].bitcast(I32))
-        warm = keep.tile([P, 1], F32)
-        nc.vector.memset(warm[:], 1.0)
-        nc.scalar.activation(warm[:], warm[:], ACT.Abs_reciprocal_sqrt)
-
-        identity = keep.tile([P, P], F32)
-        make_identity(nc, identity[:])
-        blocks = LEAD // P
-        turned = psum.tile([P, BANK], F32, name="bank")
-        for i in range(blocks):
-            nc.tensor.transpose(turned[:, P * i : P * (i + 1)], lead_rows[:, P * i : P * (i + 1)], identity[:])
-        dealt = keep.tile([P, blocks, QUADS, QUAD], F32)
-        nc.scalar.copy(
-            dealt[:],
-            turned[:, :LEAD].rearrange("p (b q t) -> p b t q", b=blocks, t=PACK)[:, :, 0:1, :].to_broadcast([P, blocks, QUADS, QUAD]),
-        )
-        back = psum.tile([P, BANK], F32, name="bank")
-        for i in range(blocks):
-            nc.tensor.transpose(back[:, P * i : P * (i + 1)], dealt[:, i].rearrange("p a q -> p (a q)"), identity[:])
-        wgs_lead = place("wgs_lead", AT_PAGE_ODD, [P, LEAD], F32)
-        nc.scalar.copy(wgs_lead[:], back[:, :LEAD])
         for r in range(4):
-            nc.scalar.dma_start(planes[r:P:QUAD, :].bitcast(I32), staged[LANDING + 2 * r : P : 8, :].bitcast(I32))
+            nc.sync.dma_start(planes[r:P:QUAD, :].bitcast(I32), staged[LANDING + 2 * r : P : 8, :].bitcast(I32))
+        pages = [page_even]
 
-        w4_w = place("w4_w", AT_W4_W, [P, 2 * H], U8)
-        nc.vector.tensor_copy(
-            w4_w[:].bitcast(U16).rearrange("p (b t m) -> p b t m", b=PASSES, t=PACK),
-            w4_raw[:].bitcast(U16).rearrange("p (b m t) -> p b t m", b=PASSES, t=PACK),
-        )
-
-        wgs_of_slot = {}
+        deal_w4(0, w4_first)
 
         def load_wgs(first, count):
             part = place("wgs%d" % first, AT_WGS[first], [P, count, S], F32)
@@ -172,10 +170,8 @@ def tile_list_print_run_forecast_kernel(
                 wgs_of_slot[first + i] = part[:, i, :]
 
         load_wgs(0, 1)
-
-        page_even = keep.tile([P, T2], F32)
-        nc.vector.memset(page_even[:], 0.0)
-        pages = [page_even]
+        w4_second = place("w4_second", AT_W4_SECOND, [P, H], U8)
+        load_w4(1, w4_second)
 
         v_w = place("v_w", AT_V_W, [P, S], U32)
         for i in range(HALVES):
@@ -336,6 +332,8 @@ def tile_list_print_run_forecast_kernel(
             )
 
         for k in range(AHEAD):
+            if k == PACK:
+                deal_w4(1, w4_second)
             first_product(k)
         for k in range(TILES):
             if k in (1, 2):
@@ -345,8 +343,6 @@ def tile_list_print_run_forecast_kernel(
                 round_load(1, 0)
                 for c in range(CHUNKS):
                     make_z(0, c, held=(c == CHUNKS - 1))
-                    if c in (1, 2):
-                        quantise_z(0, c - 1, new_z_words(0, c - 1))
             round_page(k)
             if k < PACK - 1:
                 round_load(0, k)
@@ -366,10 +362,10 @@ def tile_list_print_run_forecast_kernel(
         wgo_sb = place("wgo_sb", AT_WGO, [P, M], F32)
         nc.sync.dma_start(wgo_sb[:], wgo)
 
-        late = place("late", AT_WGS[2], [P, PASSES * P + 2 * BANK], U32)
+        late = place("late", AT_WGS[2], [P, PASSES * P + CHUNKS * BANK], U32)
         quantise_wa(0, 1, late[:, : PASSES * P])
-        for c in (2, 3):
-            quantise_z(0, c, late[:, PASSES * P + BANK * (c - 2) : PASSES * P + BANK * (c - 1)])
+        for c in range(CHUNKS):
+            quantise_z(0, c, late[:, PASSES * P + BANK * c : PASSES * P + BANK * (c + 1)])
 
         last = CHUNKS - 1
         last_parts = [slice(0, BANK // 2), slice(BANK // 2, BANK)]

@@ -30,7 +30,6 @@ PAGES = 2
 ROWS = 6
 HALVES = 2
 HALF = S // HALVES
-HALF_COLS = HALF // 16
 KIB = 1024
 SCALE_ROWS = 16
 LANDING = P - 2 * SCALE_ROWS
@@ -47,8 +46,8 @@ AT_OUT_ODD = 56 * KIB
 AT_W4_W = 63 * KIB
 AT_Y_LAST = 64 * KIB
 AT_WINDOW = 68 * KIB
-AT_W4_S_RAW = 72 * KIB
 AT_PAGE_EVEN = 129 * KIB
+AT_W4_S_RAW = AT_PAGE_EVEN
 AT_PAGE_ODD = 76 * KIB
 AT_STAGED = 137 * KIB
 AT_W4_SECOND = 137 * KIB
@@ -61,6 +60,13 @@ AT_WA_BF = 93 * KIB
 AT_SLOTS = [(101 + 4 * i) * KIB for i in range(7)]
 AT_H = AT_SLOTS[:3] + [AT_WA_BF] + AT_SLOTS[3:6] + AT_SLOTS[:1]
 AT_LOAD_BF = AT_H[:3] + AT_SLOTS[6:] + [AT_H[4], AT_H[1], AT_H[5], AT_H[6]]
+AT_Y_B1 = AT_PAGE_EVEN
+AT_Z_SLOTS = [(146 + 4 * i) * KIB for i in range(4)]
+AT_Z = {
+    (0, 0): AT_Z_SLOTS[0], (0, 1): AT_Z_SLOTS[1], (0, 2): AT_Z_SLOTS[2], (0, 3): AT_WGS[0],
+    (1, 0): AT_Z_SLOTS[3], (1, 1): AT_Z_SLOTS[0], (1, 2): AT_Z_SLOTS[1], (1, 3): AT_Z_SLOTS[2],
+}
+AT_WA_WORDS = AT_Z_SLOTS[2]
 AT_WGO = AT_SLOTS[6]
 AT_RAW_SPARE = {(0, CHUNKS - 1): AT_Y_B, (1, 0): AT_Y_LAST}
 AHEAD = TILES - 1
@@ -76,7 +82,7 @@ def tile_list_print_run_forecast_kernel(
         keep = ctx.enter_context(tc.tile_pool(name="keep", bufs=1))
         ring = ctx.enter_context(tc.tile_pool(name="ring", bufs=1))
         placed = ctx.enter_context(tc.tile_pool(name="placed", bufs=1))
-        psum = ctx.enter_context(tc.psum_pool(name="psum", bufs=8))
+        psum = ctx.enter_context(tc.psum_pool(name="psum", bufs=1))
 
         def place(name, offset, shape, dtype):
             return placed.tile(shape, dtype, name=name, tag=name, offset=offset, align_bytes=64)
@@ -111,7 +117,7 @@ def tile_list_print_run_forecast_kernel(
             return tile
 
         warm = keep.tile([P, 1], F32)
-        nc.gpsimd.memset(warm[:], 1.0)
+        nc.vector.memset(warm[:], 1.0)
         nc.scalar.activation(warm[:], warm[:], ACT.Abs_reciprocal_sqrt)
 
         idx1 = load_list("idx1", offs)
@@ -131,10 +137,10 @@ def tile_list_print_run_forecast_kernel(
         def load_w4(b, raw):
             nc.sync.dma_start(raw[:].bitcast(I32), w4_words[0].bitcast(I32)[:, 2 * P * b : 2 * P * (b + 1)])
 
-        def deal_w4(b, raw):
+        def deal_w4(b, raw, slots=slice(0, PACK)):
             nc.scalar.copy(
-                w4_w[:, H * b : H * (b + 1)].bitcast(U16).rearrange("p (t m) -> p t m", t=PACK),
-                raw[:].bitcast(U16).rearrange("p (m t) -> p t m", t=PACK),
+                w4_w[:, H * b : H * (b + 1)].bitcast(U16).rearrange("p (t m) -> p t m", t=PACK)[:, slots],
+                raw[:].bitcast(U16).rearrange("p (m t) -> p t m", t=PACK)[:, slots],
             )
 
         w4_first = keep.tile([P, H], U8)
@@ -143,11 +149,8 @@ def tile_list_print_run_forecast_kernel(
         wgs_of_slot = {}
 
         planes = place("planes", AT_PLANES, [P, H + S], U8)
-        nc.gpsimd.memset(planes[:].bitcast(I32), 0)
+        nc.vector.memset(planes[:].bitcast(I32), 0)
         w4_s, v_s = planes[:, :H], planes[:, H:]
-        page_even = place("page_even", AT_PAGE_EVEN, [P, T2], F32)
-        nc.gpsimd.memset(page_even[:], 0.0)
-
         picked = place("picked", AT_PICKED, [P, S], U8)
         nc.vector.tensor_copy(picked[:], tab_s[:].indirect(idx1[:]))
         staged = place("staged", AT_STAGED, [P, H + S], U8)
@@ -158,9 +161,12 @@ def tile_list_print_run_forecast_kernel(
         nc.vector.tensor_copy(staged[:, H:].bitcast(I32), picked[:].bitcast(I32))
         for r in range(4):
             nc.sync.dma_start(planes[r:P:QUAD, :].bitcast(I32), staged[LANDING + 2 * r : P : 8, :].bitcast(I32))
+        page_even = place("page_even", AT_PAGE_EVEN, [P, T2], F32)
+        nc.vector.memset(page_even[:], 0.0)
         pages = [page_even]
 
-        deal_w4(0, w4_first)
+        deal_w4(0, w4_first, slice(0, 1))
+        deal_w4(0, w4_first, slice(1, PACK))
 
         def load_wgs(first, count):
             part = place("wgs%d" % first, AT_WGS[first], [P, count, S], F32)
@@ -174,19 +180,17 @@ def tile_list_print_run_forecast_kernel(
         load_w4(1, w4_second)
 
         v_w = place("v_w", AT_V_W, [P, S], U32)
-        for i in range(HALVES):
-            nc.vector.tensor_copy(
-                v_w[:, HALF * i : HALF * (i + 1)], tab_w[:].indirect(idx1[:, HALF_COLS * i : HALF_COLS * (i + 1)])
-            )
+        halves = [slice(0, HALF), slice(HALF, S)]
+        first_parts = [slice(0, LEAD), slice(LEAD, HALF), slice(HALF, S)]
+        for cols in first_parts:
+            nc.vector.tensor_copy(v_w[:, cols], tab_w[:].indirect(idx1[:, cols.start // 16 : cols.stop // 16]))
 
         h_tiles = {}
-        halves = [slice(0, HALF), slice(HALF, S)]
-        first_parts = [slice(0, HALF // 2), slice(HALF // 2, HALF), slice(HALF, S)]
 
         def first_product(k):
             h = place("h%d" % k, AT_H[k], [P, S], F32)
             for cols in first_parts if k == 0 else halves:
-                bank = psum.tile([P, BANK], F32, name="bank")
+                bank = psum.tile([P, BANK], F32, name="bank", bufs=7)
                 width = cols.stop - cols.start
                 nc.tensor.matmul_mx(
                     out=bank[:, :width],
@@ -236,11 +240,8 @@ def tile_list_print_run_forecast_kernel(
 
         z_bf, z_w, z_s = {}, {}, {}
 
-        def make_z(b, c, held=False):
-            if held:
-                z = place("z_held%d" % b, AT_WGS[0], [P, BANK * PACK], BF16)
-            else:
-                z = ring.tile([P, BANK * PACK], BF16, name="z", bufs=3, align_bytes=64)
+        def make_z(b, c):
+            z = place("z%d%d" % (b, c), AT_Z[b, c], [P, BANK * PACK], BF16)
             nc.vector.tensor_tensor(
                 z[:].rearrange("p (c u e) -> p c u e", u=2, e=2),
                 page_bf[c][:].rearrange("p u c e -> p c u e"),
@@ -299,10 +300,10 @@ def tile_list_print_run_forecast_kernel(
                     at = P * (PASSES * n + b)
                     weights["a", n, b] = (words[:, at - lo : at - lo + P], wa_s[:, at : at + P])
 
-        def second_pass(which, n, c, b, cols=slice(0, BANK)):
+        def second_pass(which, n, c, b, cols=slice(0, BANK), tag="bank"):
             key = which, n, c, cols.start
             if b == 0:
-                banks[key] = psum.tile([P, BANK], F32, name="bank")
+                banks[key] = psum.tile([P, BANK], F32, name=tag, tag=tag, bufs=7 if tag == "bank" else 1)
             words, scales = weights[which, n, b]
             nc.tensor.matmul_mx(
                 out=banks[key][:, : cols.stop - cols.start],
@@ -321,7 +322,7 @@ def tile_list_print_run_forecast_kernel(
                 if which == "b" and n != 1:
                     y[which, n] = place("y_b%d" % n, AT_Y_B, [P, T2], F32)
                 elif which == "b":
-                    y[which, n] = place("y_b1", AT_WA_BF, [P, T2], F32)
+                    y[which, n] = place("y_b1", AT_Y_B1, [P, T2], F32)
                 elif n == OUT_TILES - 1:
                     y[which, n] = place("y_last", AT_Y_LAST, [P, T2], F32)
                 else:
@@ -342,7 +343,7 @@ def tile_list_print_run_forecast_kernel(
             if k == PACK:
                 round_load(1, 0)
                 for c in range(CHUNKS):
-                    make_z(0, c, held=(c == CHUNKS - 1))
+                    make_z(0, c)
             round_page(k)
             if k < PACK - 1:
                 round_load(0, k)
@@ -362,45 +363,50 @@ def tile_list_print_run_forecast_kernel(
         wgo_sb = place("wgo_sb", AT_WGO, [P, M], F32)
         nc.sync.dma_start(wgo_sb[:], wgo)
 
-        late = place("late", AT_WGS[2], [P, PASSES * P + CHUNKS * BANK], U32)
-        quantise_wa(0, 1, late[:, : PASSES * P])
-        for c in range(CHUNKS):
-            quantise_z(0, c, late[:, PASSES * P + BANK * c : PASSES * P + BANK * (c + 1)])
-
+        late = place("late", AT_WGS[2], [P, 2 * BANK], U32)
+        two = place("two", AT_WGS[1], [P, 2 * BANK], U32)
         last = CHUNKS - 1
         last_parts = [slice(0, BANK // 2), slice(BANK // 2, BANK)]
-        for which in "ba":
-            for c in range(last):
-                second_pass(which, 0, c, 0)
-        for cols in last_parts:
-            second_pass("b", 0, last, 0, cols)
-        two = place("two", AT_WGS[1], [P, 2 * BANK], U32)
+
+        def open_chunk(c, words):
+            quantise_z(0, c, words)
+            if c < last:
+                for n in range(2):
+                    second_pass("b", n, c, 0)
+            else:
+                second_pass("b", 0, last, 0, last_parts[0], tag="bank_last")
+                second_pass("b", 0, last, 0, last_parts[1])
 
         def finish_chunk(c):
             quantise_z(1, c, two[:, BANK * c : BANK * (c + 1)] if c < 2 else new_z_words(1, c))
-            for which in "ba":
-                second_pass(which, 0, c, 1)
-                if (which, c) != ("a", last - 1):
-                    empty_bank(which, 0, c)
+            for n in range(2):
+                second_pass("b", n, c, 1)
+                empty_bank("b", n, c)
 
+        for c in range(2):
+            open_chunk(c, late[:, BANK * c : BANK * (c + 1)])
         make_z(1, 0)
         make_z(1, 1)
         finish_chunk(0)
         make_z(1, 2)
         finish_chunk(1)
-        make_z(1, 3, held=True)
+        words02 = place("z_w02", AT_LOAD_BF[-2], [P, BANK], U32)
+        open_chunk(2, words02[:])
         finish_chunk(2)
+        make_z(1, 3)
+        words03 = place("z_w03", AT_LOAD_BF[-1], [P, BANK], U32)
+        open_chunk(3, words03[:])
         last_words = new_z_words(1, last)
         for cols in last_parts:
             quantise_z(1, last, last_words, cols)
             second_pass("b", 0, last, 1, cols)
             empty_bank("b", 0, last, cols)
-        wa_rest = place("wa_rest", AT_WGS[0], [P, 2 * PASSES * P], U32)
-        quantise_wa(1, 2, wa_rest[:])
-        empty_bank("a", 0, last - 1, copy=nc.vector.tensor_copy)
-        for b in range(PASSES):
-            second_pass("a", 0, last, b)
-        empty_bank("a", 0, last)
+        wa_words = place("wa_words", AT_WA_WORDS, [P, OUT_TILES * PASSES * P], U32)
+        quantise_wa(0, 1, wa_words[:, : PASSES * P])
+        quantise_wa(1, 2, wa_words[:, PASSES * P :])
+        second_pass("b", 1, last, 0, tag="bank_last")
+        second_pass("b", 1, last, 1)
+        empty_bank("b", 1, last)
 
         def second_product(which, n):
             for c in range(CHUNKS):
@@ -439,9 +445,9 @@ def tile_list_print_run_forecast_kernel(
                     queue.dma_start(out[P * n : P * (n + 1), cols], placed[:, cols])
 
         pick_damping(0)
-        pick_score(0)
-        second_product("b", 1)
+        second_product("a", 0)
         pick_damping(1)
+        pick_score(0)
         make_damping(0)
         place_out(0)
         second_product("a", 1)

@@ -47,7 +47,7 @@ AT_W4_W = 63 * KIB
 AT_Y_LAST = 64 * KIB
 AT_WINDOW = 68 * KIB
 AT_PAGE_EVEN = 129 * KIB
-AT_W4_S_RAW = AT_PAGE_EVEN
+AT_W4_S_RAW = 72 * KIB
 AT_PAGE_ODD = 76 * KIB
 AT_STAGED = 137 * KIB
 AT_W4_SECOND = 137 * KIB
@@ -113,7 +113,7 @@ def tile_list_print_run_forecast_kernel(
                 tile[LANDING:, :].bitcast(I32),
                 src.bitcast(I32).unsqueeze(1).to_broadcast([SCALE_ROWS, 2, width // 4]),
             )
-            nc.gpsimd.memset(tile[:LANDING, :].bitcast(I32), 0)
+            nc.vector.memset(tile[:LANDING, :].bitcast(I32), 0)
             return tile
 
         warm = keep.tile([P, 1], F32)
@@ -181,7 +181,7 @@ def tile_list_print_run_forecast_kernel(
 
         v_w = place("v_w", AT_V_W, [P, S], U32)
         halves = [slice(0, HALF), slice(HALF, S)]
-        first_parts = [slice(0, LEAD), slice(LEAD, HALF), slice(HALF, S)]
+        first_parts = [slice(0, LEAD), slice(LEAD, S - LEAD), slice(S - LEAD, S)]
         for cols in first_parts:
             nc.vector.tensor_copy(v_w[:, cols], tab_w[:].indirect(idx1[:, cols.start // 16 : cols.stop // 16]))
 

@@ -113,7 +113,7 @@ def tile_list_print_run_forecast_kernel(
                 tile[LANDING:, :].bitcast(I32),
                 src.bitcast(I32).unsqueeze(1).to_broadcast([SCALE_ROWS, 2, width // 4]),
             )
-            nc.vector.memset(tile[:LANDING, :].bitcast(I32), 0)
+            nc.gpsimd.memset(tile[:LANDING, :].bitcast(I32), 0)
             return tile
 
         warm = keep.tile([P, 1], F32)
@@ -125,11 +125,8 @@ def tile_list_print_run_forecast_kernel(
         w4_s_raw = land_scale_rows("w4_s_raw", AT_W4_S_RAW, w4_scales[0], H)
         wgs_rows = wgs.rearrange("(q t) j -> q t j", t=PACK)
         wgs_lead = place("wgs_lead", AT_LEAD, [P, LEAD], F32)
-        for q in range(QUADS // 2):
-            nc.sync.dma_start(wgs_lead[QUAD * q : QUAD * (q + 1), :], wgs_rows[:, 0, :LEAD])
-        nc.scalar.copy(wgs_lead[P // 2 :, :], wgs_lead[: P // 2, :])
+        nc.sync.dma_start(wgs_lead[:QUAD, :], wgs_rows[:, 0, :LEAD])
         idx2 = load_list("idx2", offs2)
-        idx3 = load_list("idx3", offs3)
         tab_w = place("tab_w", AT_TABLE, [P, T], U32)
         nc.sync.dma_start(tab_w[:].bitcast(I32), tab_words[0].rearrange("p t i -> p (t i)").bitcast(I32))
         w4_w = place("w4_w", AT_W4_W, [P, 2 * H], U8)
@@ -145,6 +142,7 @@ def tile_list_print_run_forecast_kernel(
 
         w4_first = keep.tile([P, H], U8)
         load_w4(0, w4_first)
+        idx3 = load_list("idx3", offs3)
         idx4 = load_list("idx4", offs4)
         wgs_of_slot = {}
 
@@ -161,6 +159,9 @@ def tile_list_print_run_forecast_kernel(
         nc.vector.tensor_copy(staged[:, H:].bitcast(I32), picked[:].bitcast(I32))
         for r in range(4):
             nc.sync.dma_start(planes[r:P:QUAD, :].bitcast(I32), staged[LANDING + 2 * r : P : 8, :].bitcast(I32))
+        lead_words = wgs_lead[:].bitcast(I32)
+        nc.vector.tensor_copy(lead_words[QUAD : 2 * QUAD, :], lead_words[:QUAD, :])
+        nc.scalar.copy(wgs_lead[P // 2 :, :], wgs_lead[: P // 2, :])
         page_even = place("page_even", AT_PAGE_EVEN, [P, T2], F32)
         nc.vector.memset(page_even[:], 0.0)
         pages = [page_even]

@@ -45,8 +45,8 @@ AT_W8_FIRST = 52 * KIB
 AT_OUT_ODD = 56 * KIB
 AT_W4_W = 63 * KIB
 AT_Y_LAST = 64 * KIB
-AT_WINDOW = 68 * KIB
 AT_PAGE_EVEN = 129 * KIB
+AT_WINDOW = AT_PAGE_EVEN
 AT_W4_S_RAW = 72 * KIB
 AT_PAGE_ODD = 76 * KIB
 AT_STAGED = 137 * KIB
@@ -107,25 +107,25 @@ def tile_list_print_run_forecast_kernel(
         def row(name):
             return ring.tile([P, S], F32, name=name, tag="row", bufs=ROWS)
 
-        def land_scale_rows(name, offset, src, width):
+        def land_scale_rows(queue, name, offset, src, width):
             tile = place(name, offset, [P, width], U8)
-            nc.sync.dma_start(
+            queue.dma_start(
                 tile[LANDING:, :].bitcast(I32),
                 src.bitcast(I32).unsqueeze(1).to_broadcast([SCALE_ROWS, 2, width // 4]),
             )
-            nc.gpsimd.memset(tile[:LANDING, :].bitcast(I32), 0)
+            nc.vector.memset(tile[:LANDING, :].bitcast(I32), 0)
             return tile
 
         warm = keep.tile([P, 1], F32)
         nc.vector.memset(warm[:], 1.0)
-        nc.scalar.activation(warm[:], warm[:], ACT.Abs_reciprocal_sqrt)
 
         idx1 = load_list("idx1", offs)
-        tab_s = land_scale_rows("tab_s", AT_WINDOW, tab_scales[0], T)
-        w4_s_raw = land_scale_rows("w4_s_raw", AT_W4_S_RAW, w4_scales[0], H)
+        w4_s_raw = land_scale_rows(nc.scalar, "w4_s_raw", AT_W4_S_RAW, w4_scales[0], H)
+        tab_s = land_scale_rows(nc.sync, "tab_s", AT_WINDOW, tab_scales[0], T)
         wgs_rows = wgs.rearrange("(q t) j -> q t j", t=PACK)
         wgs_lead = place("wgs_lead", AT_LEAD, [P, LEAD], F32)
-        nc.sync.dma_start(wgs_lead[:QUAD, :], wgs_rows[:, 0, :LEAD])
+        nc.scalar.dma_start(wgs_lead[:QUAD, :], wgs_rows[:, 0, :LEAD])
+        nc.scalar.activation(warm[:], warm[:], ACT.Abs_reciprocal_sqrt)
         idx2 = load_list("idx2", offs2)
         tab_w = place("tab_w", AT_TABLE, [P, T], U32)
         nc.sync.dma_start(tab_w[:].bitcast(I32), tab_words[0].rearrange("p t i -> p (t i)").bitcast(I32))
@@ -149,13 +149,13 @@ def tile_list_print_run_forecast_kernel(
         planes = place("planes", AT_PLANES, [P, H + S], U8)
         nc.vector.memset(planes[:].bitcast(I32), 0)
         w4_s, v_s = planes[:, :H], planes[:, H:]
-        picked = place("picked", AT_PICKED, [P, S], U8)
-        nc.vector.tensor_copy(picked[:], tab_s[:].indirect(idx1[:]))
         staged = place("staged", AT_STAGED, [P, H + S], U8)
         nc.vector.tensor_copy(
             staged[:, :H].rearrange("p (b t m) -> p b t m", b=PASSES, t=PACK),
             w4_s_raw[:].rearrange("p (b m t) -> p b t m", b=PASSES, t=PACK),
         )
+        picked = place("picked", AT_PICKED, [P, S], U8)
+        nc.vector.tensor_copy(picked[:], tab_s[:].indirect(idx1[:]))
         nc.vector.tensor_copy(staged[:, H:].bitcast(I32), picked[:].bitcast(I32))
         for r in range(4):
             nc.sync.dma_start(planes[r:P:QUAD, :].bitcast(I32), staged[LANDING + 2 * r : P : 8, :].bitcast(I32))

@@ -26,7 +26,6 @@ PASSES = H // (P * PACK)
 CHUNKS = T2 // BANK
 TILES = PASSES * PACK
 OUT_TILES = N // P
-PAGES = 2
 ROWS = 6
 HALVES = 2
 HALF = S // HALVES
@@ -36,26 +35,30 @@ LANDING = P - 2 * SCALE_ROWS
 LEAD = HALF // 2
 
 AT_TABLE = 8 * KIB - 64
-AT_WGS = {0: 31 * KIB, 1: 35 * KIB, 2: 8 * KIB}
-AT_RAW = (138 * KIB, 0, 23 * KIB)
-AT_Y_B = 43 * KIB
+AT_WGS = {0: 162 * KIB, 2: 8 * KIB}
+AT_RAW = (137 * KIB, 0, 23 * KIB)
+AT_Y_B = 42 * KIB + 256
 AT_V_W = 50 * KIB
 AT_W8_LAST = 51 * KIB
 AT_W8_FIRST = 52 * KIB
 AT_OUT_ODD = 56 * KIB
-AT_W4_W = 63 * KIB
+AT_W4_W = (63 * KIB + 512, 190 * KIB - 512)
 AT_Y_LAST = 64 * KIB
-AT_PAGE_EVEN = 129 * KIB
-AT_WINDOW = AT_PAGE_EVEN
+AT_PAGE_EVEN = 170 * KIB
+AT_WINDOW = 68 * KIB
 AT_W4_S_RAW = 72 * KIB
-AT_PAGE_ODD = 76 * KIB
-AT_STAGED = 137 * KIB
-AT_W4_SECOND = 137 * KIB
-AT_PICKED = 35 * KIB - 512
-AT_LEAD = AT_PAGE_ODD
+AT_PAGE_ODD = 129 * KIB
+AT_STAGED = 84 * KIB
+AT_W4_FIRST = 137 * KIB - 512
+AT_W4_SECOND = 84 * KIB
+AT_PICKED = 170 * KIB - 512
+AT_TWO = 35 * KIB
+AT_LEAD = 76 * KIB
+AT_PAGE_THIRD = AT_LEAD
 AT_OUT_EVEN = 84 * KIB
-AT_PLANES = 91 * KIB
-AT_W8_S = 92 * KIB
+AT_PLANES = 181 * KIB
+AT_W8_S = 50 * KIB + 256
+AT_PAGE_BF = [(178 + 4 * c) * KIB for c in range(CHUNKS)]
 AT_WA_BF = 93 * KIB
 AT_SLOTS = [(101 + 4 * i) * KIB for i in range(7)]
 AT_H = AT_SLOTS[:3] + [AT_WA_BF] + AT_SLOTS[3:6] + AT_SLOTS[:1]
@@ -63,7 +66,7 @@ AT_LOAD_BF = AT_H[:3] + AT_SLOTS[6:] + [AT_H[4], AT_H[1], AT_H[5], AT_H[6]]
 AT_Y_B1 = AT_PAGE_EVEN
 AT_Z_SLOTS = [(146 + 4 * i) * KIB for i in range(4)]
 AT_Z = {
-    (0, 0): AT_Z_SLOTS[0], (0, 1): AT_Z_SLOTS[1], (0, 2): AT_Z_SLOTS[2], (0, 3): AT_WGS[0],
+    (0, 0): AT_Z_SLOTS[0], (0, 1): AT_Z_SLOTS[1], (0, 2): AT_Z_SLOTS[2], (0, 3): 31 * KIB,
     (1, 0): AT_Z_SLOTS[3], (1, 1): AT_Z_SLOTS[0], (1, 2): AT_Z_SLOTS[1], (1, 3): AT_Z_SLOTS[2],
 }
 AT_WA_WORDS = AT_Z_SLOTS[2]
@@ -129,18 +132,18 @@ def tile_list_print_run_forecast_kernel(
         idx2 = load_list("idx2", offs2)
         tab_w = place("tab_w", AT_TABLE, [P, T], U32)
         nc.sync.dma_start(tab_w[:].bitcast(I32), tab_words[0].rearrange("p t i -> p (t i)").bitcast(I32))
-        w4_w = place("w4_w", AT_W4_W, [P, 2 * H], U8)
+        w4_w = [place("w4_w%d" % b, AT_W4_W[b], [P, H], U8) for b in range(PASSES)]
 
         def load_w4(b, raw):
             nc.sync.dma_start(raw[:].bitcast(I32), w4_words[0].bitcast(I32)[:, 2 * P * b : 2 * P * (b + 1)])
 
         def deal_w4(b, raw, slots=slice(0, PACK)):
             nc.scalar.copy(
-                w4_w[:, H * b : H * (b + 1)].bitcast(U16).rearrange("p (t m) -> p t m", t=PACK)[:, slots],
+                w4_w[b][:].bitcast(U16).rearrange("p (t m) -> p t m", t=PACK)[:, slots],
                 raw[:].bitcast(U16).rearrange("p (m t) -> p t m", t=PACK)[:, slots],
             )
 
-        w4_first = keep.tile([P, H], U8)
+        w4_first = place("w4_first", AT_W4_FIRST, [P, H], U8)
         load_w4(0, w4_first)
         idx3 = load_list("idx3", offs3)
         idx4 = load_list("idx4", offs4)
@@ -163,19 +166,26 @@ def tile_list_print_run_forecast_kernel(
         nc.vector.tensor_copy(lead_words[QUAD : 2 * QUAD, :], lead_words[:QUAD, :])
         nc.scalar.copy(wgs_lead[P // 2 :, :], wgs_lead[: P // 2, :])
         page_even = place("page_even", AT_PAGE_EVEN, [P, T2], F32)
-        nc.vector.memset(page_even[:], 0.0)
-        pages = [page_even]
+        nc.gpsimd.memset(page_even[:], 0.0)
 
         deal_w4(0, w4_first, slice(0, 1))
         deal_w4(0, w4_first, slice(1, PACK))
+        page_odd = place("page_odd", AT_PAGE_ODD, [P, T2], F32)
+        nc.gpsimd.memset(page_odd[:], 0.0)
+        pages = {k: (page_even, page_odd)[k % 2] for k in range(TILES)}
+
+        wgs_pair = {first: place("wgs%d" % first, AT_WGS[first], [P, 2 * S], F32) for first in AT_WGS}
 
         def load_wgs(first, count):
-            part = place("wgs%d" % first, AT_WGS[first], [P, count, S], F32)
+            part = wgs_pair[first - first % 2][:, S * (first % 2) : S * (first % 2 + count)]
             for q in (0, 2, 1, 3):
-                nc.sync.dma_start(part[QUAD * q : QUAD * (q + 1), :, :], wgs_rows[:, first : first + count, :])
+                nc.sync.dma_start(
+                    part[QUAD * q : QUAD * (q + 1), :], wgs_rows[:, first : first + count, :].rearrange("q t j -> q (t j)")
+                )
             for i in range(count):
-                wgs_of_slot[first + i] = part[:, i, :]
+                wgs_of_slot[first + i] = part[:, S * i : S * (i + 1)]
 
+        load_wgs(1, 1)
         load_wgs(0, 1)
         w4_second = place("w4_second", AT_W4_SECOND, [P, H], U8)
         load_w4(1, w4_second)
@@ -188,14 +198,16 @@ def tile_list_print_run_forecast_kernel(
 
         h_tiles = {}
 
-        def first_product(k):
-            h = place("h%d" % k, AT_H[k], [P, S], F32)
-            for cols in first_parts if k == 0 else halves:
+        def first_product(k, parts=halves):
+            if parts[0].start == 0:
+                h_tiles[k] = place("h%d" % k, AT_H[k], [P, S], F32)
+            h = h_tiles[k]
+            for cols in parts:
                 bank = psum.tile([P, BANK], F32, name="bank", bufs=7)
                 width = cols.stop - cols.start
                 nc.tensor.matmul_mx(
                     out=bank[:, :width],
-                    lhsT=w4_w[:, 2 * P * k : 2 * P * (k + 1)].bitcast(FP4X4),
+                    lhsT=w4_w[k // PACK][:, 2 * P * (k % PACK) : 2 * P * (k % PACK + 1)].bitcast(FP4X4),
                     lhsT_scale=w4_s[:, P * k : P * (k + 1)],
                     rhs=v_w[:, cols].bitcast(FP8X4),
                     rhs_scale=v_s[:, cols],
@@ -203,7 +215,6 @@ def tile_list_print_run_forecast_kernel(
                     stop=True,
                 )
                 nc.scalar.copy(h[:, cols], bank[:, :width])
-            h_tiles[k] = h
 
         load_bf = {}
 
@@ -222,22 +233,18 @@ def tile_list_print_run_forecast_kernel(
             load_bf[b, c] = rounded
 
         def place_h(k):
-            page, h, w = pages[k % PAGES], h_tiles[k], wgs_of_slot[k % PACK]
+            page, h, w = pages[k], h_tiles[k], wgs_of_slot[k % PACK]
             if k == 0:
-                nc.vector.tensor_tensor(page[:].indirect(idx2[:, : LEAD // 16]), h[:, :LEAD], wgs_lead[:], MULT)
-                page_odd = place("page_odd", AT_PAGE_ODD, [P, T2], F32)
-                nc.gpsimd.memset(page_odd[:], 0.0)
-                pages.append(page_odd)
                 nc.vector.tensor_tensor(page[:].indirect(idx2[:, LEAD // 16 :]), h[:, LEAD:], w[:, LEAD:], MULT)
             else:
                 nc.vector.tensor_tensor(page[:].indirect(idx2[:]), h[:], w, MULT)
 
-        page_bf = [keep.tile([P, 2, BANK, 2], BF16, name="page_bf", tag="page_bf%d" % c, align_bytes=64) for c in range(CHUNKS)]
+        page_bf = [place("page_bf%d" % c, AT_PAGE_BF[c], [P, 2, BANK, 2], BF16) for c in range(CHUNKS)]
 
         def round_page(k):
             t = k % PACK
             for c in range(CHUNKS):
-                nc.scalar.copy(page_bf[c][:, t // 2, :, t % 2], pages[k % PAGES][:, BANK * c : BANK * (c + 1)])
+                nc.scalar.copy(page_bf[c][:, t // 2, :, t % 2], pages[k][:, BANK * c : BANK * (c + 1)])
 
         z_bf, z_w, z_s = {}, {}, {}
 
@@ -333,12 +340,20 @@ def tile_list_print_run_forecast_kernel(
                 banks[which, n, c, cols.start][:, : cols.stop - cols.start],
             )
 
-        for k in range(AHEAD):
+        first_product(0, first_parts[:1])
+        first_product(1, first_parts)
+        first_product(0, first_parts[1:])
+        for k in range(2, AHEAD):
             if k == PACK:
                 deal_w4(1, w4_second)
             first_product(k)
-        for k in range(TILES):
-            if k in (1, 2):
+        nc.vector.tensor_tensor(page_even[:].indirect(idx2[:, : LEAD // 16]), h_tiles[0][:, :LEAD], wgs_lead[:], MULT)
+        page_third = place("page_third", AT_PAGE_THIRD, [P, T2], F32)
+        nc.gpsimd.memset(page_third[:], 0.0)
+        for k in range(2, TILES, 2):
+            pages[k] = page_third
+        for k in (1, 0) + tuple(range(2, TILES)):
+            if k == 2:
                 load_wgs(k, k)
             place_h(k)
             if k == PACK:
@@ -365,7 +380,7 @@ def tile_list_print_run_forecast_kernel(
         nc.sync.dma_start(wgo_sb[:], wgo)
 
         late = place("late", AT_WGS[2], [P, 2 * BANK], U32)
-        two = place("two", AT_WGS[1], [P, 2 * BANK], U32)
+        two = place("two", AT_TWO, [P, 2 * BANK], U32)
         last = CHUNKS - 1
         last_parts = [slice(0, BANK // 2), slice(BANK // 2, BANK)]
 

@@ -464,15 +464,15 @@ def tile_list_print_run_forecast_kernel(
         second_product("a", 0)
         pick_damping(1)
         pick_score(0)
+        second_product("b", 2)
+        pick_damping(2)
         make_damping(0)
         place_out(0)
         second_product("a", 1)
-        second_product("b", 2)
-        make_damping(1)
         second_product("a", 2)
+        make_damping(1)
         pick_score(1)
-        pick_damping(2)
-        make_damping(2)
         pick_score(2)
+        make_damping(2)
         place_out(1)
         place_out(2)

@@ -70,6 +70,7 @@ AT_Z = {
     (1, 0): AT_Z_SLOTS[3], (1, 1): AT_Z_SLOTS[0], (1, 2): AT_Z_SLOTS[1], (1, 3): AT_Z_SLOTS[2],
 }
 AT_WA_WORDS = AT_Z_SLOTS[2]
+AT_LATE = AT_RAW[0]
 AT_WGO = AT_SLOTS[6]
 AT_RAW_SPARE = {(0, CHUNKS - 1): AT_Y_B, (1, 0): AT_Y_LAST}
 AHEAD = TILES - 1
@@ -153,15 +154,21 @@ def tile_list_print_run_forecast_kernel(
         nc.vector.memset(planes[:].bitcast(I32), 0)
         w4_s, v_s = planes[:, :H], planes[:, H:]
         staged = place("staged", AT_STAGED, [P, H + S], U8)
-        nc.vector.tensor_copy(
-            staged[:, :H].rearrange("p (b t m) -> p b t m", b=PASSES, t=PACK),
-            w4_s_raw[:].rearrange("p (b m t) -> p b t m", b=PASSES, t=PACK),
-        )
+
+        def deal_scales(b):
+            nc.vector.tensor_copy(
+                staged[:, :H].rearrange("p (b t m) -> p b t m", b=PASSES, t=PACK)[:, b],
+                w4_s_raw[:].rearrange("p (b m t) -> p b t m", b=PASSES, t=PACK)[:, b],
+            )
+
+        deal_scales(0)
         picked = place("picked", AT_PICKED, [P, S], U8)
         nc.vector.tensor_copy(picked[:], tab_s[:].indirect(idx1[:]))
+        deal_scales(1)
         nc.vector.tensor_copy(staged[:, H:].bitcast(I32), picked[:].bitcast(I32))
         for r in range(4):
-            nc.sync.dma_start(planes[r:P:QUAD, :].bitcast(I32), staged[LANDING + 2 * r : P : 8, :].bitcast(I32))
+            queue = nc.scalar if r % 2 == 0 else nc.sync
+            queue.dma_start(planes[r:P:QUAD, :].bitcast(I32), staged[LANDING + 2 * r : P : 8, :].bitcast(I32))
         lead_words = wgs_lead[:].bitcast(I32)
         nc.vector.tensor_copy(lead_words[QUAD : 2 * QUAD, :], lead_words[:QUAD, :])
         nc.scalar.copy(wgs_lead[P // 2 :, :], wgs_lead[: P // 2, :])
@@ -333,6 +340,8 @@ def tile_list_print_run_forecast_kernel(
                     y[which, n] = place("y_b1", AT_Y_B1, [P, T2], F32)
                 elif n == OUT_TILES - 1:
                     y[which, n] = place("y_last", AT_Y_LAST, [P, T2], F32)
+                elif n == 1:
+                    y[which, n] = place("y_a1", AT_PAGE_THIRD, [P, T2], F32)
                 else:
                     y[which, n] = raw_rows()
             copy(
@@ -379,10 +388,10 @@ def tile_list_print_run_forecast_kernel(
         wgo_sb = place("wgo_sb", AT_WGO, [P, M], F32)
         nc.sync.dma_start(wgo_sb[:], wgo)
 
-        late = place("late", AT_WGS[2], [P, 2 * BANK], U32)
+        late = place("late", AT_LATE, [P, (CHUNKS - 1) * BANK], U32)
         two = place("two", AT_TWO, [P, 2 * BANK], U32)
         last = CHUNKS - 1
-        last_parts = [slice(0, BANK // 2), slice(BANK // 2, BANK)]
+        last_parts = [slice(0, 2 * P), slice(2 * P, 3 * P), slice(3 * P, BANK)]
 
         def open_chunk(c, words):
             quantise_z(0, c, words)
@@ -391,7 +400,8 @@ def tile_list_print_run_forecast_kernel(
                     second_pass("b", n, c, 0)
             else:
                 second_pass("b", 0, last, 0, last_parts[0], tag="bank_last")
-                second_pass("b", 0, last, 0, last_parts[1])
+                for cols in last_parts[1:]:
+                    second_pass("b", 0, last, 0, cols)
 
         def finish_chunk(c):
             quantise_z(1, c, two[:, BANK * c : BANK * (c + 1)] if c < 2 else new_z_words(1, c))
@@ -399,15 +409,13 @@ def tile_list_print_run_forecast_kernel(
                 second_pass("b", n, c, 1)
                 empty_bank("b", n, c)
 
-        for c in range(2):
+        for c in range(last):
             open_chunk(c, late[:, BANK * c : BANK * (c + 1)])
         make_z(1, 0)
         make_z(1, 1)
         finish_chunk(0)
         make_z(1, 2)
         finish_chunk(1)
-        words02 = place("z_w02", AT_LOAD_BF[-2], [P, BANK], U32)
-        open_chunk(2, words02[:])
         finish_chunk(2)
         make_z(1, 3)
         words03 = place("z_w03", AT_LOAD_BF[-1], [P, BANK], U32)

@@ -19,61 +19,63 @@ MAX = mybir.AluOpType.max
 
 P = 128
 PACK = 4
-QUADS = 4
 QUAD = 32
 BANK = 512
+STRIPE = 16
 PASSES = H // (P * PACK)
 CHUNKS = T2 // BANK
 TILES = PASSES * PACK
 OUT_TILES = N // P
-ROWS = 6
-HALVES = 2
-HALF = S // HALVES
-KIB = 1024
+HALF = S // 2
 SCALE_ROWS = 16
+ROWS_PER_QUAD = 4
 LANDING = P - 2 * SCALE_ROWS
-LEAD = HALF // 2
+LEAD = S // 4
+RING_BANKS = 7
+PICKED_ROWS = 2 * OUT_TILES
+KIB = 1024
 
 AT_TABLE = 8 * KIB - 64
-AT_WGS = {0: 162 * KIB, 2: 8 * KIB}
 AT_RAW = (137 * KIB, 0, 23 * KIB)
-AT_Y_B = 42 * KIB + 256
-AT_V_W = 50 * KIB
-AT_W8_LAST = 51 * KIB
-AT_W8_FIRST = 52 * KIB
-AT_OUT_ODD = 56 * KIB
-AT_W4_W = (63 * KIB + 512, 190 * KIB - 512)
-AT_Y_LAST = 64 * KIB
-AT_PAGE_EVEN = 170 * KIB
+AT_WGS = {0: 162 * KIB, 2: 8 * KIB}
+AT_PAGE_FIRST = 170 * KIB
+AT_PICKED = AT_PAGE_FIRST - 512
+AT_PAGE_ODD = 129 * KIB
+AT_W4_RAW = (AT_RAW[0] - 512, 84 * KIB)
+AT_STAGED = AT_W4_RAW[1]
+AT_OUT = (AT_STAGED, 56 * KIB)
+AT_PAGE_EVEN = 76 * KIB
+AT_LEAD = AT_PAGE_EVEN
 AT_WINDOW = 68 * KIB
 AT_W4_S_RAW = 72 * KIB
-AT_PAGE_ODD = 129 * KIB
-AT_STAGED = 84 * KIB
-AT_W4_FIRST = 137 * KIB - 512
-AT_W4_SECOND = 84 * KIB
-AT_PICKED = 170 * KIB - 512
-AT_TWO = 35 * KIB
-AT_LEAD = 76 * KIB
-AT_PAGE_THIRD = AT_LEAD
-AT_OUT_EVEN = 84 * KIB
-AT_PLANES = 181 * KIB
-AT_W8_S = 50 * KIB + 256
+AT_V_W = 50 * KIB
+AT_W8_S = AT_V_W + 256
+AT_W8_LAST = 51 * KIB
+AT_W8_FIRST = 52 * KIB
 AT_PAGE_BF = [(178 + 4 * c) * KIB for c in range(CHUNKS)]
+AT_PLANES = AT_PAGE_BF[1] - KIB
+AT_W4_W = (64 * KIB - 512, AT_PAGE_BF[3] - 512)
 AT_WA_BF = 93 * KIB
 AT_SLOTS = [(101 + 4 * i) * KIB for i in range(7)]
 AT_H = AT_SLOTS[:3] + [AT_WA_BF] + AT_SLOTS[3:6] + AT_SLOTS[:1]
 AT_LOAD_BF = AT_H[:3] + AT_SLOTS[6:] + [AT_H[4], AT_H[1], AT_H[5], AT_H[6]]
-AT_Y_B1 = AT_PAGE_EVEN
-AT_Z_SLOTS = [(146 + 4 * i) * KIB for i in range(4)]
-AT_Z = {
-    (0, 0): AT_Z_SLOTS[0], (0, 1): AT_Z_SLOTS[1], (0, 2): AT_Z_SLOTS[2], (0, 3): 31 * KIB,
-    (1, 0): AT_Z_SLOTS[3], (1, 1): AT_Z_SLOTS[0], (1, 2): AT_Z_SLOTS[1], (1, 3): AT_Z_SLOTS[2],
+AT_Y = {
+    ("b", 0): AT_V_W - 8 * KIB + 256,
+    ("b", 1): AT_PAGE_FIRST,
+    ("b", 2): AT_V_W - 8 * KIB + 256,
+    ("a", 0): AT_RAW[2],
+    ("a", 1): AT_PAGE_EVEN,
+    ("a", 2): 64 * KIB,
 }
-AT_WA_WORDS = AT_Z_SLOTS[2]
-AT_LATE = AT_RAW[0]
+AT_RAW_SPARE = {(0, CHUNKS - 1): AT_Y["b", 0], (1, 0): AT_Y["a", 2]}
+AT_Z_SLOTS = [(146 + 4 * i) * KIB for i in range(CHUNKS)]
+AT_Z = AT_Z_SLOTS[:3] + [31 * KIB] + AT_Z_SLOTS[3:] + AT_Z_SLOTS[:3]
+AT_Z_W_EARLY = AT_RAW[0]
+AT_Z_W_LATE = AT_LOAD_BF[-2]
+AT_Z_W_PAIR = 35 * KIB
+AT_WA_W = AT_Z[-1]
 AT_WGO = AT_SLOTS[6]
-AT_RAW_SPARE = {(0, CHUNKS - 1): AT_Y_B, (1, 0): AT_Y_LAST}
-AHEAD = TILES - 1
+AT_DAMP_FIRST = AT_W8_FIRST
 
 
 def tile_list_print_run_forecast_kernel(
@@ -92,15 +94,18 @@ def tile_list_print_run_forecast_kernel(
             return placed.tile(shape, dtype, name=name, tag=name, offset=offset, align_bytes=64)
 
         def load_list(name, src):
-            tile = lists.tile([P, S // 16], U16, name=name)
+            tile = lists.tile([P, S // STRIPE], U16, name=name)
             nc.sync.dma_start(tile[:], src)
             return tile
 
-        def load_scale_rows(queue, tile, src, clear):
-            clear.memset(tile[:].bitcast(I32), 0)
-            rows = src.rearrange("a (q r) c -> r q a c", r=4)
-            for r in range(4):
-                queue.dma_start(tile[r:P:QUAD, :, :].bitcast(I32), rows[r].bitcast(I32))
+        def entries(list_tile, cols):
+            return list_tile[:, cols.start // STRIPE : cols.stop // STRIPE]
+
+        def ring_bank():
+            return psum.tile([P, BANK], F32, name="bank", tag="bank", bufs=RING_BANKS)
+
+        def last_bank():
+            return psum.tile([P, BANK], F32, name="bank_last", tag="bank_last", bufs=1)
 
         raw_uses = []
 
@@ -108,8 +113,8 @@ def tile_list_print_run_forecast_kernel(
             raw_uses.append(len(raw_uses))
             return place("raw%d" % raw_uses[-1], AT_RAW[raw_uses[-1] % len(AT_RAW)], [P, T2], F32)
 
-        def row(name):
-            return ring.tile([P, S], F32, name=name, tag="row", bufs=ROWS)
+        def picked_row(name):
+            return ring.tile([P, S], F32, name=name, tag="row", bufs=PICKED_ROWS)
 
         def land_scale_rows(queue, name, offset, src, width):
             tile = place(name, offset, [P, width], U8)
@@ -135,20 +140,20 @@ def tile_list_print_run_forecast_kernel(
         nc.sync.dma_start(tab_w[:].bitcast(I32), tab_words[0].rearrange("p t i -> p (t i)").bitcast(I32))
         w4_w = [place("w4_w%d" % b, AT_W4_W[b], [P, H], U8) for b in range(PASSES)]
 
-        def load_w4(b, raw):
+        def load_w4(b):
+            raw = place("w4_raw%d" % b, AT_W4_RAW[b], [P, H], U8)
             nc.sync.dma_start(raw[:].bitcast(I32), w4_words[0].bitcast(I32)[:, 2 * P * b : 2 * P * (b + 1)])
+            return raw
 
-        def deal_w4(b, raw, slots=slice(0, PACK)):
+        def deal_w4(b, raw, slots):
             nc.scalar.copy(
                 w4_w[b][:].bitcast(U16).rearrange("p (t m) -> p t m", t=PACK)[:, slots],
                 raw[:].bitcast(U16).rearrange("p (m t) -> p t m", t=PACK)[:, slots],
             )
 
-        w4_first = place("w4_first", AT_W4_FIRST, [P, H], U8)
-        load_w4(0, w4_first)
+        w4_first = load_w4(0)
         idx3 = load_list("idx3", offs3)
         idx4 = load_list("idx4", offs4)
-        wgs_of_slot = {}
 
         planes = place("planes", AT_PLANES, [P, H + S], U8)
         nc.vector.memset(planes[:].bitcast(I32), 0)
@@ -162,26 +167,30 @@ def tile_list_print_run_forecast_kernel(
             )
 
         deal_scales(0)
-        picked = place("picked", AT_PICKED, [P, S], U8)
-        nc.vector.tensor_copy(picked[:], tab_s[:].indirect(idx1[:]))
+        picked_s = place("picked_s", AT_PICKED, [P, S], U8)
+        nc.vector.tensor_copy(picked_s[:], tab_s[:].indirect(idx1[:]))
         deal_scales(1)
-        nc.vector.tensor_copy(staged[:, H:].bitcast(I32), picked[:].bitcast(I32))
-        for r in range(4):
+        nc.vector.tensor_copy(staged[:, H:].bitcast(I32), picked_s[:].bitcast(I32))
+        for r in range(ROWS_PER_QUAD):
             queue = nc.scalar if r % 2 == 0 else nc.sync
-            queue.dma_start(planes[r:P:QUAD, :].bitcast(I32), staged[LANDING + 2 * r : P : 8, :].bitcast(I32))
+            rows = staged[LANDING + 2 * r : P : 2 * ROWS_PER_QUAD, :]
+            queue.dma_start(planes[r:P:QUAD, :].bitcast(I32), rows.bitcast(I32))
         lead_words = wgs_lead[:].bitcast(I32)
         nc.vector.tensor_copy(lead_words[QUAD : 2 * QUAD, :], lead_words[:QUAD, :])
         nc.scalar.copy(wgs_lead[P // 2 :, :], wgs_lead[: P // 2, :])
-        page_even = place("page_even", AT_PAGE_EVEN, [P, T2], F32)
-        nc.gpsimd.memset(page_even[:], 0.0)
 
+        page_first = place("page_first", AT_PAGE_FIRST, [P, T2], F32)
+        nc.gpsimd.memset(page_first[:], 0.0)
         deal_w4(0, w4_first, slice(0, 1))
         deal_w4(0, w4_first, slice(1, PACK))
         page_odd = place("page_odd", AT_PAGE_ODD, [P, T2], F32)
         nc.gpsimd.memset(page_odd[:], 0.0)
-        pages = {k: (page_even, page_odd)[k % 2] for k in range(TILES)}
+        pages = {0: page_first}
+        for k in range(1, TILES, 2):
+            pages[k] = page_odd
 
         wgs_pair = {first: place("wgs%d" % first, AT_WGS[first], [P, 2 * S], F32) for first in AT_WGS}
+        wgs_of_slot = {}
 
         def load_wgs(first, count):
             part = wgs_pair[first - first % 2][:, S * (first % 2) : S * (first % 2 + count)]
@@ -194,42 +203,44 @@ def tile_list_print_run_forecast_kernel(
 
         load_wgs(1, 1)
         load_wgs(0, 1)
-        w4_second = place("w4_second", AT_W4_SECOND, [P, H], U8)
-        load_w4(1, w4_second)
+        w4_second = load_w4(1)
 
         v_w = place("v_w", AT_V_W, [P, S], U32)
+        whole = slice(0, S)
         halves = [slice(0, HALF), slice(HALF, S)]
-        first_parts = [slice(0, LEAD), slice(LEAD, S - LEAD), slice(S - LEAD, S)]
-        for cols in first_parts:
-            nc.vector.tensor_copy(v_w[:, cols], tab_w[:].indirect(idx1[:, cols.start // 16 : cols.stop // 16]))
+        pieces = [slice(0, LEAD), slice(LEAD, S - LEAD), slice(S - LEAD, S)]
+        for cols in pieces:
+            nc.vector.tensor_copy(v_w[:, cols], tab_w[:].indirect(entries(idx1, cols)))
 
         h_tiles = {}
 
-        def first_product(k, parts=halves):
+        def first_product(k, parts):
             if parts[0].start == 0:
                 h_tiles[k] = place("h%d" % k, AT_H[k], [P, S], F32)
-            h = h_tiles[k]
+            b, t = divmod(k, PACK)
             for cols in parts:
-                bank = psum.tile([P, BANK], F32, name="bank", bufs=7)
+                bank = ring_bank()
                 width = cols.stop - cols.start
                 nc.tensor.matmul_mx(
                     out=bank[:, :width],
-                    lhsT=w4_w[k // PACK][:, 2 * P * (k % PACK) : 2 * P * (k % PACK + 1)].bitcast(FP4X4),
+                    lhsT=w4_w[b][:, 2 * P * t : 2 * P * (t + 1)].bitcast(FP4X4),
                     lhsT_scale=w4_s[:, P * k : P * (k + 1)],
                     rhs=v_w[:, cols].bitcast(FP8X4),
                     rhs_scale=v_s[:, cols],
                     start=True,
                     stop=True,
                 )
-                nc.scalar.copy(h[:, cols], bank[:, :width])
+                nc.scalar.copy(h_tiles[k][:, cols], bank[:, :width])
+
+        def place_h(k, cols, weights_of_cols):
+            nc.vector.tensor_tensor(pages[k][:].indirect(entries(idx2, cols)), h_tiles[k][:, cols], weights_of_cols, MULT)
 
         load_bf = {}
 
         def round_load(b, c):
             raw = place("spare%d" % b, AT_RAW_SPARE[b, c], [P, T2], F32) if (b, c) in AT_RAW_SPARE else raw_rows()
-            raw3 = raw[:].rearrange("p (t c) -> p t c", t=PACK)
             nc.sync.dma_start(
-                raw3,
+                raw[:].rearrange("p (t c) -> p t c", t=PACK),
                 load[P * PACK * b : P * PACK * (b + 1), BANK * c : BANK * (c + 1)].rearrange("(p t) c -> p t c", t=PACK),
             )
             rounded = place("load_bf%d%d" % (b, c), AT_LOAD_BF[CHUNKS * b + c], [P, BANK * PACK], BF16)
@@ -239,24 +250,17 @@ def tile_list_print_run_forecast_kernel(
             )
             load_bf[b, c] = rounded
 
-        def place_h(k):
-            page, h, w = pages[k], h_tiles[k], wgs_of_slot[k % PACK]
-            if k == 0:
-                nc.vector.tensor_tensor(page[:].indirect(idx2[:, LEAD // 16 :]), h[:, LEAD:], w[:, LEAD:], MULT)
-            else:
-                nc.vector.tensor_tensor(page[:].indirect(idx2[:]), h[:], w, MULT)
-
         page_bf = [place("page_bf%d" % c, AT_PAGE_BF[c], [P, 2, BANK, 2], BF16) for c in range(CHUNKS)]
 
         def round_page(k):
-            t = k % PACK
+            u, e = divmod(k % PACK, 2)
             for c in range(CHUNKS):
-                nc.scalar.copy(page_bf[c][:, t // 2, :, t % 2], pages[k][:, BANK * c : BANK * (c + 1)])
+                nc.scalar.copy(page_bf[c][:, u, :, e], pages[k][:, BANK * c : BANK * (c + 1)])
 
         z_bf, z_w, z_s = {}, {}, {}
 
         def make_z(b, c):
-            z = place("z%d%d" % (b, c), AT_Z[b, c], [P, BANK * PACK], BF16)
+            z = place("z%d%d" % (b, c), AT_Z[CHUNKS * b + c], [P, BANK * PACK], BF16)
             nc.vector.tensor_tensor(
                 z[:].rearrange("p (c u e) -> p c u e", u=2, e=2),
                 page_bf[c][:].rearrange("p u c e -> p c u e"),
@@ -265,7 +269,9 @@ def tile_list_print_run_forecast_kernel(
             )
             z_bf[b, c] = z
 
-        def quantise_z(b, c, words, cols=slice(0, BANK)):
+        chunk = slice(0, BANK)
+
+        def quantise_z(b, c, words, cols):
             if cols.start == 0:
                 z_w[b, c] = words
                 z_s[b, c] = keep.tile([P, BANK], U8, name="z_s%d%d" % (b, c), align_bytes=64)
@@ -298,14 +304,16 @@ def tile_list_print_run_forecast_kernel(
             words = w8_words.rearrange("a p c i -> p a (c i)").bitcast(I32)
             nc.sync.dma_start(w8_first[:].bitcast(I32), words[:, :, : 2 * P])
             nc.sync.dma_start(w8_last[:].bitcast(I32), words[:, :, 2 * P :])
-            load_scale_rows(nc.sync, w8_s, w8_scales, nc.gpsimd)
+            nc.gpsimd.memset(w8_s[:].bitcast(I32), 0)
+            rows = w8_scales.rearrange("a (q r) c -> r q a c", r=ROWS_PER_QUAD)
+            for r in range(ROWS_PER_QUAD):
+                nc.sync.dma_start(w8_s[r:P:QUAD, :, :].bitcast(I32), rows[r].bitcast(I32))
 
         weights = {}
         for n in range(OUT_TILES):
             for b in range(PASSES):
                 cols = slice(P * n, P * (n + 1))
-                weights["b", n, b] = (w8_first[:, b, cols] if n < 2 else w8_last[:, b, :], w8_s[:, b, cols])
-        banks = {}
+                weights["b", n, b] = (w8_first[:, b, cols] if n < OUT_TILES - 1 else w8_last[:, b, :], w8_s[:, b, cols])
 
         def quantise_wa(first, count, words):
             lo, hi = PASSES * P * first, PASSES * P * (first + count)
@@ -315,10 +323,12 @@ def tile_list_print_run_forecast_kernel(
                     at = P * (PASSES * n + b)
                     weights["a", n, b] = (words[:, at - lo : at - lo + P], wa_s[:, at : at + P])
 
-        def second_pass(which, n, c, b, cols=slice(0, BANK), tag="bank"):
+        banks, y = {}, {}
+
+        def second_pass(which, n, c, b, cols, new_bank=ring_bank):
             key = which, n, c, cols.start
             if b == 0:
-                banks[key] = psum.tile([P, BANK], F32, name=tag, tag=tag, bufs=7 if tag == "bank" else 1)
+                banks[key] = new_bank()
             words, scales = weights[which, n, b]
             nc.tensor.matmul_mx(
                 out=banks[key][:, : cols.stop - cols.start],
@@ -330,41 +340,31 @@ def tile_list_print_run_forecast_kernel(
                 stop=(b == PASSES - 1),
             )
 
-        y = {}
-
-        def empty_bank(which, n, c, cols=slice(0, BANK), copy=nc.scalar.copy):
+        def empty_bank(which, n, c, cols):
             if c == 0:
-                if which == "b" and n != 1:
-                    y[which, n] = place("y_b%d" % n, AT_Y_B, [P, T2], F32)
-                elif which == "b":
-                    y[which, n] = place("y_b1", AT_Y_B1, [P, T2], F32)
-                elif n == OUT_TILES - 1:
-                    y[which, n] = place("y_last", AT_Y_LAST, [P, T2], F32)
-                elif n == 1:
-                    y[which, n] = place("y_a1", AT_PAGE_THIRD, [P, T2], F32)
-                else:
-                    y[which, n] = raw_rows()
-            copy(
+                y[which, n] = place("y_%s%d" % (which, n), AT_Y[which, n], [P, T2], F32)
+            nc.scalar.copy(
                 y[which, n][:, BANK * c + cols.start : BANK * c + cols.stop],
                 banks[which, n, c, cols.start][:, : cols.stop - cols.start],
             )
 
-        first_product(0, first_parts[:1])
-        first_product(1, first_parts)
-        first_product(0, first_parts[1:])
-        for k in range(2, AHEAD):
+        first_product(0, pieces[:1])
+        first_product(1, pieces)
+        first_product(0, pieces[1:])
+        for k in range(2, TILES - 1):
             if k == PACK:
-                deal_w4(1, w4_second)
-            first_product(k)
-        nc.vector.tensor_tensor(page_even[:].indirect(idx2[:, : LEAD // 16]), h_tiles[0][:, :LEAD], wgs_lead[:], MULT)
-        page_third = place("page_third", AT_PAGE_THIRD, [P, T2], F32)
-        nc.gpsimd.memset(page_third[:], 0.0)
+                deal_w4(1, w4_second, slice(0, PACK))
+            first_product(k, halves)
+        place_h(0, pieces[0], wgs_lead[:])
+        page_even = place("page_even", AT_PAGE_EVEN, [P, T2], F32)
+        nc.gpsimd.memset(page_even[:], 0.0)
         for k in range(2, TILES, 2):
-            pages[k] = page_third
+            pages[k] = page_even
         for k in (1, 0) + tuple(range(2, TILES)):
             if k == 2:
-                load_wgs(k, k)
-            place_h(k)
+                load_wgs(2, 2)
+            cols = slice(LEAD, S) if k == 0 else whole
+            place_h(k, cols, wgs_of_slot[k % PACK][:, cols])
             if k == PACK:
                 round_load(1, 0)
                 for c in range(CHUNKS):
@@ -373,81 +373,77 @@ def tile_list_print_run_forecast_kernel(
             if k < PACK - 1:
                 round_load(0, k)
             if k == PACK - 2:
-                round_load(0, k + 1)
+                round_load(0, CHUNKS - 1)
             if k == PACK - 1:
                 prepare_second_weights()
             if k == PACK:
-                first_product(AHEAD)
+                first_product(TILES - 1, halves)
             if PACK <= k < TILES - 1:
                 round_load(1, k + 1 - PACK)
-        out_odd = place("out_odd", AT_OUT_ODD, [P, T2], F32)
-        out_even = place("out_even", AT_OUT_EVEN, [P, T2], F32)
+        out_odd = place("out_odd", AT_OUT[1], [P, T2], F32)
+        out_even = place("out_even", AT_OUT[0], [P, T2], F32)
         outs = [out_even, out_odd]
         for tile in outs:
             nc.gpsimd.memset(tile[:], 0.0)
         wgo_sb = place("wgo_sb", AT_WGO, [P, M], F32)
         nc.sync.dma_start(wgo_sb[:], wgo)
 
-        late = place("late", AT_LATE, [P, (CHUNKS - 1) * BANK], U32)
-        two = place("two", AT_TWO, [P, 2 * BANK], U32)
+        z_w_early = place("z_w_early", AT_Z_W_EARLY, [P, (CHUNKS - 1) * BANK], U32)
+        z_w_pair = place("z_w_pair", AT_Z_W_PAIR, [P, 2 * BANK], U32)
         last = CHUNKS - 1
         last_parts = [slice(0, 2 * P), slice(2 * P, 3 * P), slice(3 * P, BANK)]
 
-        def open_chunk(c, words):
-            quantise_z(0, c, words)
-            if c < last:
-                for n in range(2):
-                    second_pass("b", n, c, 0)
-            else:
-                second_pass("b", 0, last, 0, last_parts[0], tag="bank_last")
-                for cols in last_parts[1:]:
-                    second_pass("b", 0, last, 0, cols)
+        def open_chunk(c):
+            quantise_z(0, c, z_w_early[:, BANK * c : BANK * (c + 1)], chunk)
+            for n in range(2):
+                second_pass("b", n, c, 0, chunk)
 
         def finish_chunk(c):
-            quantise_z(1, c, two[:, BANK * c : BANK * (c + 1)] if c < 2 else new_z_words(1, c))
+            quantise_z(1, c, z_w_pair[:, BANK * c : BANK * (c + 1)] if c < 2 else new_z_words(1, c), chunk)
             for n in range(2):
-                second_pass("b", n, c, 1)
-                empty_bank("b", n, c)
+                second_pass("b", n, c, 1, chunk)
+                empty_bank("b", n, c, chunk)
 
         for c in range(last):
-            open_chunk(c, late[:, BANK * c : BANK * (c + 1)])
+            open_chunk(c)
         make_z(1, 0)
         make_z(1, 1)
         finish_chunk(0)
         make_z(1, 2)
         finish_chunk(1)
         finish_chunk(2)
-        make_z(1, 3)
-        words03 = place("z_w03", AT_LOAD_BF[-1], [P, BANK], U32)
-        open_chunk(3, words03[:])
+        make_z(1, last)
+        z_w_late = place("z_w_late", AT_Z_W_LATE, [P, BANK], U32)
+        quantise_z(0, last, z_w_late[:], chunk)
+        second_pass("b", 0, last, 0, last_parts[0], last_bank)
+        for cols in last_parts[1:]:
+            second_pass("b", 0, last, 0, cols)
         last_words = new_z_words(1, last)
         for cols in last_parts:
             quantise_z(1, last, last_words, cols)
             second_pass("b", 0, last, 1, cols)
             empty_bank("b", 0, last, cols)
-        wa_words = place("wa_words", AT_WA_WORDS, [P, OUT_TILES * PASSES * P], U32)
-        quantise_wa(0, 1, wa_words[:, : PASSES * P])
-        quantise_wa(1, 2, wa_words[:, PASSES * P :])
-        second_pass("b", 1, last, 0, tag="bank_last")
-        second_pass("b", 1, last, 1)
-        empty_bank("b", 1, last)
+        wa_w = place("wa_w", AT_WA_W, [P, OUT_TILES * PASSES * P], U32)
+        quantise_wa(0, 1, wa_w[:, : PASSES * P])
+        quantise_wa(1, OUT_TILES - 1, wa_w[:, PASSES * P :])
+        second_pass("b", 1, last, 0, chunk, last_bank)
+        second_pass("b", 1, last, 1, chunk)
+        empty_bank("b", 1, last, chunk)
 
         def second_product(which, n):
             for c in range(CHUNKS):
                 for b in range(PASSES):
-                    second_pass(which, n, c, b)
-                empty_bank(which, n, c)
+                    second_pass(which, n, c, b, chunk)
+                empty_bank(which, n, c, chunk)
 
-        damp, score = {}, {}
-
-        picked_b = {}
+        picked_b, damp, score = {}, {}, {}
 
         def pick_damping(n):
-            picked_b[n] = row("picked_b")
+            picked_b[n] = picked_row("picked_b")
             nc.vector.tensor_copy(picked_b[n][:], y["b", n][:].indirect(idx3[:]))
 
         def make_damping(n):
-            damp[n] = place("damp0", AT_W8_FIRST, [P, M], F32) if n == 0 else picked_b[n]
+            damp[n] = place("damp0", AT_DAMP_FIRST, [P, M], F32) if n == 0 else picked_b[n]
             for cols in halves:
                 nc.scalar.activation(damp[n][:, cols], picked_b[n][:, cols], ACT.Abs)
             for cols in halves:
@@ -456,17 +452,17 @@ def tile_list_print_run_forecast_kernel(
                 nc.scalar.activation(damp[n][:, cols], damp[n][:, cols], ACT.Square)
 
         def pick_score(n):
-            score[n] = row("score")
+            score[n] = picked_row("score")
             nc.vector.tensor_tensor(score[n][:], y["a", n][:].indirect(idx3[:]), wgo_sb[:], MULT)
 
         def place_out(n):
-            placed = outs[n % 2]
-            nc.vector.tensor_tensor(placed[:].indirect(idx4[:]), score[n][:], damp[n][:], MULT)
+            window = outs[n % 2]
+            nc.vector.tensor_tensor(window[:].indirect(idx4[:]), score[n][:], damp[n][:], MULT)
             if n < OUT_TILES - 1:
-                nc.sync.dma_start(out[P * n : P * (n + 1), :], placed[:])
+                nc.sync.dma_start(out[P * n : P * (n + 1), :], window[:])
             else:
                 for queue, cols in ((nc.sync, slice(0, T2 // 2)), (nc.scalar, slice(T2 // 2, T2))):
-                    queue.dma_start(out[P * n : P * (n + 1), cols], placed[:, cols])
+                    queue.dma_start(out[P * n : P * (n + 1), cols], window[:, cols])
 
         pick_damping(0)
         second_product("a", 0)

from contextlib import ExitStack

import concourse.mybir as mybir

K, T, S, H, T2, M, N = 512, 4096, 1024, 1024, 2048, 1024, 384
FLOPS = 2 * K * H * S + 2 * 2 * H * N * T2

F32 = mybir.dt.float32
BF16 = mybir.dt.bfloat16
I32 = mybir.dt.int32
U32 = mybir.dt.uint32
U16 = mybir.dt.uint16
U8 = mybir.dt.uint8
FP8X4 = mybir.dt.float8_e4m3fn_x4
FP4X4 = mybir.dt.float4_e2m1fn_x4
ACT = mybir.ActivationFunctionType
MULT = mybir.AluOpType.mult
MAX = mybir.AluOpType.max

P = 128
PACK = 4
QUAD = 32
BANK = 512
STRIPE = 16
PASSES = H // (P * PACK)
CHUNKS = T2 // BANK
TILES = PASSES * PACK
OUT_TILES = N // P
HALF = S // 2
SCALE_ROWS = 16
ROWS_PER_QUAD = 4
LANDING = P - 2 * SCALE_ROWS
LEAD = S // 4
RING_BANKS = 7
PICKED_ROWS = 2 * OUT_TILES
KIB = 1024

AT_TABLE = 8 * KIB - 64
AT_RAW = (137 * KIB, 0, 23 * KIB)
AT_WGS = {0: 162 * KIB, 2: 8 * KIB}
AT_PAGE_FIRST = 170 * KIB
AT_PICKED = AT_PAGE_FIRST - 512
AT_PAGE_ODD = 129 * KIB
AT_W4_RAW = (AT_RAW[0] - 512, 84 * KIB)
AT_STAGED = AT_W4_RAW[1]
AT_OUT = (AT_STAGED, 56 * KIB)
AT_PAGE_EVEN = 76 * KIB
AT_LEAD = AT_PAGE_EVEN
AT_WINDOW = 68 * KIB
AT_W4_S_RAW = 72 * KIB
AT_V_W = 50 * KIB
AT_W8_S = AT_V_W + 256
AT_W8_LAST = 51 * KIB
AT_W8_FIRST = 52 * KIB
AT_PAGE_BF = [(178 + 4 * c) * KIB for c in range(CHUNKS)]
AT_PLANES = AT_PAGE_BF[1] - KIB
AT_W4_W = (64 * KIB - 512, AT_PAGE_BF[3] - 512)
AT_WA_BF = 93 * KIB
AT_SLOTS = [(101 + 4 * i) * KIB for i in range(7)]
AT_H = AT_SLOTS[:3] + [AT_WA_BF] + AT_SLOTS[3:6] + AT_SLOTS[:1]
AT_LOAD_BF = AT_H[:3] + AT_SLOTS[6:] + [AT_H[4], AT_H[1], AT_H[5], AT_H[6]]
AT_Y = {
    ("b", 0): AT_V_W - 8 * KIB + 256,
    ("b", 1): AT_PAGE_FIRST,
    ("b", 2): AT_V_W - 8 * KIB + 256,
    ("a", 0): AT_RAW[2],
    ("a", 1): AT_PAGE_EVEN,
    ("a", 2): 64 * KIB,
}
AT_RAW_SPARE = {(0, CHUNKS - 1): AT_Y["b", 0], (1, 0): AT_Y["a", 2]}
AT_Z_SLOTS = [(146 + 4 * i) * KIB for i in range(CHUNKS)]
AT_Z = AT_Z_SLOTS[:3] + [31 * KIB] + AT_Z_SLOTS[3:] + AT_Z_SLOTS[:3]
AT_Z_W_EARLY = AT_RAW[0]
AT_Z_W_LATE = AT_LOAD_BF[-2]
AT_Z_W_PAIR = 35 * KIB
AT_WA_W = AT_Z[-1]
AT_WGO = AT_SLOTS[6]
AT_DAMP_FIRST = AT_W8_FIRST


def tile_list_print_run_forecast_kernel(
    tc, tab_words, tab_scales, offs, w4_words, w4_scales, wgs, offs2, load,
    wa, w8_words, w8_scales, offs3, offs4, wgo, out,
):
    nc = tc.nc
    with ExitStack() as ctx:
        lists = ctx.enter_context(tc.tile_pool(name="lists", bufs=1))
        keep = ctx.enter_context(tc.tile_pool(name="keep", bufs=1))
        ring = ctx.enter_context(tc.tile_pool(name="ring", bufs=1))
        placed = ctx.enter_context(tc.tile_pool(name="placed", bufs=1))
        psum = ctx.enter_context(tc.psum_pool(name="psum", bufs=1))

        def place(name, offset, shape, dtype):
            return placed.tile(shape, dtype, name=name, tag=name, offset=offset, align_bytes=64)

        def load_list(name, src):
            tile = lists.tile([P, S // STRIPE], U16, name=name)
            nc.sync.dma_start(tile[:], src)
            return tile

        def entries(list_tile, cols):
            return list_tile[:, cols.start // STRIPE : cols.stop // STRIPE]

        def ring_bank():
            return psum.tile([P, BANK], F32, name="bank", tag="bank", bufs=RING_BANKS)

        def last_bank():
            return psum.tile([P, BANK], F32, name="bank_last", tag="bank_last", bufs=1)

        raw_uses = []

        def raw_rows():
            raw_uses.append(len(raw_uses))
            return place("raw%d" % raw_uses[-1], AT_RAW[raw_uses[-1] % len(AT_RAW)], [P, T2], F32)

        def picked_row(name):
            return ring.tile([P, S], F32, name=name, tag="row", bufs=PICKED_ROWS)

        def land_scale_rows(queue, name, offset, src, width):
            tile = place(name, offset, [P, width], U8)
            queue.dma_start(
                tile[LANDING:, :].bitcast(I32),
                src.bitcast(I32).unsqueeze(1).to_broadcast([SCALE_ROWS, 2, width // 4]),
            )
            nc.vector.memset(tile[:LANDING, :].bitcast(I32), 0)
            return tile

        warm = keep.tile([P, 1], F32)
        nc.vector.memset(warm[:], 1.0)

        idx1 = load_list("idx1", offs)
        w4_s_raw = land_scale_rows(nc.scalar, "w4_s_raw", AT_W4_S_RAW, w4_scales[0], H)
        tab_s = land_scale_rows(nc.sync, "tab_s", AT_WINDOW, tab_scales[0], T)
        wgs_rows = wgs.rearrange("(q t) j -> q t j", t=PACK)
        wgs_lead = place("wgs_lead", AT_LEAD, [P, LEAD], F32)
        nc.scalar.dma_start(wgs_lead[:QUAD, :], wgs_rows[:, 0, :LEAD])
        nc.scalar.activation(warm[:], warm[:], ACT.Abs_reciprocal_sqrt)
        idx2 = load_list("idx2", offs2)
        tab_w = place("tab_w", AT_TABLE, [P, T], U32)
        nc.sync.dma_start(tab_w[:].bitcast(I32), tab_words[0].rearrange("p t i -> p (t i)").bitcast(I32))
        w4_w = [place("w4_w%d" % b, AT_W4_W[b], [P, H], U8) for b in range(PASSES)]

        def load_w4(b):
            raw = place("w4_raw%d" % b, AT_W4_RAW[b], [P, H], U8)
            nc.sync.dma_start(raw[:].bitcast(I32), w4_words[0].bitcast(I32)[:, 2 * P * b : 2 * P * (b + 1)])
            return raw

        def deal_w4(b, raw, slots):
            nc.scalar.copy(
                w4_w[b][:].bitcast(U16).rearrange("p (t m) -> p t m", t=PACK)[:, slots],
                raw[:].bitcast(U16).rearrange("p (m t) -> p t m", t=PACK)[:, slots],
            )

        w4_first = load_w4(0)
        idx3 = load_list("idx3", offs3)
        idx4 = load_list("idx4", offs4)

        planes = place("planes", AT_PLANES, [P, H + S], U8)
        nc.vector.memset(planes[:].bitcast(I32), 0)
        w4_s, v_s = planes[:, :H], planes[:, H:]
        staged = place("staged", AT_STAGED, [P, H + S], U8)

        def deal_scales(b):
            nc.vector.tensor_copy(
                staged[:, :H].rearrange("p (b t m) -> p b t m", b=PASSES, t=PACK)[:, b],
                w4_s_raw[:].rearrange("p (b m t) -> p b t m", b=PASSES, t=PACK)[:, b],
            )

        deal_scales(0)
        picked_s = place("picked_s", AT_PICKED, [P, S], U8)
        nc.vector.tensor_copy(picked_s[:], tab_s[:].indirect(idx1[:]))
        deal_scales(1)
        nc.vector.tensor_copy(staged[:, H:].bitcast(I32), picked_s[:].bitcast(I32))
        for r in range(ROWS_PER_QUAD):
            queue = nc.scalar if r % 2 == 0 else nc.sync
            rows = staged[LANDING + 2 * r : P : 2 * ROWS_PER_QUAD, :]
            queue.dma_start(planes[r:P:QUAD, :].bitcast(I32), rows.bitcast(I32))
        lead_words = wgs_lead[:].bitcast(I32)
        nc.vector.tensor_copy(lead_words[QUAD : 2 * QUAD, :], lead_words[:QUAD, :])
        nc.scalar.copy(wgs_lead[P // 2 :, :], wgs_lead[: P // 2, :])

        page_first = place("page_first", AT_PAGE_FIRST, [P, T2], F32)
        nc.gpsimd.memset(page_first[:], 0.0)
        deal_w4(0, w4_first, slice(0, 1))
        deal_w4(0, w4_first, slice(1, PACK))
        page_odd = place("page_odd", AT_PAGE_ODD, [P, T2], F32)
        nc.gpsimd.memset(page_odd[:], 0.0)
        pages = {0: page_first}
        for k in range(1, TILES, 2):
            pages[k] = page_odd

        wgs_pair = {first: place("wgs%d" % first, AT_WGS[first], [P, 2 * S], F32) for first in AT_WGS}
        wgs_of_slot = {}

        def load_wgs(first, count):
            part = wgs_pair[first - first % 2][:, S * (first % 2) : S * (first % 2 + count)]
            for q in (0, 2, 1, 3):
                nc.sync.dma_start(
                    part[QUAD * q : QUAD * (q + 1), :], wgs_rows[:, first : first + count, :].rearrange("q t j -> q (t j)")
                )
            for i in range(count):
                wgs_of_slot[first + i] = part[:, S * i : S * (i + 1)]

        load_wgs(1, 1)
        load_wgs(0, 1)
        w4_second = load_w4(1)

        v_w = place("v_w", AT_V_W, [P, S], U32)
        whole = slice(0, S)
        halves = [slice(0, HALF), slice(HALF, S)]
        pieces = [slice(0, LEAD), slice(LEAD, S - LEAD), slice(S - LEAD, S)]
        for cols in pieces:
            nc.vector.tensor_copy(v_w[:, cols], tab_w[:].indirect(entries(idx1, cols)))

        h_tiles = {}

        def first_product(k, parts):
            if parts[0].start == 0:
                h_tiles[k] = place("h%d" % k, AT_H[k], [P, S], F32)
            b, t = divmod(k, PACK)
            for cols in parts:
                bank = ring_bank()
                width = cols.stop - cols.start
                nc.tensor.matmul_mx(
                    out=bank[:, :width],
                    lhsT=w4_w[b][:, 2 * P * t : 2 * P * (t + 1)].bitcast(FP4X4),
                    lhsT_scale=w4_s[:, P * k : P * (k + 1)],
                    rhs=v_w[:, cols].bitcast(FP8X4),
                    rhs_scale=v_s[:, cols],
                    start=True,
                    stop=True,
                )
                nc.scalar.copy(h_tiles[k][:, cols], bank[:, :width])

        def place_h(k, cols, weights_of_cols):
            nc.vector.tensor_tensor(pages[k][:].indirect(entries(idx2, cols)), h_tiles[k][:, cols], weights_of_cols, MULT)

        load_bf = {}

        def round_load(b, c):
            raw = place("spare%d" % b, AT_RAW_SPARE[b, c], [P, T2], F32) if (b, c) in AT_RAW_SPARE else raw_rows()
            nc.sync.dma_start(
                raw[:].rearrange("p (t c) -> p t c", t=PACK),
                load[P * PACK * b : P * PACK * (b + 1), BANK * c : BANK * (c + 1)].rearrange("(p t) c -> p t c", t=PACK),
            )
            rounded = place("load_bf%d%d" % (b, c), AT_LOAD_BF[CHUNKS * b + c], [P, BANK * PACK], BF16)
            nc.scalar.copy(
                rounded[:].rearrange("p (c i t) -> p c t i", i=4, t=PACK),
                raw[:].rearrange("p (t c i) -> p c t i", t=PACK, i=4),
            )
            load_bf[b, c] = rounded

        page_bf = [place("page_bf%d" % c, AT_PAGE_BF[c], [P, 2, BANK, 2], BF16) for c in range(CHUNKS)]

        def round_page(k):
            u, e = divmod(k % PACK, 2)
            for c in range(CHUNKS):
                nc.scalar.copy(page_bf[c][:, u, :, e], pages[k][:, BANK * c : BANK * (c + 1)])

        z_bf, z_w, z_s = {}, {}, {}

        def make_z(b, c):
            z = place("z%d%d" % (b, c), AT_Z[CHUNKS * b + c], [P, BANK * PACK], BF16)
            nc.vector.tensor_tensor(
                z[:].rearrange("p (c u e) -> p c u e", u=2, e=2),
                page_bf[c][:].rearrange("p u c e -> p c u e"),
                load_bf[b, c][:].rearrange("p (c u e) -> p c u e", u=2, e=2),
                MAX,
            )
            z_bf[b, c] = z

        chunk = slice(0, BANK)

        def quantise_z(b, c, words, cols):
            if cols.start == 0:
                z_w[b, c] = words
                z_s[b, c] = keep.tile([P, BANK], U8, name="z_s%d%d" % (b, c), align_bytes=64)
            nc.vector.quantize_mx(
                out=z_w[b, c][:, cols].bitcast(FP8X4),
                scales=z_s[b, c][:, cols],
                in_=z_bf[b, c][:, PACK * cols.start : PACK * cols.stop],
            )

        def new_z_words(b, c):
            words = keep.tile([P, BANK], U32, name="z_w%d%d" % (b, c), align_bytes=64)
            return words[:]

        wa_bf = place("wa_bf", AT_WA_BF, [P, PASSES * N * PACK], BF16)
        wa_s = keep.tile([P, PASSES * N], U8, align_bytes=64)
        w8_first = place("w8_first", AT_W8_FIRST, [P, PASSES, 2 * P], U32)
        w8_last = place("w8_last", AT_W8_LAST, [P, PASSES, P], U32)
        w8_s = place("w8_s", AT_W8_S, [P, PASSES, N], U8)

        def prepare_second_weights():
            for b in range(PASSES):
                raw = raw_rows()
                nc.sync.dma_start(
                    raw[:, : PACK * N], wa[P * PACK * b : P * PACK * (b + 1), :].rearrange("(p t) n -> p (t n)", t=PACK)
                )
                nc.scalar.copy(
                    wa_bf[:].rearrange("p (n b c i t) -> p b n c t i", n=OUT_TILES, b=PASSES, i=4, t=PACK)[:, b],
                    raw[:, : PACK * N].rearrange("p (t n c i) -> p n c t i", t=PACK, n=OUT_TILES, i=4),
                )
            words = w8_words.rearrange("a p c i -> p a (c i)").bitcast(I32)
            nc.sync.dma_start(w8_first[:].bitcast(I32), words[:, :, : 2 * P])
            nc.sync.dma_start(w8_last[:].bitcast(I32), words[:, :, 2 * P :])
            nc.gpsimd.memset(w8_s[:].bitcast(I32), 0)
            rows = w8_scales.rearrange("a (q r) c -> r q a c", r=ROWS_PER_QUAD)
            for r in range(ROWS_PER_QUAD):
                nc.sync.dma_start(w8_s[r:P:QUAD, :, :].bitcast(I32), rows[r].bitcast(I32))

        weights = {}
        for n in range(OUT_TILES):
            for b in range(PASSES):
                cols = slice(P * n, P * (n + 1))
                weights["b", n, b] = (w8_first[:, b, cols] if n < OUT_TILES - 1 else w8_last[:, b, :], w8_s[:, b, cols])

        def quantise_wa(first, count, words):
            lo, hi = PASSES * P * first, PASSES * P * (first + count)
            nc.vector.quantize_mx(out=words.bitcast(FP8X4), scales=wa_s[:, lo:hi], in_=wa_bf[:, PACK * lo : PACK * hi])
            for n in range(first, first + count):
                for b in range(PASSES):
                    at = P * (PASSES * n + b)
                    weights["a", n, b] = (words[:, at - lo : at - lo + P], wa_s[:, at : at + P])

        banks, y = {}, {}

        def second_pass(which, n, c, b, cols, new_bank=ring_bank):
            key = which, n, c, cols.start
            if b == 0:
                banks[key] = new_bank()
            words, scales = weights[which, n, b]
            nc.tensor.matmul_mx(
                out=banks[key][:, : cols.stop - cols.start],
                lhsT=words.bitcast(FP8X4),
                lhsT_scale=scales,
                rhs=z_w[b, c][:, cols].bitcast(FP8X4),
                rhs_scale=z_s[b, c][:, cols],
                start=(b == 0),
                stop=(b == PASSES - 1),
            )

        def empty_bank(which, n, c, cols):
            if c == 0:
                y[which, n] = place("y_%s%d" % (which, n), AT_Y[which, n], [P, T2], F32)
            nc.scalar.copy(
                y[which, n][:, BANK * c + cols.start : BANK * c + cols.stop],
                banks[which, n, c, cols.start][:, : cols.stop - cols.start],
            )

        first_product(0, pieces[:1])
        first_product(1, pieces)
        first_product(0, pieces[1:])
        for k in range(2, TILES - 1):
            if k == PACK:
                deal_w4(1, w4_second, slice(0, PACK))
            first_product(k, halves)
        place_h(0, pieces[0], wgs_lead[:])
        page_even = place("page_even", AT_PAGE_EVEN, [P, T2], F32)
        nc.gpsimd.memset(page_even[:], 0.0)
        for k in range(2, TILES, 2):
            pages[k] = page_even
        for k in (1, 0) + tuple(range(2, TILES)):
            if k == 2:
                load_wgs(2, 2)
            cols = slice(LEAD, S) if k == 0 else whole
            place_h(k, cols, wgs_of_slot[k % PACK][:, cols])
            if k == PACK:
                round_load(1, 0)
                for c in range(CHUNKS):
                    make_z(0, c)
            round_page(k)
            if k < PACK - 1:
                round_load(0, k)
            if k == PACK - 2:
                round_load(0, CHUNKS - 1)
            if k == PACK - 1:
                prepare_second_weights()
            if k == PACK:
                first_product(TILES - 1, halves)
            if PACK <= k < TILES - 1:
                round_load(1, k + 1 - PACK)
        out_odd = place("out_odd", AT_OUT[1], [P, T2], F32)
        out_even = place("out_even", AT_OUT[0], [P, T2], F32)
        outs = [out_even, out_odd]
        for tile in outs:
            nc.gpsimd.memset(tile[:], 0.0)
        wgo_sb = place("wgo_sb", AT_WGO, [P, M], F32)
        nc.sync.dma_start(wgo_sb[:], wgo)

        z_w_early = place("z_w_early", AT_Z_W_EARLY, [P, (CHUNKS - 1) * BANK], U32)
        z_w_pair = place("z_w_pair", AT_Z_W_PAIR, [P, 2 * BANK], U32)
        last = CHUNKS - 1
        last_parts = [slice(0, 2 * P), slice(2 * P, 3 * P), slice(3 * P, BANK)]

        def open_chunk(c):
            quantise_z(0, c, z_w_early[:, BANK * c : BANK * (c + 1)], chunk)
            for n in range(2):
                second_pass("b", n, c, 0, chunk)

        def finish_chunk(c):
            quantise_z(1, c, z_w_pair[:, BANK * c : BANK * (c + 1)] if c < 2 else new_z_words(1, c), chunk)
            for n in range(2):
                second_pass("b", n, c, 1, chunk)
                empty_bank("b", n, c, chunk)

        for c in range(last):
            open_chunk(c)
        make_z(1, 0)
        make_z(1, 1)
        finish_chunk(0)
        make_z(1, 2)
        finish_chunk(1)
        finish_chunk(2)
        make_z(1, last)
        z_w_late = place("z_w_late", AT_Z_W_LATE, [P, BANK], U32)
        quantise_z(0, last, z_w_late[:], chunk)
        second_pass("b", 0, last, 0, last_parts[0], last_bank)
        for cols in last_parts[1:]:
            second_pass("b", 0, last, 0, cols)
        last_words = new_z_words(1, last)
        for cols in last_parts:
            quantise_z(1, last, last_words, cols)
            second_pass("b", 0, last, 1, cols)
            empty_bank("b", 0, last, cols)
        wa_w = place("wa_w", AT_WA_W, [P, OUT_TILES * PASSES * P], U32)
        quantise_wa(0, 1, wa_w[:, : PASSES * P])
        quantise_wa(1, OUT_TILES - 1, wa_w[:, PASSES * P :])
        second_pass("b", 1, last, 0, chunk, last_bank)
        second_pass("b", 1, last, 1, chunk)
        empty_bank("b", 1, last, chunk)

        def second_product(which, n):
            for c in range(CHUNKS):
                for b in range(PASSES):
                    second_pass(which, n, c, b, chunk)
                empty_bank(which, n, c, chunk)

        picked_b, damp, score = {}, {}, {}

        def pick_damping(n):
            picked_b[n] = picked_row("picked_b")
            nc.vector.tensor_copy(picked_b[n][:], y["b", n][:].indirect(idx3[:]))

        def make_damping(n):
            damp[n] = place("damp0", AT_DAMP_FIRST, [P, M], F32) if n == 0 else picked_b[n]
            for cols in halves:
                nc.scalar.activation(damp[n][:, cols], picked_b[n][:, cols], ACT.Abs)
            for cols in halves:
                nc.scalar.activation(damp[n][:, cols], damp[n][:, cols], ACT.Abs_reciprocal_sqrt, bias=1.0)
            for cols in halves:
                nc.scalar.activation(damp[n][:, cols], damp[n][:, cols], ACT.Square)

        def pick_score(n):
            score[n] = picked_row("score")
            nc.vector.tensor_tensor(score[n][:], y["a", n][:].indirect(idx3[:]), wgo_sb[:], MULT)

        def place_out(n):
            window = outs[n % 2]
            nc.vector.tensor_tensor(window[:].indirect(idx4[:]), score[n][:], damp[n][:], MULT)
            if n < OUT_TILES - 1:
                nc.sync.dma_start(out[P * n : P * (n + 1), :], window[:])
            else:
                for queue, cols in ((nc.sync, slice(0, T2 // 2)), (nc.scalar, slice(T2 // 2, T2))):
                    queue.dma_start(out[P * n : P * (n + 1), cols], window[:, cols])

        pick_damping(0)
        second_product("a", 0)
        pick_damping(1)
        pick_score(0)
        second_product("b", 2)
        pick_damping(2)
        make_damping(0)
        place_out(0)
        second_product("a", 1)
        second_product("a", 2)
        make_damping(1)
        pick_score(1)
        pick_score(2)
        make_damping(2)
        place_out(1)
        place_out(2)
